import numpy as np
import ml_dtypes


def mxq(x, axis, fmt="e4m3"):
    dtype, down = {"e4m3": (ml_dtypes.float8_e4m3fn, 7), "e5m2": (ml_dtypes.float8_e5m2, 14)}[fmt]
    v = np.moveaxis(np.asarray(x, np.float32).astype(ml_dtypes.bfloat16).astype(np.float64), axis, -1)
    blocks = v.reshape(v.shape[:-1] + (-1, 32))
    amax = np.abs(blocks).max(-1, keepdims=True)
    byte = np.maximum(np.where(amax > 0, np.frexp(amax)[1] - 1 + 127, 0) - down, 1)
    scale = np.exp2(byte - 127.0)
    codes = (blocks / scale).astype(np.float32).astype(dtype).astype(np.float64)
    return np.moveaxis((codes * scale).reshape(v.shape), -1, axis)


WIDE = False


def mx_kscale(k):
    if not WIDE:
        return np.ones(k)
    levels = np.array([10, -10, 5, -5, 0])
    if k % 512:
        return np.exp2(np.random.permutation(np.resize(levels, k // 32))).repeat(32)
    a = np.empty((k // 512, 16))
    for p in range(k // 512):
        a[p, :8] = np.random.permutation(np.resize(levels, 8))
        for g in range(8):
            far = levels[np.abs(levels - a[p, g]) >= 10]
            a[p, g + 8] = far[np.random.randint(len(far))]
    return np.exp2(a.ravel()).repeat(32)


def f64(x):
    return np.asarray(x).astype(np.float64)


def striped(idx):
    return np.tile(idx.reshape(-1, 16).T, (8, 1)).astype(np.uint16)


def unstriped(offs):
    return offs[:16].T.reshape(-1).astype(np.int64)


def relu(v):
    return np.maximum(v, 0.0)


K, T, E, C, H, N = 1024, 768, 6, 256, 512, 128


def by_expert(wq, xq):
    return np.concatenate([wq[e].T @ xq[:, e * C:(e + 1) * C] for e in range(E)], axis=1)


def setup_inputs():
    n = np.random.standard_normal
    s = mx_kscale(K)[:, None]
    u = mx_kscale(H)
    first = np.random.permutation(np.repeat(np.arange(E), T // E))
    second = (first + 1 + np.random.permutation(np.repeat(np.arange(E - 1), -(-T // (E - 1)))[:T])) % E
    while np.bincount(second, minlength=E).max() != T // E:
        load = np.bincount(second, minlength=E); hi, lo = int(load.argmax()), int(load.argmin())
        t = np.flatnonzero((second == hi) & (first != lo))[0]; second[t] = lo
    slot_token = np.empty(E * C, np.int64); pos = np.empty((2, T), np.int64); fill = np.zeros(E, np.int64)
    place = np.stack([np.random.permutation(C) for _ in range(E)])
    for r, deal in enumerate((first, second)):
        for t in np.random.permutation(T):
            e = deal[t]; j = e * C + place[e, fill[e]]; fill[e] += 1; slot_token[j] = t; pos[r, t] = j
    g = np.random.uniform(0.2, 0.8, T)
    return {
        "xT": (n((K, T)) * s).astype(np.float32),
        "w1": (n((E, K, H)) / np.sqrt(K) / s[None]).astype(np.float32),
        "w3": (n((E, K, H)) / np.sqrt(K) / s[None] * u[None, None, :]).astype(np.float32),
        "w2": (n((E, H, N)) / np.sqrt(H) / u[None, :, None]).astype(np.float32),
        "gate": np.stack([np.tile(g, (N, 1)), np.tile(1.0 - g, (N, 1))]).astype(np.float32),
        "offs": striped(slot_token),
        "pos1": striped(pos[0]),
        "pos2": striped(pos[1]),
    }


def reference(xT, w1, w3, w2, gate, offs, pos1, pos2):
    idx = unstriped(offs)
    xq = mxq(f64(xT)[:, idx], 0, "e4m3")
    h = relu(by_expert(mxq(f64(w1), 1, "e4m3"), xq))
    h = h * by_expert(mxq(f64(w3), 1, "e4m3"), xq)
    y = by_expert(mxq(f64(w2), 1, "e4m3"), mxq(h, 0, "e4m3"))
    return f64(gate[0]) * y[:, unstriped(pos1)] + f64(gate[1]) * y[:, unstriped(pos2)]

@@ -1,0 +1,286 @@
+from contextlib import ExitStack
+
+import concourse.mybir as mybir
+
+K, T, E, C, H, N = 1024, 768, 6, 256, 512, 128
+P = 128
+PACK = 4
+K_PASS = P * PACK
+PASSES = K // K_PASS
+SLOTS = E * C
+FLOPS = 2 * SLOTS * (2 * K * H + H * N)
+
+F32 = mybir.dt.float32
+BF16 = mybir.dt.bfloat16
+U32 = mybir.dt.uint32
+U16 = mybir.dt.uint16
+U8 = mybir.dt.uint8
+FP8X4 = mybir.dt.float8_e4m3fn_x4
+MULT = mybir.AluOpType.mult
+ADD = mybir.AluOpType.add
+RELU = mybir.ActivationFunctionType.Relu
+
+SLICE = 512
+HALF = 128
+PIECE = 256
+AHEAD = 9
+SHARE = 88
+LAST_SHARE = 44
+SCALE_ROW = (0, 4)
+
+
+def tile_routed_moe_kernel(tc, xT, w1, w3, w2, gate, offs, pos1, pos2, out):
+    nc = tc.nc
+    with ExitStack() as ctx:
+        keep = ctx.enter_context(tc.tile_pool(name="keep", bufs=1))
+        stage = ctx.enter_context(tc.tile_pool(name="stage", bufs=11))
+        work = ctx.enter_context(tc.tile_pool(name="work", bufs=3))
+        quant = ctx.enter_context(tc.tile_pool(name="quant", bufs=10))
+        psum = ctx.enter_context(tc.psum_pool(name="psum", bufs=3))
+        psum_y = ctx.enter_context(tc.psum_pool(name="psum_y", bufs=2))
+
+        offs_t = keep.tile([P, SLOTS // 16], U16, name="offs_t")
+        pos1_t = keep.tile([P, T // 16], U16, name="pos1_t")
+        pos2_t = keep.tile([P, T // 16], U16, name="pos2_t")
+        x_raw = [keep.tile([P, PACK, T], F32, name=f"x_raw{s}") for s in range(PASSES)]
+        x_bf = [keep.tile([P, T * PACK], BF16, name=f"x_bf{s}", align_bytes=64) for s in range(PASSES)]
+        x_words = [keep.tile([P, T], U32, name=f"x_words{s}", align_bytes=64) for s in range(PASSES)]
+        x_bytes = keep.tile([P, T], U8, name="x_bytes", align_bytes=64)
+        slot_words = {}
+        slot_bytes = {}
+        y_all = keep.tile([P, SLOTS], F32, name="y_all")
+
+        nc.gpsimd.memset(x_bytes[:], 0)
+        nc.sync.dma_start(offs_t[:], offs)
+        for s in range(PASSES):
+            nc.sync.dma_start(
+                out=x_raw[s][:], in_=xT[s * K_PASS : (s + 1) * K_PASS, :].rearrange("(p t) n -> p t n", t=PACK)
+            )
+
+        tiles = [(w, e, s) for e in range(E) for w in (0, 1) for s in range(PASSES)]
+        last = len(tiles) - 1
+        raws = {}
+        cast = {}
+        quantised = {}
+        w2_raw = {}
+        w2_cast = {}
+        w2_quantised = {}
+        relus = {}
+        sums = {}
+        hidden = {}
+        hidden_q = {}
+        results = {}
+
+        def load(i):
+            w, e, s = tiles[i]
+            raw = stage.tile([P, PACK, H], F32, name="raw")
+            nc.sync.dma_start(
+                out=raw[:],
+                in_=(w1, w3)[w][e, s * K_PASS : (s + 1) * K_PASS, :].rearrange("(p t) c -> p t c", t=PACK),
+            )
+            raws[i] = raw
+
+        def load_w2(e):
+            raw = stage.tile([P, PACK, N], F32, name="raw")
+            nc.sync.dma_start(out=raw[:], in_=w2[e].rearrange("(p t) n -> p t n", t=PACK))
+            w2_raw[e] = raw
+
+        def cast_w(i, scalar_m):
+            w_bf = work.tile([P, H * PACK], BF16, name="w_bf", align_bytes=64, bufs=4)
+            dst = w_bf[:].rearrange("p (t m k) -> p m k t", t=PACK, k=PACK)
+            src = raws[i][:].rearrange("p k (m t) -> p m k t", t=PACK)
+            nc.scalar.copy(dst[:, 0:scalar_m], src[:, 0:scalar_m])
+            if scalar_m < P:
+                nc.vector.tensor_copy(dst[:, scalar_m:P], src[:, scalar_m:P])
+            cast[i] = w_bf
+
+        def quantise_w(i):
+            words = quant.tile([P, H], U32, name="w_words", align_bytes=64)
+            scales = quant.tile([P, H], U8, name="w_scales", align_bytes=64)
+            step = H // 2 if i == last else H
+            for a in range(0, H, step):
+                nc.vector.quantize_mx(
+                    out=words[:, a : a + step].bitcast(FP8X4),
+                    scales=scales[:, a : a + step],
+                    in_=cast[i][:, PACK * a : PACK * (a + step)],
+                )
+            quantised[tiles[i]] = (words, scales)
+
+        def cast_w2(e):
+            w_bf = work.tile([P, N * PACK], BF16, name="w2_bf", align_bytes=64, bufs=2)
+            nc.scalar.copy(
+                w_bf[:].rearrange("p (c i t) -> p c t i", i=4, t=PACK),
+                w2_raw[e][:].rearrange("p t (c i) -> p c t i", i=4),
+            )
+            w2_cast[e] = w_bf
+
+        def quantise_w2(e):
+            words = work.tile([P, N], U32, name="w2_words", align_bytes=64)
+            scales = work.tile([P, N], U8, name="w2_scales", align_bytes=64)
+            nc.vector.quantize_mx(out=words[:].bitcast(FP8X4), scales=scales[:], in_=w2_cast[e][:])
+            w2_quantised[e] = (words, scales)
+
+        def gather_words(q, s):
+            a, b = q * SLICE, (q + 1) * SLICE
+            if s == 0:
+                words = work.tile([P, PASSES, SLICE], U32, name="slot_words", align_bytes=64, bufs=2)
+                slot_words[q] = words
+            nc.vector.tensor_copy(slot_words[q][:, s, :], x_words[s][:].indirect(offs_t[:, a // 16 : b // 16]))
+
+        def gather_bytes(q):
+            a, b = q * SLICE, (q + 1) * SLICE
+            scales = work.tile([P, SLICE], U8, name="slot_bytes", align_bytes=64, bufs=2)
+            nc.vector.tensor_copy(scales[:], x_bytes[:].indirect(offs_t[:, a // 16 : b // 16]))
+            slot_bytes[q] = scales
+
+        def project(w, e, half):
+            q, a = divmod(e * C + half * HALF, SLICE)
+            acc = psum.tile([P, PACK, HALF], F32, name=("acc_a", "acc_b")[w])
+            for t in range(PACK):
+                for s in range(PASSES):
+                    words, scales = quantised[(w, e, s)]
+                    nc.tensor.matmul_mx(
+                        out=acc[:, t, :],
+                        lhsT=words[:, t * P : (t + 1) * P].bitcast(FP8X4),
+                        lhsT_scale=scales[:, t * P : (t + 1) * P],
+                        rhs=slot_words[q][:, s, a : a + HALF].bitcast(FP8X4),
+                        rhs_scale=slot_bytes[q][SCALE_ROW[s] : P, a : a + HALF],
+                        start=(s == 0),
+                        stop=(s == PASSES - 1),
+                    )
+            sums[(w, e, half)] = acc
+
+        def rectify(e, half):
+            r = raws[4 * e + 3][:, :, half * HALF : (half + 1) * HALF].rearrange("p k (n t) -> p k n t", t=PACK)
+            nc.scalar.activation(r, sums[(0, e, half)][:].rearrange("p t (k n) -> p k n t", k=PACK), RELU)
+            relus[(e, half)] = r
+
+        def hide(e, half):
+            h = work.tile([P, HALF, PACK], BF16, name="h", align_bytes=64)
+            nc.vector.tensor_tensor(
+                h[:].rearrange("p (k n) t -> p k n t", k=PACK),
+                sums[(1, e, half)][:].rearrange("p t (k n) -> p k n t", k=PACK),
+                relus[(e, half)],
+                MULT,
+            )
+            hidden[(e, half)] = h
+
+        def quantise_h(e, half):
+            words = work.tile([P, HALF], U32, name="h_words", align_bytes=64)
+            scales = work.tile([P, HALF], U8, name="h_scales", align_bytes=64)
+            nc.vector.quantize_mx(
+                out=words[:].bitcast(FP8X4),
+                scales=scales[:],
+                in_=hidden[(e, half)][:].rearrange("p n t -> p (n t)"),
+            )
+            hidden_q[(e, half)] = (words, scales)
+
+        def project_back(e, half):
+            acc = psum_y.tile([P, HALF], F32, name="acc_y")
+            w_words, w_scales = w2_quantised[e]
+            h_words, h_scales = hidden_q[(e, half)]
+            nc.tensor.matmul_mx(
+                out=acc[:],
+                lhsT=w_words[:].bitcast(FP8X4),
+                lhsT_scale=w_scales[:],
+                rhs=h_words[:].bitcast(FP8X4),
+                rhs_scale=h_scales[:],
+                start=True,
+                stop=True,
+            )
+            results[(e, half)] = acc
+
+        def keep_y(e, half):
+            a = e * C + half * HALF
+            copy = nc.scalar.copy if e == E - 1 else nc.vector.tensor_copy
+            copy(y_all[:, a : a + HALF], results[(e, half)][:])
+
+        def load_next(i):
+            if i < len(tiles):
+                load(i)
+                if i % 4 == 3:
+                    load_w2(i // 4)
+
+        for i in range(AHEAD):
+            load_next(i)
+        for s in range(PASSES):
+            dst = x_bf[s][:].rearrange("p (c i t) -> p c t i", i=4, t=PACK)
+            src = x_raw[s][:].rearrange("p t (c i) -> p c t i", i=4)
+            nc.scalar.copy(dst[:, 128:192], src[:, 128:192])
+            nc.vector.tensor_copy(dst[:, 0:128], src[:, 0:128])
+            for a, b in ((0, 512), (512, 768)):
+                nc.vector.quantize_mx(
+                    out=x_words[s][:, a:b].bitcast(FP8X4),
+                    scales=x_bytes[SCALE_ROW[s] : P, a:b],
+                    in_=x_bf[s][:, PACK * a : PACK * b],
+                )
+            gather_words(0, s)
+        gather_bytes(0)
+        nc.sync.dma_start(pos1_t[:], pos1)
+        nc.sync.dma_start(pos2_t[:], pos2)
+
+        gate_t = None
+        for i in range(len(tiles) + 4):
+            e, r = divmod(i, 4)
+            load_next(i + AHEAD)
+            if i + AHEAD == last:
+                gate_t = stage.tile([P, 2, T], F32, name="raw")
+                nc.sync.dma_start(out=gate_t[:], in_=gate.rearrange("r p t -> p r t"))
+            if i <= last:
+                cast_w(i, LAST_SHARE if i == last else SHARE)
+            if 1 <= i <= last + 1:
+                quantise_w(i - 1)
+            if r == 2 and e < E:
+                for half in range(2):
+                    project(0, e, half)
+            if r == 3 and e < E:
+                cast_w2(e)
+                for half in range(2):
+                    rectify(e, half)
+            if r == 0 and e > 0:
+                for half in range(2):
+                    project(1, e - 1, half)
+                quantise_w2(e - 1)
+            if r == 1 and e > 0:
+                for half in range(2):
+                    hide(e - 1, half)
+            if r == 2 and e > 0:
+                for half in range(2):
+                    quantise_h(e - 1, half)
+                for half in range(2):
+                    project_back(e - 1, half)
+            if r == 3 and e > 0:
+                for half in range(2):
+                    keep_y(e - 1, half)
+            if i in (6, 7):
+                gather_words(1, i - 6)
+            if i == 8:
+                gather_bytes(1)
+            if i in (12, 13):
+                gather_words(2, i - 12)
+            if i == 14:
+                gather_bytes(2)
+
+        pieces = ((0, 512), (512, T))
+        products = {}
+
+        def fetch(piece, which, pos_t):
+            a, b = piece
+            prod = work.tile([P, b - a], F32, name=f"prod{which}", bufs=2)
+            nc.vector.tensor_tensor(
+                prod[:], y_all[:].indirect(pos_t[:, a // 16 : b // 16]), gate_t[:, which, a:b], MULT
+            )
+            products[(piece, which)] = prod
+
+        def finish(piece):
+            a, b = piece
+            o = work.tile([P, b - a], F32, name="o", bufs=2)
+            nc.vector.tensor_tensor(o[:], products[(piece, 0)][:], products[(piece, 1)][:], ADD)
+            nc.sync.dma_start(out=out[:, a:b], in_=o[:])
+
+        fetch(pieces[0], 0, pos1_t)
+        fetch(pieces[0], 1, pos2_t)
+        fetch(pieces[1], 0, pos1_t)
+        fetch(pieces[1], 1, pos2_t)
+        finish(pieces[0])
+        finish(pieces[1])

@@ -22,10 +22,16 @@ RELU = mybir.ActivationFunctionType.Relu
 
 SLICE = 512
 HALF = 128
-PIECE = 256
-AHEAD = 9
-SHARE = 88
-LAST_SHARE = 44
+RING = 5
+WHOLE = 9
+EARLY_W2 = 4
+SHARE = 80
+LAST_SHARE = 22
+FIRST_HALF_SHARE = 40
+END_SHARE = 56
+LAST = (1, E - 1, PASSES - 1)
+AHEAD = 3
+X_SHARE = 80
 SCALE_ROW = (0, 4)
 
 
@@ -33,11 +39,10 @@ def tile_routed_moe_kernel(tc, xT, w1, w3, w2, gate, offs, pos1, pos2, out):
     nc = tc.nc
     with ExitStack() as ctx:
         keep = ctx.enter_context(tc.tile_pool(name="keep", bufs=1))
-        stage = ctx.enter_context(tc.tile_pool(name="stage", bufs=11))
-        work = ctx.enter_context(tc.tile_pool(name="work", bufs=3))
-        quant = ctx.enter_context(tc.tile_pool(name="quant", bufs=10))
-        psum = ctx.enter_context(tc.psum_pool(name="psum", bufs=3))
-        psum_y = ctx.enter_context(tc.psum_pool(name="psum_y", bufs=2))
+        work = ctx.enter_context(tc.tile_pool(name="work", bufs=2))
+        quant = ctx.enter_context(tc.tile_pool(name="quant", bufs=8))
+        psum = ctx.enter_context(tc.psum_pool(name="psum", bufs=2))
+        psum_y = ctx.enter_context(tc.psum_pool(name="psum_y", bufs=3))
 
         offs_t = keep.tile([P, SLOTS // 16], U16, name="offs_t")
         pos1_t = keep.tile([P, T // 16], U16, name="pos1_t")
@@ -46,23 +51,15 @@ def tile_routed_moe_kernel(tc, xT, w1, w3, w2, gate, offs, pos1, pos2, out):
         x_bf = [keep.tile([P, T * PACK], BF16, name=f"x_bf{s}", align_bytes=64) for s in range(PASSES)]
         x_words = [keep.tile([P, T], U32, name=f"x_words{s}", align_bytes=64) for s in range(PASSES)]
         x_bytes = keep.tile([P, T], U8, name="x_bytes", align_bytes=64)
+        y_all = keep.tile([P, SLOTS], F32, name="y_all")
+        gate_t = keep.tile([P, 2, T], F32, name="gate_t")
+        ring = [keep.tile([P, PASSES, PACK, H], F32, name=f"ring{r}", align_bytes=64) for r in range(RING)]
+        w2_early = keep.tile([P, EARLY_W2, PACK, N], F32, name="w2_early")
+        w2_late = keep.tile([P, E - EARLY_W2, PACK, N], F32, name="w2_late")
         slot_words = {}
         slot_bytes = {}
-        y_all = keep.tile([P, SLOTS], F32, name="y_all")
-
-        nc.gpsimd.memset(x_bytes[:], 0)
-        nc.sync.dma_start(offs_t[:], offs)
-        for s in range(PASSES):
-            nc.sync.dma_start(
-                out=x_raw[s][:], in_=xT[s * K_PASS : (s + 1) * K_PASS, :].rearrange("(p t) n -> p t n", t=PACK)
-            )
-
-        tiles = [(w, e, s) for e in range(E) for w in (0, 1) for s in range(PASSES)]
-        last = len(tiles) - 1
-        raws = {}
         cast = {}
         quantised = {}
-        w2_raw = {}
         w2_cast = {}
         w2_quantised = {}
         relus = {}
@@ -71,65 +68,86 @@ def tile_routed_moe_kernel(tc, xT, w1, w3, w2, gate, offs, pos1, pos2, out):
         hidden_q = {}
         results = {}
 
-        def load(i):
-            w, e, s = tiles[i]
-            raw = stage.tile([P, PACK, H], F32, name="raw")
-            nc.sync.dma_start(
-                out=raw[:],
-                in_=(w1, w3)[w][e, s * K_PASS : (s + 1) * K_PASS, :].rearrange("(p t) c -> p t c", t=PACK),
-            )
-            raws[i] = raw
+        def staged(w, e):
+            return ring[(2 * e + w) % RING]
 
-        def load_w2(e):
-            raw = stage.tile([P, PACK, N], F32, name="raw")
-            nc.sync.dma_start(out=raw[:], in_=w2[e].rearrange("(p t) n -> p t n", t=PACK))
-            w2_raw[e] = raw
+        def whole(w, e):
+            return 2 * e + w < WHOLE
 
-        def cast_w(i, scalar_m):
+        def last_half(c):
+            rows = staged(*LAST[:2])[:, LAST[2]].rearrange("p k c -> p (k c)")
+            return rows[:, c * 2 * H : (c + 1) * 2 * H].rearrange("p (k c) -> p k c", k=PACK)
+
+        def load(w, e):
+            src = (w1, w3)[w][e].rearrange("(s p t) c -> p s t c", s=PASSES, t=PACK)
+            if whole(w, e):
+                nc.sync.dma_start(out=staged(w, e)[:], in_=src)
+            else:
+                for s in range(PASSES):
+                    if (w, e, s) != LAST:
+                        nc.sync.dma_start(out=staged(w, e)[:, s], in_=src[:, s])
+                    else:
+                        for c in range(2):
+                            nc.sync.dma_start(out=last_half(c), in_=src[:, s, :, c * H // 2 : (c + 1) * H // 2])
+
+        def load_w2(tile, a, b):
+            nc.sync.dma_start(out=tile[:], in_=w2[a:b].rearrange("e (p t) n -> p e t n", t=PACK))
+
+        def cast_w(w, e, s, scalar_m):
             w_bf = work.tile([P, H * PACK], BF16, name="w_bf", align_bytes=64, bufs=4)
             dst = w_bf[:].rearrange("p (t m k) -> p m k t", t=PACK, k=PACK)
-            src = raws[i][:].rearrange("p k (m t) -> p m k t", t=PACK)
-            nc.scalar.copy(dst[:, 0:scalar_m], src[:, 0:scalar_m])
-            if scalar_m < P:
-                nc.vector.tensor_copy(dst[:, scalar_m:P], src[:, scalar_m:P])
-            cast[i] = w_bf
+            if (w, e, s) != LAST:
+                parts = [(staged(w, e)[:, s], dst, scalar_m)]
+            else:
+                parts = [(last_half(0), dst[:, 0 : P // 2], FIRST_HALF_SHARE), (last_half(1), dst[:, P // 2 : P], LAST_SHARE)]
+            for raw, to, m in parts:
+                src = raw.rearrange("p k (m t) -> p m k t", t=PACK)
+                if m > 0:
+                    nc.scalar.copy(to[:, 0:m], src[:, 0:m])
+                if m < to.shape[1]:
+                    nc.vector.tensor_copy(to[:, m:], src[:, m:])
+            cast[(w, e, s)] = w_bf
 
-        def quantise_w(i):
+        def quantise_w(w, e, s):
             words = quant.tile([P, H], U32, name="w_words", align_bytes=64)
             scales = quant.tile([P, H], U8, name="w_scales", align_bytes=64)
-            step = H // 2 if i == last else H
+            step = P if (w, e, s) == LAST else H
             for a in range(0, H, step):
                 nc.vector.quantize_mx(
                     out=words[:, a : a + step].bitcast(FP8X4),
                     scales=scales[:, a : a + step],
-                    in_=cast[i][:, PACK * a : PACK * (a + step)],
+                    in_=cast[(w, e, s)][:, PACK * a : PACK * (a + step)],
                 )
-            quantised[tiles[i]] = (words, scales)
+            quantised[(w, e, s)] = (words, scales)
 
-        def cast_w2(e):
-            w_bf = work.tile([P, N * PACK], BF16, name="w2_bf", align_bytes=64, bufs=2)
-            nc.scalar.copy(
-                w_bf[:].rearrange("p (c i t) -> p c t i", i=4, t=PACK),
-                w2_raw[e][:].rearrange("p t (c i) -> p c t i", i=4),
-            )
-            w2_cast[e] = w_bf
+        def cast_w2(a, b):
+            w_bf = keep.tile([P, (b - a) * N * PACK], BF16, name=f"w2_bf{a}", align_bytes=64)
+            for e in range(a, b):
+                raw = w2_early[:, e] if e < EARLY_W2 else w2_late[:, e - EARLY_W2]
+                nc.scalar.copy(
+                    w_bf[:, (e - a) * K_PASS : (e - a + 1) * K_PASS].rearrange("p (c i t) -> p c t i", i=4, t=PACK),
+                    raw.rearrange("p t (c i) -> p c t i", i=4),
+                )
+            w2_cast[a] = w_bf
 
-        def quantise_w2(e):
-            words = work.tile([P, N], U32, name="w2_words", align_bytes=64)
-            scales = work.tile([P, N], U8, name="w2_scales", align_bytes=64)
-            nc.vector.quantize_mx(out=words[:].bitcast(FP8X4), scales=scales[:], in_=w2_cast[e][:])
-            w2_quantised[e] = (words, scales)
+        def quantise_w2(a, b):
+            words = keep.tile([P, (b - a) * N], U32, name=f"w2_words{a}", align_bytes=64)
+            scales = keep.tile([P, (b - a) * N], U8, name=f"w2_scales{a}", align_bytes=64)
+            nc.vector.quantize_mx(out=words[:].bitcast(FP8X4), scales=scales[:], in_=w2_cast[a][:])
+            for e in range(a, b):
+                cols = slice((e - a) * N, (e - a + 1) * N)
+                w2_quantised[e] = (words[:, cols], scales[:, cols])
 
         def gather_words(q, s):
             a, b = q * SLICE, (q + 1) * SLICE
             if s == 0:
-                words = work.tile([P, PASSES, SLICE], U32, name="slot_words", align_bytes=64, bufs=2)
+                words = work.tile([P, PASSES, SLICE], U32, name="slot_words", align_bytes=64, bufs=3)
                 slot_words[q] = words
             nc.vector.tensor_copy(slot_words[q][:, s, :], x_words[s][:].indirect(offs_t[:, a // 16 : b // 16]))
 
         def gather_bytes(q):
             a, b = q * SLICE, (q + 1) * SLICE
-            scales = work.tile([P, SLICE], U8, name="slot_bytes", align_bytes=64, bufs=2)
+            scales = work.tile([P, SLICE], U8, name="slot_bytes", align_bytes=64, bufs=3)
             nc.vector.tensor_copy(scales[:], x_bytes[:].indirect(offs_t[:, a // 16 : b // 16]))
             slot_bytes[q] = scales
 
@@ -150,64 +168,99 @@ def tile_routed_moe_kernel(tc, xT, w1, w3, w2, gate, offs, pos1, pos2, out):
                     )
             sums[(w, e, half)] = acc
 
+        def by_slot(acc, rows):
+            return acc[:].rearrange("p t (k n) -> p k n t", k=rows)
+
         def rectify(e, half):
-            r = raws[4 * e + 3][:, :, half * HALF : (half + 1) * HALF].rearrange("p k (n t) -> p k n t", t=PACK)
-            nc.scalar.activation(r, sums[(0, e, half)][:].rearrange("p t (k n) -> p k n t", k=PACK), RELU)
+            s = 0 if whole(1, e) else 1
+            if e < E - 1:
+                dead = staged(1, e)[:, s, :, half * HALF : (half + 1) * HALF]
+            else:
+                dead = last_half(1)[:, 2 * half : 2 * half + 2]
+            r = dead.rearrange("p k (n t) -> p k n t", t=PACK)
+            nc.scalar.activation(r, by_slot(sums[(0, e, half)], r.shape[1]), RELU)
             relus[(e, half)] = r
 
         def hide(e, half):
-            h = work.tile([P, HALF, PACK], BF16, name="h", align_bytes=64)
+            if e < E - 1:
+                s = 1 if whole(0, e + 1) else 0
+                h = staged(0, e + 1)[:, s, 2 * half : 2 * half + 2, H - HALF : H].bitcast(BF16)
+            else:
+                h_tile = work.tile([P, HALF * PACK], BF16, name="h", align_bytes=64)
+                h = h_tile[:].rearrange("p (k c) -> p k c", k=2)
+            rows = relus[(e, half)].shape[1]
             nc.vector.tensor_tensor(
-                h[:].rearrange("p (k n) t -> p k n t", k=PACK),
-                sums[(1, e, half)][:].rearrange("p t (k n) -> p k n t", k=PACK),
-                relus[(e, half)],
+                h.rearrange("p r (k n t) -> p r k n t", k=rows // 2, t=PACK),
+                by_slot(sums[(1, e, half)], rows).rearrange("p (r k) n t -> p r k n t", r=2),
+                relus[(e, half)].rearrange("p (r k) n t -> p r k n t", r=2),
                 MULT,
             )
             hidden[(e, half)] = h
 
         def quantise_h(e, half):
-            words = work.tile([P, HALF], U32, name="h_words", align_bytes=64)
-            scales = work.tile([P, HALF], U8, name="h_scales", align_bytes=64)
-            nc.vector.quantize_mx(
-                out=words[:].bitcast(FP8X4),
-                scales=scales[:],
-                in_=hidden[(e, half)][:].rearrange("p n t -> p (n t)"),
-            )
+            words = work.tile([P, HALF], U32, name="h_words", align_bytes=64, bufs=4)
+            scales = work.tile([P, HALF], U8, name="h_scales", align_bytes=64, bufs=4)
+            h = hidden[(e, half)]
+            if e < E - 1:
+                for r in range(2):
+                    cols = slice(r * HALF // 2, (r + 1) * HALF // 2)
+                    nc.vector.quantize_mx(out=words[:, cols].bitcast(FP8X4), scales=scales[:, cols], in_=h[:, r])
+            else:
+                nc.vector.quantize_mx(
+                    out=words[:].bitcast(FP8X4), scales=scales[:], in_=h.rearrange("p r c -> p (r c)")
+                )
             hidden_q[(e, half)] = (words, scales)
 
-        def project_back(e, half):
-            acc = psum_y.tile([P, HALF], F32, name="acc_y")
+        def project_back(e, half, acc):
             w_words, w_scales = w2_quantised[e]
             h_words, h_scales = hidden_q[(e, half)]
             nc.tensor.matmul_mx(
-                out=acc[:],
-                lhsT=w_words[:].bitcast(FP8X4),
-                lhsT_scale=w_scales[:],
+                out=acc,
+                lhsT=w_words.bitcast(FP8X4),
+                lhsT_scale=w_scales,
                 rhs=h_words[:].bitcast(FP8X4),
                 rhs_scale=h_scales[:],
                 start=True,
                 stop=True,
             )
-            results[(e, half)] = acc
 
-        def keep_y(e, half):
-            a = e * C + half * HALF
-            copy = nc.scalar.copy if e == E - 1 else nc.vector.tensor_copy
-            copy(y_all[:, a : a + HALF], results[(e, half)][:])
+        def finish_expert(e):
+            if e < E - 1:
+                acc = psum_y.tile([P, C], F32, name="acc_y")
+                for half in range(2):
+                    project_back(e, half, acc[:, half * HALF : (half + 1) * HALF])
+                copy = nc.vector.tensor_copy if e < EARLY_W2 else nc.scalar.copy
+                copy(y_all[:, e * C : (e + 1) * C], acc[:])
+            else:
+                for half in range(2):
+                    acc = psum_y.tile([P, C], F32, name="acc_y")
+                    project_back(e, half, acc[:, 0:HALF])
+                    a = e * C + half * HALF
+                    nc.scalar.copy(y_all[:, a : a + HALF], acc[:, 0:HALF])
 
-        def load_next(i):
-            if i < len(tiles):
-                load(i)
-                if i % 4 == 3:
-                    load_w2(i // 4)
+        def hide_expert(e):
+            for half in range(2):
+                hide(e, half)
+            for half in range(2):
+                quantise_h(e, half)
 
-        for i in range(AHEAD):
-            load_next(i)
+        nc.gpsimd.memset(x_bytes[:], 0)
+        for s in range(PASSES):
+            nc.sync.dma_start(
+                out=x_raw[s][:], in_=xT[s * K_PASS : (s + 1) * K_PASS, :].rearrange("(p t) n -> p t n", t=PACK)
+            )
+            if s == 0:
+                nc.sync.dma_start(offs_t[:], offs)
+        load_w2(w2_early, 0, EARLY_W2)
+        matrices = [(w, e) for e in range(E) for w in range(2)]
+        for w, e in matrices[:AHEAD]:
+            load(w, e)
+
         for s in range(PASSES):
             dst = x_bf[s][:].rearrange("p (c i t) -> p c t i", i=4, t=PACK)
             src = x_raw[s][:].rearrange("p t (c i) -> p c t i", i=4)
-            nc.scalar.copy(dst[:, 128:192], src[:, 128:192])
-            nc.vector.tensor_copy(dst[:, 0:128], src[:, 0:128])
+            nc.scalar.copy(dst[:, X_SHARE:], src[:, X_SHARE:])
+            nc.vector.tensor_copy(dst[:, 0:X_SHARE], src[:, 0:X_SHARE])
             for a, b in ((0, 512), (512, 768)):
                 nc.vector.quantize_mx(
                     out=x_words[s][:, a:b].bitcast(FP8X4),
@@ -216,57 +269,62 @@ def tile_routed_moe_kernel(tc, xT, w1, w3, w2, gate, offs, pos1, pos2, out):
                 )
             gather_words(0, s)
         gather_bytes(0)
-        nc.sync.dma_start(pos1_t[:], pos1)
-        nc.sync.dma_start(pos2_t[:], pos2)
+        cast_w2(0, EARLY_W2)
 
-        gate_t = None
-        for i in range(len(tiles) + 4):
-            e, r = divmod(i, 4)
-            load_next(i + AHEAD)
-            if i + AHEAD == last:
-                gate_t = stage.tile([P, 2, T], F32, name="raw")
+        for i, (w, e) in enumerate(matrices):
+            if i + AHEAD < len(matrices):
+                load(*matrices[i + AHEAD])
+            if i + AHEAD == len(matrices):
+                load_w2(w2_late, EARLY_W2, E)
+                nc.sync.dma_start(pos1_t[:], pos1)
+                nc.sync.dma_start(pos2_t[:], pos2)
                 nc.sync.dma_start(out=gate_t[:], in_=gate.rearrange("r p t -> p r t"))
-            if i <= last:
-                cast_w(i, LAST_SHARE if i == last else SHARE)
-            if 1 <= i <= last + 1:
-                quantise_w(i - 1)
-            if r == 2 and e < E:
-                for half in range(2):
-                    project(0, e, half)
-            if r == 3 and e < E:
-                cast_w2(e)
+            last = i == len(matrices) - 1
+            if i == 0:
+                order = ((1, P), (0, P))
+            elif whole(w, e):
+                order = ((1, 0), (0, P))
+            else:
+                order = ((0, END_SHARE if last else SHARE), (1, SHARE))
+            cast_w(w, e, *order[0])
+            if whole(w, e):
+                cast_w(w, e, *order[1])
+            if w == 0 and e > 0:
+                hide_expert(e - 1)
+            quantise_w(w, e, order[0][0])
+            if not whole(w, e):
+                cast_w(w, e, *order[1])
+            if w == 1:
                 for half in range(2):
                     rectify(e, half)
-            if r == 0 and e > 0:
-                for half in range(2):
-                    project(1, e - 1, half)
-                quantise_w2(e - 1)
-            if r == 1 and e > 0:
-                for half in range(2):
-                    hide(e - 1, half)
-            if r == 2 and e > 0:
-                for half in range(2):
-                    quantise_h(e - 1, half)
-                for half in range(2):
-                    project_back(e - 1, half)
-            if r == 3 and e > 0:
-                for half in range(2):
-                    keep_y(e - 1, half)
-            if i in (6, 7):
-                gather_words(1, i - 6)
-            if i == 8:
-                gather_bytes(1)
-            if i in (12, 13):
-                gather_words(2, i - 12)
-            if i == 14:
-                gather_bytes(2)
+            quantise_w(w, e, order[1][0])
+            for half in range(2):
+                project(w, e, half)
+            if w == 0 and 0 < e <= EARLY_W2:
+                finish_expert(e - 1)
+            if i == 0:
+                quantise_w2(0, EARLY_W2)
+                for q in range(1, SLOTS // SLICE):
+                    gather_words(q, 0)
+                    gather_words(q, 1)
+                    gather_bytes(q)
+        for e in range(EARLY_W2, E):
+            cast_w2(e, e + 1)
+        hide(E - 1, 0)
+        quantise_w2(E - 2, E - 1)
+        hide(E - 1, 1)
+        quantise_w2(E - 1, E)
+        finish_expert(E - 2)
+        for half in range(2):
+            quantise_h(E - 1, half)
+        finish_expert(E - 1)
 
         pieces = ((0, 512), (512, T))
         products = {}
 
         def fetch(piece, which, pos_t):
             a, b = piece
-            prod = work.tile([P, b - a], F32, name=f"prod{which}", bufs=2)
+            prod = work.tile([P, b - a], F32, name=f"prod{which}")
             nc.vector.tensor_tensor(
                 prod[:], y_all[:].indirect(pos_t[:, a // 16 : b // 16]), gate_t[:, which, a:b], MULT
             )
@@ -274,7 +332,7 @@ def tile_routed_moe_kernel(tc, xT, w1, w3, w2, gate, offs, pos1, pos2, out):
 
         def finish(piece):
             a, b = piece
-            o = work.tile([P, b - a], F32, name="o", bufs=2)
+            o = work.tile([P, b - a], F32, name="o")
             nc.vector.tensor_tensor(o[:], products[(piece, 0)][:], products[(piece, 1)][:], ADD)
             nc.sync.dma_start(out=out[:, a:b], in_=o[:])
 

@@ -47,15 +47,15 @@ def tile_routed_moe_kernel(tc, xT, w1, w3, w2, gate, offs, pos1, pos2, out):
         offs_t = keep.tile([P, SLOTS // 16], U16, name="offs_t")
         pos1_t = keep.tile([P, T // 16], U16, name="pos1_t")
         pos2_t = keep.tile([P, T // 16], U16, name="pos2_t")
-        x_raw = [keep.tile([P, PACK, T], F32, name=f"x_raw{s}") for s in range(PASSES)]
+        x_raw = [keep.tile([P, PACK, T], F32, name=f"x_raw{s}", align_bytes=256) for s in range(PASSES)]
         x_bf = [keep.tile([P, T * PACK], BF16, name=f"x_bf{s}", align_bytes=64) for s in range(PASSES)]
         x_words = [keep.tile([P, T], U32, name=f"x_words{s}", align_bytes=64) for s in range(PASSES)]
         x_bytes = keep.tile([P, T], U8, name="x_bytes", align_bytes=64)
         y_all = keep.tile([P, SLOTS], F32, name="y_all")
-        gate_t = keep.tile([P, 2, T], F32, name="gate_t")
-        ring = [keep.tile([P, PASSES, PACK, H], F32, name=f"ring{r}", align_bytes=64) for r in range(RING)]
-        w2_early = keep.tile([P, EARLY_W2, PACK, N], F32, name="w2_early")
-        w2_late = keep.tile([P, E - EARLY_W2, PACK, N], F32, name="w2_late")
+        gate_t = keep.tile([P, 2, T], F32, name="gate_t", align_bytes=256)
+        ring = [keep.tile([P, PASSES, PACK, H], F32, name=f"ring{r}", align_bytes=256) for r in range(RING)]
+        w2_early = keep.tile([P, EARLY_W2, PACK, N], F32, name="w2_early", align_bytes=256)
+        w2_late = keep.tile([P, E - EARLY_W2, PACK, N], F32, name="w2_late", align_bytes=256)
         slot_words = {}
         slot_bytes = {}
         cast = {}
@@ -332,7 +332,7 @@ def tile_routed_moe_kernel(tc, xT, w1, w3, w2, gate, offs, pos1, pos2, out):
 
         def finish(piece):
             a, b = piece
-            o = work.tile([P, b - a], F32, name="o")
+            o = work.tile([P, b - a], F32, name="o", align_bytes=256)
             nc.vector.tensor_tensor(o[:], products[(piece, 0)][:], products[(piece, 1)][:], ADD)
             nc.sync.dma_start(out=out[:, a:b], in_=o[:])
 

@@ -23,12 +23,11 @@ RELU = mybir.ActivationFunctionType.Relu
 SLICE = 512
 HALF = 128
 RING = 5
-WHOLE = 9
-EARLY_W2 = 4
-SHARE = 80
+WHOLE = 8
+EARLY_W2 = 3
+SHARES = ((40, 96), (64, 64))
 LAST_SHARE = 22
-FIRST_HALF_SHARE = 40
-END_SHARE = 56
+FIRST_HALF_SHARE = 48
 LAST = (1, E - 1, PASSES - 1)
 AHEAD = 3
 X_SHARE = 80
@@ -42,7 +41,7 @@ def tile_routed_moe_kernel(tc, xT, w1, w3, w2, gate, offs, pos1, pos2, out):
         work = ctx.enter_context(tc.tile_pool(name="work", bufs=2))
         quant = ctx.enter_context(tc.tile_pool(name="quant", bufs=8))
         psum = ctx.enter_context(tc.psum_pool(name="psum", bufs=2))
-        psum_y = ctx.enter_context(tc.psum_pool(name="psum_y", bufs=3))
+        psum_y = ctx.enter_context(tc.psum_pool(name="psum_y", bufs=4))
 
         offs_t = keep.tile([P, SLOTS // 16], U16, name="offs_t")
         pos1_t = keep.tile([P, T // 16], U16, name="pos1_t")
@@ -91,7 +90,7 @@ def tile_routed_moe_kernel(tc, xT, w1, w3, w2, gate, offs, pos1, pos2, out):
                             nc.sync.dma_start(out=last_half(c), in_=src[:, s, :, c * H // 2 : (c + 1) * H // 2])
 
         def load_w2(tile, a, b):
-            nc.sync.dma_start(out=tile[:], in_=w2[a:b].rearrange("e (p t) n -> p e t n", t=PACK))
+            nc.sync.dma_start(out=tile, in_=w2[a:b].rearrange("e (p t) n -> p e t n", t=PACK))
 
         def cast_w(w, e, s, scalar_m):
             w_bf = work.tile([P, H * PACK], BF16, name="w_bf", align_bytes=64, bufs=4)
@@ -184,7 +183,7 @@ def tile_routed_moe_kernel(tc, xT, w1, w3, w2, gate, offs, pos1, pos2, out):
         def hide(e, half):
             if e < E - 1:
                 s = 1 if whole(0, e + 1) else 0
-                h = staged(0, e + 1)[:, s, 2 * half : 2 * half + 2, H - HALF : H].bitcast(BF16)
+                h = staged(0, e + 1)[:, s, half, H // 2 : H].bitcast(BF16).rearrange("p (k c) -> p k c", k=2)
             else:
                 h_tile = work.tile([P, HALF * PACK], BF16, name="h", align_bytes=64)
                 h = h_tile[:].rearrange("p (k c) -> p k c", k=2)
@@ -198,17 +197,10 @@ def tile_routed_moe_kernel(tc, xT, w1, w3, w2, gate, offs, pos1, pos2, out):
             hidden[(e, half)] = h
 
         def quantise_h(e, half):
-            words = work.tile([P, HALF], U32, name="h_words", align_bytes=64, bufs=4)
-            scales = work.tile([P, HALF], U8, name="h_scales", align_bytes=64, bufs=4)
+            words = work.tile([P, HALF], U32, name="h_words", align_bytes=64, bufs=6)
+            scales = work.tile([P, HALF], U8, name="h_scales", align_bytes=64, bufs=6)
             h = hidden[(e, half)]
-            if e < E - 1:
-                for r in range(2):
-                    cols = slice(r * HALF // 2, (r + 1) * HALF // 2)
-                    nc.vector.quantize_mx(out=words[:, cols].bitcast(FP8X4), scales=scales[:, cols], in_=h[:, r])
-            else:
-                nc.vector.quantize_mx(
-                    out=words[:].bitcast(FP8X4), scales=scales[:], in_=h.rearrange("p r c -> p (r c)")
-                )
+            nc.vector.quantize_mx(out=words[:].bitcast(FP8X4), scales=scales[:], in_=h.rearrange("p r c -> p (r c)"))
             hidden_q[(e, half)] = (words, scales)
 
         def project_back(e, half, acc):
@@ -236,13 +228,7 @@ def tile_routed_moe_kernel(tc, xT, w1, w3, w2, gate, offs, pos1, pos2, out):
                     acc = psum_y.tile([P, C], F32, name="acc_y")
                     project_back(e, half, acc[:, 0:HALF])
                     a = e * C + half * HALF
-                    nc.scalar.copy(y_all[:, a : a + HALF], acc[:, 0:HALF])
-
-        def hide_expert(e):
-            for half in range(2):
-                hide(e, half)
-            for half in range(2):
-                quantise_h(e, half)
+                    (nc.scalar.copy, nc.vector.tensor_copy)[half](y_all[:, a : a + HALF], acc[:, 0:HALF])
 
         nc.gpsimd.memset(x_bytes[:], 0)
         for s in range(PASSES):
@@ -251,7 +237,7 @@ def tile_routed_moe_kernel(tc, xT, w1, w3, w2, gate, offs, pos1, pos2, out):
             )
             if s == 0:
                 nc.sync.dma_start(offs_t[:], offs)
-        load_w2(w2_early, 0, EARLY_W2)
+        load_w2(w2_early[:], 0, EARLY_W2)
         matrices = [(w, e) for e in range(E) for w in range(2)]
         for w, e in matrices[:AHEAD]:
             load(w, e)
@@ -269,13 +255,15 @@ def tile_routed_moe_kernel(tc, xT, w1, w3, w2, gate, offs, pos1, pos2, out):
                 )
             gather_words(0, s)
         gather_bytes(0)
-        cast_w2(0, EARLY_W2)
+        cast_w2(0, 2)
+        cast_w2(2, 3)
 
         for i, (w, e) in enumerate(matrices):
             if i + AHEAD < len(matrices):
                 load(*matrices[i + AHEAD])
             if i + AHEAD == len(matrices):
-                load_w2(w2_late, EARLY_W2, E)
+                load_w2(w2_late[:, 0:1], EARLY_W2, EARLY_W2 + 1)
+                load_w2(w2_late[:, 1:], EARLY_W2 + 1, E)
                 nc.sync.dma_start(pos1_t[:], pos1)
                 nc.sync.dma_start(pos2_t[:], pos2)
                 nc.sync.dma_start(out=gate_t[:], in_=gate.rearrange("r p t -> p r t"))
@@ -285,41 +273,52 @@ def tile_routed_moe_kernel(tc, xT, w1, w3, w2, gate, offs, pos1, pos2, out):
             elif whole(w, e):
                 order = ((1, 0), (0, P))
             else:
-                order = ((0, END_SHARE if last else SHARE), (1, SHARE))
+                order = ((0, SHARES[w][0]), (1, SHARES[w][1]))
             cast_w(w, e, *order[0])
             if whole(w, e):
                 cast_w(w, e, *order[1])
             if w == 0 and e > 0:
-                hide_expert(e - 1)
+                hide(e - 1, 0)
+                if whole(w, e):
+                    hide(e - 1, 1)
+                    quantise_h(e - 1, 0)
             quantise_w(w, e, order[0][0])
+            if w == 0 and e > 0 and not whole(w, e):
+                hide(e - 1, 1)
+                quantise_h(e - 1, 0)
             if not whole(w, e):
                 cast_w(w, e, *order[1])
             if w == 1:
                 for half in range(2):
                     rectify(e, half)
+            elif e > 0:
+                quantise_h(e - 1, 1)
             quantise_w(w, e, order[1][0])
             for half in range(2):
                 project(w, e, half)
             if w == 0 and 0 < e <= EARLY_W2:
                 finish_expert(e - 1)
             if i == 0:
-                quantise_w2(0, EARLY_W2)
+                quantise_w2(0, 2)
+                quantise_w2(2, 3)
                 for q in range(1, SLOTS // SLICE):
                     gather_words(q, 0)
                     gather_words(q, 1)
                     gather_bytes(q)
         for e in range(EARLY_W2, E):
             cast_w2(e, e + 1)
-        hide(E - 1, 0)
-        quantise_w2(E - 2, E - 1)
-        hide(E - 1, 1)
-        quantise_w2(E - 1, E)
-        finish_expert(E - 2)
+        for half in range(2):
+            hide(E - 1, half)
+        quantise_w2(E - 3, E - 2)
+        finish_expert(E - 3)
         for half in range(2):
             quantise_h(E - 1, half)
+        quantise_w2(E - 2, E - 1)
+        quantise_w2(E - 1, E)
+        finish_expert(E - 2)
         finish_expert(E - 1)
 
-        pieces = ((0, 512), (512, T))
+        pieces = ((0, 640), (640, T))
         products = {}
 
         def fetch(piece, which, pos_t):
@@ -339,6 +338,6 @@ def tile_routed_moe_kernel(tc, xT, w1, w3, w2, gate, offs, pos1, pos2, out):
         fetch(pieces[0], 0, pos1_t)
         fetch(pieces[0], 1, pos2_t)
         fetch(pieces[1], 0, pos1_t)
-        fetch(pieces[1], 1, pos2_t)
         finish(pieces[0])
+        fetch(pieces[1], 1, pos2_t)
         finish(pieces[1])

@@ -119,11 +119,11 @@ def tile_routed_moe_kernel(tc, xT, w1, w3, w2, gate, offs, pos1, pos2, out):
                 )
             quantised[(w, e, s)] = (words, scales)
 
-        def cast_w2(a, b):
+        def cast_w2(a, b, copy):
             w_bf = keep.tile([P, (b - a) * N * PACK], BF16, name=f"w2_bf{a}", align_bytes=64)
             for e in range(a, b):
                 raw = w2_early[:, e] if e < EARLY_W2 else w2_late[:, e - EARLY_W2]
-                nc.scalar.copy(
+                copy(
                     w_bf[:, (e - a) * K_PASS : (e - a + 1) * K_PASS].rearrange("p (c i t) -> p c t i", i=4, t=PACK),
                     raw.rearrange("p t (c i) -> p c t i", i=4),
                 )
@@ -175,7 +175,8 @@ def tile_routed_moe_kernel(tc, xT, w1, w3, w2, gate, offs, pos1, pos2, out):
             if e < E - 1:
                 dead = staged(1, e)[:, s, :, half * HALF : (half + 1) * HALF]
             else:
-                dead = last_half(1)[:, 2 * half : 2 * half + 2]
+                rows = staged(1, e)[:, s].rearrange("p k (c x) -> p (k c) x", c=2)
+                dead = rows[:, :, half * HALF // 2 : (half + 1) * HALF // 2]
             r = dead.rearrange("p k (n t) -> p k n t", t=PACK)
             nc.scalar.activation(r, by_slot(sums[(0, e, half)], r.shape[1]), RELU)
             relus[(e, half)] = r
@@ -218,11 +219,14 @@ def tile_routed_moe_kernel(tc, xT, w1, w3, w2, gate, offs, pos1, pos2, out):
 
         def finish_expert(e):
             if e < E - 1:
-                acc = psum_y.tile([P, C], F32, name="acc_y")
+                if e == EARLY_W2:
+                    acc = sums[(1, E - 1, 1)][:].rearrange("p t n -> p (t n)")
+                else:
+                    acc = psum_y.tile([P, C], F32, name="acc_y")
                 for half in range(2):
                     project_back(e, half, acc[:, half * HALF : (half + 1) * HALF])
                 copy = nc.vector.tensor_copy if e < EARLY_W2 else nc.scalar.copy
-                copy(y_all[:, e * C : (e + 1) * C], acc[:])
+                copy(y_all[:, e * C : (e + 1) * C], acc[:, 0:C])
             else:
                 for half in range(2):
                     acc = psum_y.tile([P, C], F32, name="acc_y")
@@ -255,8 +259,8 @@ def tile_routed_moe_kernel(tc, xT, w1, w3, w2, gate, offs, pos1, pos2, out):
                 )
             gather_words(0, s)
         gather_bytes(0)
-        cast_w2(0, 2)
-        cast_w2(2, 3)
+        cast_w2(0, 2, nc.scalar.copy)
+        cast_w2(2, 3, nc.scalar.copy)
 
         for i, (w, e) in enumerate(matrices):
             if i + AHEAD < len(matrices):
@@ -305,11 +309,12 @@ def tile_routed_moe_kernel(tc, xT, w1, w3, w2, gate, offs, pos1, pos2, out):
                     gather_words(q, 0)
                     gather_words(q, 1)
                     gather_bytes(q)
-        for e in range(EARLY_W2, E):
-            cast_w2(e, e + 1)
+        cast_w2(E - 3, E - 2, nc.vector.tensor_copy)
+        quantise_w2(E - 3, E - 2)
+        for e in range(E - 2, E):
+            cast_w2(e, e + 1, nc.scalar.copy)
         for half in range(2):
             hide(E - 1, half)
-        quantise_w2(E - 3, E - 2)
         finish_expert(E - 3)
         for half in range(2):
             quantise_h(E - 1, half)

@@ -26,8 +26,7 @@ RING = 5
 WHOLE = 8
 EARLY_W2 = 3
 SHARES = ((40, 96), (64, 64))
-LAST_SHARE = 22
-FIRST_HALF_SHARE = 48
+LAST_PIECES = ((0, 64, 48), (64, 96, 16), (96, 128, 10))
 LAST = (1, E - 1, PASSES - 1)
 AHEAD = 3
 X_SHARE = 80
@@ -73,9 +72,9 @@ def tile_routed_moe_kernel(tc, xT, w1, w3, w2, gate, offs, pos1, pos2, out):
         def whole(w, e):
             return 2 * e + w < WHOLE
 
-        def last_half(c):
+        def last_piece(a, b):
             rows = staged(*LAST[:2])[:, LAST[2]].rearrange("p k c -> p (k c)")
-            return rows[:, c * 2 * H : (c + 1) * 2 * H].rearrange("p (k c) -> p k c", k=PACK)
+            return rows[:, a * PACK * PACK : b * PACK * PACK].rearrange("p (k c) -> p k c", k=PACK)
 
         def load(w, e):
             src = (w1, w3)[w][e].rearrange("(s p t) c -> p s t c", s=PASSES, t=PACK)
@@ -86,8 +85,8 @@ def tile_routed_moe_kernel(tc, xT, w1, w3, w2, gate, offs, pos1, pos2, out):
                     if (w, e, s) != LAST:
                         nc.sync.dma_start(out=staged(w, e)[:, s], in_=src[:, s])
                     else:
-                        for c in range(2):
-                            nc.sync.dma_start(out=last_half(c), in_=src[:, s, :, c * H // 2 : (c + 1) * H // 2])
+                        for a, b, m in LAST_PIECES:
+                            nc.sync.dma_start(out=last_piece(a, b), in_=src[:, s, :, a * PACK : b * PACK])
 
         def load_w2(tile, a, b):
             nc.sync.dma_start(out=tile, in_=w2[a:b].rearrange("e (p t) n -> p e t n", t=PACK))
@@ -98,7 +97,7 @@ def tile_routed_moe_kernel(tc, xT, w1, w3, w2, gate, offs, pos1, pos2, out):
             if (w, e, s) != LAST:
                 parts = [(staged(w, e)[:, s], dst, scalar_m)]
             else:
-                parts = [(last_half(0), dst[:, 0 : P // 2], FIRST_HALF_SHARE), (last_half(1), dst[:, P // 2 : P], LAST_SHARE)]
+                parts = [(last_piece(a, b), dst[:, a:b], m) for a, b, m in LAST_PIECES]
             for raw, to, m in parts:
                 src = raw.rearrange("p k (m t) -> p m k t", t=PACK)
                 if m > 0:
@@ -175,8 +174,8 @@ def tile_routed_moe_kernel(tc, xT, w1, w3, w2, gate, offs, pos1, pos2, out):
             if e < E - 1:
                 dead = staged(1, e)[:, s, :, half * HALF : (half + 1) * HALF]
             else:
-                rows = staged(1, e)[:, s].rearrange("p k (c x) -> p (k c) x", c=2)
-                dead = rows[:, :, half * HALF // 2 : (half + 1) * HALF // 2]
+                rows = staged(1, e)[:, s].rearrange("p k (c x) -> p (k c) x", c=4)
+                dead = rows[:, :, half * HALF // 4 : (half + 1) * HALF // 4]
             r = dead.rearrange("p k (n t) -> p k n t", t=PACK)
             nc.scalar.activation(r, by_slot(sums[(0, e, half)], r.shape[1]), RELU)
             relus[(e, half)] = r

@@ -24,12 +24,20 @@ SLICE = 512
 HALF = 128
 RING = 5
 WHOLE = 8
-EARLY_W2 = 3
-SHARES = ((40, 96), (64, 64))
-LAST_PIECES = ((0, 64, 48), (64, 96, 16), (96, 128, 10))
+EARLY_W2 = 1
+WHOLE_SHARES = ((128, 24), (112, 0))
+SHARES = ((40, 96), (64, 40))
+LAST_SHARES = ((64, 72), (56, 0))
+LAST_PIECES = ((0, 64, 44), (64, 96, 20), (96, 128, 10))
+RELU_AT = (2, 2)
+PREQ = False
+GCAST = 1
+LATE_LOADS = ((1, 2), (2, 3), (3, 4), (4, 5))
+VCOPY = 4
+CUT = 512
 LAST = (1, E - 1, PASSES - 1)
 AHEAD = 3
-X_SHARE = 80
+X_SHARE = (128, 40)
 SCALE_ROW = (0, 4)
 
 
@@ -49,11 +57,12 @@ def tile_routed_moe_kernel(tc, xT, w1, w3, w2, gate, offs, pos1, pos2, out):
         x_bf = [keep.tile([P, T * PACK], BF16, name=f"x_bf{s}", align_bytes=64) for s in range(PASSES)]
         x_words = [keep.tile([P, T], U32, name=f"x_words{s}", align_bytes=64) for s in range(PASSES)]
         x_bytes = keep.tile([P, T], U8, name="x_bytes", align_bytes=64)
-        y_all = keep.tile([P, SLOTS], F32, name="y_all")
+        y_all = keep.tile([P, SLOTS], F32, name="y_all", align_bytes=256)
         gate_t = keep.tile([P, 2, T], F32, name="gate_t", align_bytes=256)
         ring = [keep.tile([P, PASSES, PACK, H], F32, name=f"ring{r}", align_bytes=256) for r in range(RING)]
         w2_early = keep.tile([P, EARLY_W2, PACK, N], F32, name="w2_early", align_bytes=256)
-        w2_late = keep.tile([P, E - EARLY_W2, PACK, N], F32, name="w2_late", align_bytes=256)
+        w2_late = keep.tile([P, E - 1 - EARLY_W2, PACK, N], F32, name="w2_late", align_bytes=256)
+        w2_last = y_all[:, (E - 5) * C : (E - 1) * C].rearrange("p (e t n) -> p e t n", e=1, t=PACK)[:, :, :, 0:N]
         slot_words = {}
         slot_bytes = {}
         cast = {}
@@ -91,47 +100,58 @@ def tile_routed_moe_kernel(tc, xT, w1, w3, w2, gate, offs, pos1, pos2, out):
         def load_w2(tile, a, b):
             nc.sync.dma_start(out=tile, in_=w2[a:b].rearrange("e (p t) n -> p e t n", t=PACK))
 
-        def cast_w(w, e, s, scalar_m):
-            w_bf = work.tile([P, H * PACK], BF16, name="w_bf", align_bytes=64, bufs=4)
-            dst = w_bf[:].rearrange("p (t m k) -> p m k t", t=PACK, k=PACK)
-            if (w, e, s) != LAST:
-                parts = [(staged(w, e)[:, s], dst, scalar_m)]
-            else:
-                parts = [(last_piece(a, b), dst[:, a:b], m) for a, b, m in LAST_PIECES]
-            for raw, to, m in parts:
-                src = raw.rearrange("p k (m t) -> p m k t", t=PACK)
-                if m > 0:
-                    nc.scalar.copy(to[:, 0:m], src[:, 0:m])
-                if m < to.shape[1]:
-                    nc.vector.tensor_copy(to[:, m:], src[:, m:])
-            cast[(w, e, s)] = w_bf
+        def share_cast(raw, to, m):
+            src = raw.rearrange("p k (m t) -> p m k t", t=PACK)
+            if m > 0:
+                nc.scalar.copy(to[:, 0:m], src[:, 0:m])
+            if m < to.shape[1]:
+                nc.vector.tensor_copy(to[:, m:], src[:, m:])
 
-        def quantise_w(w, e, s):
+        def cast_tile(w, e, s):
+            w_bf = work.tile([P, H * PACK], BF16, name="w_bf", align_bytes=64, bufs=4)
+            cast[(w, e, s)] = w_bf
+            return w_bf[:].rearrange("p (t m k) -> p m k t", t=PACK, k=PACK)
+
+        def cast_w(w, e, s, scalar_m):
+            share_cast(staged(w, e)[:, s], cast_tile(w, e, s), scalar_m)
+
+        def code_tiles(w, e, s):
             words = quant.tile([P, H], U32, name="w_words", align_bytes=64)
             scales = quant.tile([P, H], U8, name="w_scales", align_bytes=64)
-            step = P if (w, e, s) == LAST else H
-            for a in range(0, H, step):
-                nc.vector.quantize_mx(
-                    out=words[:, a : a + step].bitcast(FP8X4),
-                    scales=scales[:, a : a + step],
-                    in_=cast[(w, e, s)][:, PACK * a : PACK * (a + step)],
-                )
             quantised[(w, e, s)] = (words, scales)
 
+        def quantise_columns(w, e, s, a, b):
+            words, scales = quantised[(w, e, s)]
+            nc.vector.quantize_mx(
+                out=words[:, a:b].bitcast(FP8X4), scales=scales[:, a:b], in_=cast[(w, e, s)][:, PACK * a : PACK * b]
+            )
+
+        def quantise_w(w, e, s):
+            code_tiles(w, e, s)
+            quantise_columns(w, e, s, 0, H)
+
         def cast_w2(a, b, copy):
-            w_bf = keep.tile([P, (b - a) * N * PACK], BF16, name=f"w2_bf{a}", align_bytes=64)
+            if a == EARLY_W2 + 1 and GCAST:
+                w_bf = cast[LAST][:, (PACK - 1) * K_PASS :]
+            else:
+                own = keep.tile([P, (b - a) * N * PACK], BF16, name=f"w2_bf{a}", align_bytes=64)
+                w_bf = own[:]
             for e in range(a, b):
-                raw = w2_early[:, e] if e < EARLY_W2 else w2_late[:, e - EARLY_W2]
+                raw = w2_early[:, e] if e < EARLY_W2 else w2_late[:, e - EARLY_W2] if e < E - 1 else w2_last[:, 0]
+                order = "c i t" if e == EARLY_W2 + 1 else "c t i"
                 copy(
-                    w_bf[:, (e - a) * K_PASS : (e - a + 1) * K_PASS].rearrange("p (c i t) -> p c t i", i=4, t=PACK),
-                    raw.rearrange("p t (c i) -> p c t i", i=4),
+                    w_bf[:, (e - a) * K_PASS : (e - a + 1) * K_PASS].rearrange("p (c i t) -> p " + order, i=4, t=PACK),
+                    raw.rearrange("p t (c i) -> p " + order, i=4),
                 )
             w2_cast[a] = w_bf
+
+        def gpsimd_cast(to, src):
+            nc.gpsimd.tensor_scalar(to, src, 1.0, 0.0, MULT, ADD)
 
         def quantise_w2(a, b):
             words = keep.tile([P, (b - a) * N], U32, name=f"w2_words{a}", align_bytes=64)
             scales = keep.tile([P, (b - a) * N], U8, name=f"w2_scales{a}", align_bytes=64)
-            nc.vector.quantize_mx(out=words[:].bitcast(FP8X4), scales=scales[:], in_=w2_cast[a][:])
+            nc.vector.quantize_mx(out=words[:].bitcast(FP8X4), scales=scales[:], in_=w2_cast[a])
             for e in range(a, b):
                 cols = slice((e - a) * N, (e - a + 1) * N)
                 w2_quantised[e] = (words[:, cols], scales[:, cols])
@@ -149,22 +169,23 @@ def tile_routed_moe_kernel(tc, xT, w1, w3, w2, gate, offs, pos1, pos2, out):
             nc.vector.tensor_copy(scales[:], x_bytes[:].indirect(offs_t[:, a // 16 : b // 16]))
             slot_bytes[q] = scales
 
-        def project(w, e, half):
+        def project(w, e, half, s, first):
             q, a = divmod(e * C + half * HALF, SLICE)
-            acc = psum.tile([P, PACK, HALF], F32, name=("acc_a", "acc_b")[w])
-            for t in range(PACK):
-                for s in range(PASSES):
-                    words, scales = quantised[(w, e, s)]
-                    nc.tensor.matmul_mx(
-                        out=acc[:, t, :],
-                        lhsT=words[:, t * P : (t + 1) * P].bitcast(FP8X4),
-                        lhsT_scale=scales[:, t * P : (t + 1) * P],
-                        rhs=slot_words[q][:, s, a : a + HALF].bitcast(FP8X4),
-                        rhs_scale=slot_bytes[q][SCALE_ROW[s] : P, a : a + HALF],
-                        start=(s == 0),
-                        stop=(s == PASSES - 1),
-                    )
-            sums[(w, e, half)] = acc
+            if first:
+                acc = psum.tile([P, PACK, HALF], F32, name=("acc_a", "acc_b")[w])
+                sums[(w, e, half)] = acc
+            words, scales = quantised[(w, e, s)]
+            tiles = list(range(PACK)) if first or half == 0 else list(reversed(range(PACK)))
+            for t in tiles:
+                nc.tensor.matmul_mx(
+                    out=sums[(w, e, half)][:, t, :],
+                    lhsT=words[:, t * P : (t + 1) * P].bitcast(FP8X4),
+                    lhsT_scale=scales[:, t * P : (t + 1) * P],
+                    rhs=slot_words[q][:, s, a : a + HALF].bitcast(FP8X4),
+                    rhs_scale=slot_bytes[q][SCALE_ROW[s] : P, a : a + HALF],
+                    start=(first and t == tiles[0]),
+                    stop=(not first and t == tiles[-1]),
+                )
 
         def by_slot(acc, rows):
             return acc[:].rearrange("p t (k n) -> p k n t", k=rows)
@@ -174,8 +195,8 @@ def tile_routed_moe_kernel(tc, xT, w1, w3, w2, gate, offs, pos1, pos2, out):
             if e < E - 1:
                 dead = staged(1, e)[:, s, :, half * HALF : (half + 1) * HALF]
             else:
-                rows = staged(1, e)[:, s].rearrange("p k (c x) -> p (k c) x", c=4)
-                dead = rows[:, :, half * HALF // 4 : (half + 1) * HALF // 4]
+                rows = staged(1, e)[:, 1].rearrange("p k c -> p (k c)").rearrange("p (k c) -> p k c", k=2)
+                dead = rows[:, :, (RELU_AT[0] * 2 - 2 + half) * C : (RELU_AT[0] * 2 - 1 + half) * C]
             r = dead.rearrange("p k (n t) -> p k n t", t=PACK)
             nc.scalar.activation(r, by_slot(sums[(0, e, half)], r.shape[1]), RELU)
             relus[(e, half)] = r
@@ -197,8 +218,8 @@ def tile_routed_moe_kernel(tc, xT, w1, w3, w2, gate, offs, pos1, pos2, out):
             hidden[(e, half)] = h
 
         def quantise_h(e, half):
-            words = work.tile([P, HALF], U32, name="h_words", align_bytes=64, bufs=6)
-            scales = work.tile([P, HALF], U8, name="h_scales", align_bytes=64, bufs=6)
+            words = work.tile([P, HALF], U32, name="h_words", align_bytes=64, bufs=2 * E)
+            scales = work.tile([P, HALF], U8, name="h_scales", align_bytes=64, bufs=2 * E)
             h = hidden[(e, half)]
             nc.vector.quantize_mx(out=words[:].bitcast(FP8X4), scales=scales[:], in_=h.rearrange("p r c -> p (r c)"))
             hidden_q[(e, half)] = (words, scales)
@@ -217,21 +238,21 @@ def tile_routed_moe_kernel(tc, xT, w1, w3, w2, gate, offs, pos1, pos2, out):
             )
 
         def finish_expert(e):
-            if e < E - 1:
-                if e == EARLY_W2:
-                    acc = sums[(1, E - 1, 1)][:].rearrange("p t n -> p (t n)")
+            if e == E - 1:
+                for half in range(2):
+                    acc = sums[(0, e, half)][:, 0, :]
+                    project_back(e, half, acc)
+                    a = e * C + half * HALF
+                    (nc.scalar.copy, nc.vector.tensor_copy)[half](y_all[:, a : a + HALF], acc)
+            else:
+                if e < EARLY_W2:
+                    acc = sums[(0, e + 1, 0)][:].rearrange("p t n -> p (t n)")
                 else:
                     acc = psum_y.tile([P, C], F32, name="acc_y")
                 for half in range(2):
                     project_back(e, half, acc[:, half * HALF : (half + 1) * HALF])
-                copy = nc.vector.tensor_copy if e < EARLY_W2 else nc.scalar.copy
+                copy = nc.vector.tensor_copy if e == VCOPY else nc.scalar.copy
                 copy(y_all[:, e * C : (e + 1) * C], acc[:, 0:C])
-            else:
-                for half in range(2):
-                    acc = psum_y.tile([P, C], F32, name="acc_y")
-                    project_back(e, half, acc[:, 0:HALF])
-                    a = e * C + half * HALF
-                    (nc.scalar.copy, nc.vector.tensor_copy)[half](y_all[:, a : a + HALF], acc[:, 0:HALF])
 
         nc.gpsimd.memset(x_bytes[:], 0)
         for s in range(PASSES):
@@ -248,8 +269,8 @@ def tile_routed_moe_kernel(tc, xT, w1, w3, w2, gate, offs, pos1, pos2, out):
         for s in range(PASSES):
             dst = x_bf[s][:].rearrange("p (c i t) -> p c t i", i=4, t=PACK)
             src = x_raw[s][:].rearrange("p t (c i) -> p c t i", i=4)
-            nc.scalar.copy(dst[:, X_SHARE:], src[:, X_SHARE:])
-            nc.vector.tensor_copy(dst[:, 0:X_SHARE], src[:, 0:X_SHARE])
+            nc.scalar.copy(dst[:, X_SHARE[s] :], src[:, X_SHARE[s] :])
+            nc.vector.tensor_copy(dst[:, 0 : X_SHARE[s]], src[:, 0 : X_SHARE[s]])
             for a, b in ((0, 512), (512, 768)):
                 nc.vector.quantize_mx(
                     out=x_words[s][:, a:b].bitcast(FP8X4),
@@ -258,25 +279,28 @@ def tile_routed_moe_kernel(tc, xT, w1, w3, w2, gate, offs, pos1, pos2, out):
                 )
             gather_words(0, s)
         gather_bytes(0)
-        cast_w2(0, 2, nc.scalar.copy)
-        cast_w2(2, 3, nc.scalar.copy)
+        for e in range(EARLY_W2):
+            cast_w2(e, e + 1, nc.scalar.copy)
 
         for i, (w, e) in enumerate(matrices):
             if i + AHEAD < len(matrices):
                 load(*matrices[i + AHEAD])
             if i + AHEAD == len(matrices):
-                load_w2(w2_late[:, 0:1], EARLY_W2, EARLY_W2 + 1)
-                load_w2(w2_late[:, 1:], EARLY_W2 + 1, E)
+                for a, b in LATE_LOADS:
+                    load_w2(w2_late[:, a - EARLY_W2 : b - EARLY_W2], a, b)
+                load_w2(w2_last, E - 1, E)
                 nc.sync.dma_start(pos1_t[:], pos1)
                 nc.sync.dma_start(pos2_t[:], pos2)
                 nc.sync.dma_start(out=gate_t[:], in_=gate.rearrange("r p t -> p r t"))
-            last = i == len(matrices) - 1
+            if i == len(matrices) - 1:
+                break
             if i == 0:
                 order = ((1, P), (0, P))
             elif whole(w, e):
-                order = ((1, 0), (0, P))
+                order = ((1, WHOLE_SHARES[w][1]), (0, WHOLE_SHARES[w][0]))
             else:
-                order = ((0, SHARES[w][0]), (1, SHARES[w][1]))
+                shares = SHARES if e < E - 1 else LAST_SHARES
+                order = ((0, shares[w][0]), (1, shares[w][1]))
             cast_w(w, e, *order[0])
             if whole(w, e):
                 cast_w(w, e, *order[1])
@@ -286,6 +310,8 @@ def tile_routed_moe_kernel(tc, xT, w1, w3, w2, gate, offs, pos1, pos2, out):
                     hide(e - 1, 1)
                     quantise_h(e - 1, 0)
             quantise_w(w, e, order[0][0])
+            for half in range(2):
+                project(w, e, half, order[0][0], True)
             if w == 0 and e > 0 and not whole(w, e):
                 hide(e - 1, 1)
                 quantise_h(e - 1, 0)
@@ -294,35 +320,55 @@ def tile_routed_moe_kernel(tc, xT, w1, w3, w2, gate, offs, pos1, pos2, out):
             if w == 1:
                 for half in range(2):
                     rectify(e, half)
+                if 0 < e <= EARLY_W2:
+                    finish_expert(e - 1)
             elif e > 0:
                 quantise_h(e - 1, 1)
             quantise_w(w, e, order[1][0])
             for half in range(2):
-                project(w, e, half)
-            if w == 0 and 0 < e <= EARLY_W2:
-                finish_expert(e - 1)
+                project(w, e, half, order[1][0], False)
             if i == 0:
-                quantise_w2(0, 2)
-                quantise_w2(2, 3)
+                for early in range(EARLY_W2):
+                    quantise_w2(early, early + 1)
                 for q in range(1, SLOTS // SLICE):
                     gather_words(q, 0)
                     gather_words(q, 1)
                     gather_bytes(q)
-        cast_w2(E - 3, E - 2, nc.vector.tensor_copy)
-        quantise_w2(E - 3, E - 2)
-        for e in range(E - 2, E):
-            cast_w2(e, e + 1, nc.scalar.copy)
-        for half in range(2):
-            hide(E - 1, half)
-        finish_expert(E - 3)
-        for half in range(2):
-            quantise_h(E - 1, half)
-        quantise_w2(E - 2, E - 1)
-        quantise_w2(E - 1, E)
-        finish_expert(E - 2)
-        finish_expert(E - 1)
 
-        pieces = ((0, 640), (640, T))
+        late_casts = (nc.vector.tensor_copy, gpsimd_cast if GCAST else nc.scalar.copy, nc.scalar.copy)
+        w, e, s = LAST
+        cast_w(w, e, 0, LAST_SHARES[w][0])
+        dst = cast_tile(*LAST)
+        code_tiles(*LAST)
+        for j, (a, b, m) in enumerate(LAST_PIECES):
+            share_cast(last_piece(a, b), dst[:, a:b], m)
+            for half in range(2):
+                if RELU_AT[half] == j:
+                    rectify(e, half)
+            if j == 0:
+                quantise_w(w, e, 0)
+                for half in range(2):
+                    project(w, e, half, 0, True)
+                for t in range(PACK):
+                    if PREQ:
+                        quantise_columns(w, e, s, t * P, t * P + P // 2)
+        for t in range(PACK):
+            quantise_columns(w, e, s, t * P + (P // 2 if PREQ else 0), (t + 1) * P)
+        for half in range(2):
+            project(w, e, half, s, False)
+        for late in range(EARLY_W2, E):
+            cast_w2(late, late + 1, late_casts[min(late - EARLY_W2, 2)])
+        hide(e, 0)
+        hide(e, 1)
+        quantise_h(e, 0)
+        quantise_w2(EARLY_W2, EARLY_W2 + 1)
+        quantise_h(e, 1)
+        for late in range(EARLY_W2 + 1, E):
+            quantise_w2(late, late + 1)
+        for late in range(EARLY_W2, E):
+            finish_expert(late)
+
+        pieces = ((0, CUT), (CUT, T))
         products = {}
 
         def fetch(piece, which, pos_t):

@@ -1,6 +1,7 @@
 from contextlib import ExitStack
 
 import concourse.mybir as mybir
+from concourse.masks import make_identity
 
 K, T, E, C, H, N = 1024, 768, 6, 256, 512, 128
 P = 128
@@ -34,7 +35,7 @@ PREQ = False
 GCAST = 1
 LATE_LOADS = ((1, 2), (2, 3), (3, 4), (4, 5))
 VCOPY = 4
-CUT = 512
+PIECES = ((0, 256), (256, 512), (512, 768))
 LAST = (1, E - 1, PASSES - 1)
 AHEAD = 3
 X_SHARE = (128, 40)
@@ -255,6 +256,8 @@ def tile_routed_moe_kernel(tc, xT, w1, w3, w2, gate, offs, pos1, pos2, out):
                 copy(y_all[:, e * C : (e + 1) * C], acc[:, 0:C])
 
         nc.gpsimd.memset(x_bytes[:], 0)
+        identity = keep.tile([P, P], F32, name="identity")
+        make_identity(nc, identity[:])
         for s in range(PASSES):
             nc.sync.dma_start(
                 out=x_raw[s][:], in_=xT[s * K_PASS : (s + 1) * K_PASS, :].rearrange("(p t) n -> p t n", t=PACK)
@@ -368,26 +371,21 @@ def tile_routed_moe_kernel(tc, xT, w1, w3, w2, gate, offs, pos1, pos2, out):
         for late in range(EARLY_W2, E):
             finish_expert(late)
 
-        pieces = ((0, CUT), (CUT, T))
-        products = {}
-
-        def fetch(piece, which, pos_t):
-            a, b = piece
-            prod = work.tile([P, b - a], F32, name=f"prod{which}")
-            nc.vector.tensor_tensor(
-                prod[:], y_all[:].indirect(pos_t[:, a // 16 : b // 16]), gate_t[:, which, a:b], MULT
-            )
-            products[(piece, which)] = prod
-
-        def finish(piece):
-            a, b = piece
-            o = work.tile([P, b - a], F32, name="o", align_bytes=256)
-            nc.vector.tensor_tensor(o[:], products[(piece, 0)][:], products[(piece, 1)][:], ADD)
-            nc.sync.dma_start(out=out[:, a:b], in_=o[:])
-
-        fetch(pieces[0], 0, pos1_t)
-        fetch(pieces[0], 1, pos2_t)
-        fetch(pieces[1], 0, pos1_t)
-        finish(pieces[0])
-        fetch(pieces[1], 1, pos2_t)
-        finish(pieces[1])
+        for a, b in PIECES:
+            products = []
+            for which, pos_t in enumerate((pos1_t, pos2_t)):
+                prod = work.tile([P, b - a], F32, name=f"prod{which}", bufs=3)
+                nc.vector.tensor_tensor(
+                    prod[:], y_all[:].indirect(pos_t[:, a // 16 : b // 16]), gate_t[:, which, a:b], MULT
+                )
+                products.append(prod)
+            o = work.tile([P, b - a], F32, name="o", align_bytes=256, bufs=3)
+            if b < T:
+                acc = psum_y.tile([P, b - a], F32, name="acc_y")
+                for which in range(2):
+                    nc.tensor.matmul(acc[:], identity[:], products[which][:], start=(which == 0), stop=(which == 1))
+                nc.scalar.copy(o[:], acc[:])
+                nc.scalar.dma_start(out=out[:, a:b], in_=o[:])
+            else:
+                nc.vector.tensor_tensor(o[:], products[0][:], products[1][:], ADD)
+                nc.sync.dma_start(out=out[:, a:b], in_=o[:])

@@ -1,7 +1,6 @@
 from contextlib import ExitStack
 
 import concourse.mybir as mybir
-from concourse.masks import make_identity
 
 K, T, E, C, H, N = 1024, 768, 6, 256, 512, 128
 P = 128
@@ -25,17 +24,17 @@ SLICE = 512
 HALF = 128
 RING = 5
 WHOLE = 8
-EARLY_W2 = 1
+EARLY_W2 = 0
 WHOLE_SHARES = ((128, 24), (112, 0))
 SHARES = ((40, 96), (64, 40))
 LAST_SHARES = ((64, 72), (56, 0))
 LAST_PIECES = ((0, 64, 44), (64, 96, 20), (96, 128, 10))
 RELU_AT = (2, 2)
 PREQ = False
-GCAST = 1
-LATE_LOADS = ((1, 2), (2, 3), (3, 4), (4, 5))
+WARM = 3
+LATE_LOADS = ((0, 1), (1, 2), (2, 3), (3, 4), (4, 5))
 VCOPY = 4
-PIECES = ((0, 256), (256, 512), (512, 768))
+PIECES = ((0, 352), (352, 608), (608, 768))
 LAST = (1, E - 1, PASSES - 1)
 AHEAD = 3
 X_SHARE = (128, 40)
@@ -61,9 +60,8 @@ def tile_routed_moe_kernel(tc, xT, w1, w3, w2, gate, offs, pos1, pos2, out):
         y_all = keep.tile([P, SLOTS], F32, name="y_all", align_bytes=256)
         gate_t = keep.tile([P, 2, T], F32, name="gate_t", align_bytes=256)
         ring = [keep.tile([P, PASSES, PACK, H], F32, name=f"ring{r}", align_bytes=256) for r in range(RING)]
-        w2_early = keep.tile([P, EARLY_W2, PACK, N], F32, name="w2_early", align_bytes=256)
         w2_late = keep.tile([P, E - 1 - EARLY_W2, PACK, N], F32, name="w2_late", align_bytes=256)
-        w2_last = y_all[:, (E - 5) * C : (E - 1) * C].rearrange("p (e t n) -> p e t n", e=1, t=PACK)[:, :, :, 0:N]
+        w2_last = y_all[:, C : (1 + PACK) * C].rearrange("p (e t n) -> p e t n", e=1, t=PACK)[:, :, :, 0:N]
         slot_words = {}
         slot_bytes = {}
         cast = {}
@@ -132,16 +130,17 @@ def tile_routed_moe_kernel(tc, xT, w1, w3, w2, gate, offs, pos1, pos2, out):
             quantise_columns(w, e, s, 0, H)
 
         def cast_w2(a, b, copy):
-            if a == EARLY_W2 + 1 and GCAST:
-                w_bf = cast[LAST][:, (PACK - 1) * K_PASS :]
+            if a in (1, 2):
+                w_bf = cast[LAST][:, (PACK - a) * K_PASS : (PACK + 1 - a) * K_PASS]
             else:
                 own = keep.tile([P, (b - a) * N * PACK], BF16, name=f"w2_bf{a}", align_bytes=64)
                 w_bf = own[:]
             for e in range(a, b):
-                raw = w2_early[:, e] if e < EARLY_W2 else w2_late[:, e - EARLY_W2] if e < E - 1 else w2_last[:, 0]
-                order = "c i t" if e == EARLY_W2 + 1 else "c t i"
+                raw = w2_late[:, e - EARLY_W2] if e < E - 1 else w2_last[:, 0]
+                to = w_bf[:, (e - a) * K_PASS : (e - a + 1) * K_PASS]
+                order = "c i t" if e in (1, 2) else "c t i"
                 copy(
-                    w_bf[:, (e - a) * K_PASS : (e - a + 1) * K_PASS].rearrange("p (c i t) -> p " + order, i=4, t=PACK),
+                    to.rearrange("p (c i t) -> p " + order, i=4, t=PACK),
                     raw.rearrange("p t (c i) -> p " + order, i=4),
                 )
             w2_cast[a] = w_bf
@@ -238,33 +237,29 @@ def tile_routed_moe_kernel(tc, xT, w1, w3, w2, gate, offs, pos1, pos2, out):
                 stop=True,
             )
 
-        def finish_expert(e):
-            if e == E - 1:
+        def finish_experts(a, b, copy):
+            acc = psum_y.tile([P, (b - a) * C], F32, name="acc_y")
+            for e in range(a, b):
                 for half in range(2):
-                    acc = sums[(0, e, half)][:, 0, :]
-                    project_back(e, half, acc)
-                    a = e * C + half * HALF
-                    (nc.scalar.copy, nc.vector.tensor_copy)[half](y_all[:, a : a + HALF], acc)
-            else:
-                if e < EARLY_W2:
-                    acc = sums[(0, e + 1, 0)][:].rearrange("p t n -> p (t n)")
-                else:
-                    acc = psum_y.tile([P, C], F32, name="acc_y")
-                for half in range(2):
-                    project_back(e, half, acc[:, half * HALF : (half + 1) * HALF])
-                copy = nc.vector.tensor_copy if e == VCOPY else nc.scalar.copy
-                copy(y_all[:, e * C : (e + 1) * C], acc[:, 0:C])
+                    c = (e - a) * C + half * HALF
+                    project_back(e, half, acc[:, c : c + HALF])
+            copy(y_all[:, a * C : b * C], acc[:])
+
+        def finish_last():
+            e = E - 1
+            for half in range(2):
+                acc = sums[(0, e, half)][:, 0, :]
+                project_back(e, half, acc)
+                c = e * C + half * HALF
+                (nc.vector.tensor_copy, nc.scalar.copy)[half](y_all[:, c : c + HALF], acc)
 
         nc.gpsimd.memset(x_bytes[:], 0)
-        identity = keep.tile([P, P], F32, name="identity")
-        make_identity(nc, identity[:])
         for s in range(PASSES):
             nc.sync.dma_start(
                 out=x_raw[s][:], in_=xT[s * K_PASS : (s + 1) * K_PASS, :].rearrange("(p t) n -> p t n", t=PACK)
             )
             if s == 0:
                 nc.sync.dma_start(offs_t[:], offs)
-        load_w2(w2_early[:], 0, EARLY_W2)
         matrices = [(w, e) for e in range(E) for w in range(2)]
         for w, e in matrices[:AHEAD]:
             load(w, e)
@@ -323,8 +318,6 @@ def tile_routed_moe_kernel(tc, xT, w1, w3, w2, gate, offs, pos1, pos2, out):
             if w == 1:
                 for half in range(2):
                     rectify(e, half)
-                if 0 < e <= EARLY_W2:
-                    finish_expert(e - 1)
             elif e > 0:
                 quantise_h(e - 1, 1)
             quantise_w(w, e, order[1][0])
@@ -338,7 +331,7 @@ def tile_routed_moe_kernel(tc, xT, w1, w3, w2, gate, offs, pos1, pos2, out):
                     gather_words(q, 1)
                     gather_bytes(q)
 
-        late_casts = (nc.vector.tensor_copy, gpsimd_cast if GCAST else nc.scalar.copy, nc.scalar.copy)
+        late_casts = (nc.vector.tensor_copy, gpsimd_cast, gpsimd_cast, nc.scalar.copy)
         w, e, s = LAST
         cast_w(w, e, 0, LAST_SHARES[w][0])
         dst = cast_tile(*LAST)
@@ -360,7 +353,10 @@ def tile_routed_moe_kernel(tc, xT, w1, w3, w2, gate, offs, pos1, pos2, out):
         for half in range(2):
             project(w, e, half, s, False)
         for late in range(EARLY_W2, E):
-            cast_w2(late, late + 1, late_casts[min(late - EARLY_W2, 2)])
+            cast_w2(late, late + 1, late_casts[min(late, 3)])
+        idle = psum_y.tile([P, K_PASS], F32, name="acc_y")
+        for warm in range(WARM):
+            nc.tensor.matmul(idle[:], w2_cast[0][:, 0:P], w2_cast[0], start=True, stop=True)
         hide(e, 0)
         hide(e, 1)
         quantise_h(e, 0)
@@ -368,24 +364,27 @@ def tile_routed_moe_kernel(tc, xT, w1, w3, w2, gate, offs, pos1, pos2, out):
         quantise_h(e, 1)
         for late in range(EARLY_W2 + 1, E):
             quantise_w2(late, late + 1)
-        for late in range(EARLY_W2, E):
-            finish_expert(late)
+        finish_experts(0, 2, nc.scalar.copy)
+        finish_experts(2, 4, nc.vector.tensor_copy)
+        finish_experts(4, 5, nc.scalar.copy)
+        finish_last()
 
-        for a, b in PIECES:
-            products = []
-            for which, pos_t in enumerate((pos1_t, pos2_t)):
-                prod = work.tile([P, b - a], F32, name=f"prod{which}", bufs=3)
-                nc.vector.tensor_tensor(
-                    prod[:], y_all[:].indirect(pos_t[:, a // 16 : b // 16]), gate_t[:, which, a:b], MULT
-                )
-                products.append(prod)
+        first = keep.tile([P, T], F32, name="first")
+        nc.vector.tensor_tensor(first[:], y_all[:].indirect(pos1_t[:]), gate_t[:, 0, :], MULT)
+        second = {}
+
+        def fetch(a, b):
+            prod = work.tile([P, b - a], F32, name="second", bufs=3)
+            nc.vector.tensor_tensor(prod[:], y_all[:].indirect(pos2_t[:, a // 16 : b // 16]), gate_t[:, 1, a:b], MULT)
+            second[a] = prod
+
+        def finish(a, b):
             o = work.tile([P, b - a], F32, name="o", align_bytes=256, bufs=3)
-            if b < T:
-                acc = psum_y.tile([P, b - a], F32, name="acc_y")
-                for which in range(2):
-                    nc.tensor.matmul(acc[:], identity[:], products[which][:], start=(which == 0), stop=(which == 1))
-                nc.scalar.copy(o[:], acc[:])
-                nc.scalar.dma_start(out=out[:, a:b], in_=o[:])
-            else:
-                nc.vector.tensor_tensor(o[:], products[0][:], products[1][:], ADD)
-                nc.sync.dma_start(out=out[:, a:b], in_=o[:])
+            nc.vector.tensor_tensor(o[:], first[:, a:b], second[a][:], ADD)
+            nc.sync.dma_start(out=out[:, a:b], in_=o[:])
+
+        fetch(*PIECES[0])
+        for done, ahead in zip(PIECES, PIECES[1:]):
+            fetch(*ahead)
+            finish(*done)
+        finish(*PIECES[-1])

@@ -28,13 +28,13 @@ EARLY_W2 = 0
 WHOLE_SHARES = ((128, 24), (112, 0))
 SHARES = ((40, 96), (64, 40))
 LAST_SHARES = ((64, 72), (56, 0))
-LAST_PIECES = ((0, 64, 44), (64, 96, 20), (96, 128, 10))
+LAST_PIECES = ((0, 80, 52), (80, 128, 16))
 RELU_AT = (2, 2)
 PREQ = False
 WARM = 3
 LATE_LOADS = ((0, 1), (1, 2), (2, 3), (3, 4), (4, 5))
 VCOPY = 4
-PIECES = ((0, 352), (352, 608), (608, 768))
+PIECES = ((0, 384), (384, 768))
 LAST = (1, E - 1, PASSES - 1)
 AHEAD = 3
 X_SHARE = (128, 40)
@@ -61,7 +61,8 @@ def tile_routed_moe_kernel(tc, xT, w1, w3, w2, gate, offs, pos1, pos2, out):
         gate_t = keep.tile([P, 2, T], F32, name="gate_t", align_bytes=256)
         ring = [keep.tile([P, PASSES, PACK, H], F32, name=f"ring{r}", align_bytes=256) for r in range(RING)]
         w2_late = keep.tile([P, E - 1 - EARLY_W2, PACK, N], F32, name="w2_late", align_bytes=256)
-        w2_last = y_all[:, C : (1 + PACK) * C].rearrange("p (e t n) -> p e t n", e=1, t=PACK)[:, :, :, 0:N]
+        w2_last = y_all[:, 3 * HALF : 11 * HALF].rearrange("p (r c) -> p r c", r=2)[:, :, 0:C]
+        w2_last = w2_last.rearrange("p r (t n) -> p r t n", t=2)
         slot_words = {}
         slot_bytes = {}
         cast = {}
@@ -130,18 +131,18 @@ def tile_routed_moe_kernel(tc, xT, w1, w3, w2, gate, offs, pos1, pos2, out):
             quantise_columns(w, e, s, 0, H)
 
         def cast_w2(a, b, copy):
-            if a in (1, 2):
+            if a == 1:
                 w_bf = cast[LAST][:, (PACK - a) * K_PASS : (PACK + 1 - a) * K_PASS]
             else:
                 own = keep.tile([P, (b - a) * N * PACK], BF16, name=f"w2_bf{a}", align_bytes=64)
                 w_bf = own[:]
             for e in range(a, b):
-                raw = w2_late[:, e - EARLY_W2] if e < E - 1 else w2_last[:, 0]
+                raw = w2_late[:, e - EARLY_W2].rearrange("p (r t) n -> p r t n", r=2) if e < E - 1 else w2_last
                 to = w_bf[:, (e - a) * K_PASS : (e - a + 1) * K_PASS]
-                order = "c i t" if e in (1, 2) else "c t i"
+                order = "c i r t" if e == 1 else "c r t i"
                 copy(
-                    to.rearrange("p (c i t) -> p " + order, i=4, t=PACK),
-                    raw.rearrange("p t (c i) -> p " + order, i=4),
+                    to.rearrange("p (c i r t) -> p " + order, i=4, r=2, t=2),
+                    raw.rearrange("p r t (c i) -> p " + order, i=4),
                 )
             w2_cast[a] = w_bf
 
@@ -286,10 +287,10 @@ def tile_routed_moe_kernel(tc, xT, w1, w3, w2, gate, offs, pos1, pos2, out):
             if i + AHEAD == len(matrices):
                 for a, b in LATE_LOADS:
                     load_w2(w2_late[:, a - EARLY_W2 : b - EARLY_W2], a, b)
-                load_w2(w2_last, E - 1, E)
-                nc.sync.dma_start(pos1_t[:], pos1)
-                nc.sync.dma_start(pos2_t[:], pos2)
-                nc.sync.dma_start(out=gate_t[:], in_=gate.rearrange("r p t -> p r t"))
+                nc.sync.dma_start(out=w2_last, in_=w2[E - 1].rearrange("(p r t) n -> p r t n", r=2, t=2))
+                for which, (pos_t, pos) in enumerate(((pos1_t, pos1), (pos2_t, pos2))):
+                    nc.sync.dma_start(pos_t[:], pos)
+                    nc.sync.dma_start(out=gate_t[:, which, :], in_=gate[which])
             if i == len(matrices) - 1:
                 break
             if i == 0:
@@ -331,7 +332,7 @@ def tile_routed_moe_kernel(tc, xT, w1, w3, w2, gate, offs, pos1, pos2, out):
                     gather_words(q, 1)
                     gather_bytes(q)
 
-        late_casts = (nc.vector.tensor_copy, gpsimd_cast, gpsimd_cast, nc.scalar.copy)
+        late_casts = (nc.vector.tensor_copy, gpsimd_cast, nc.scalar.copy, nc.scalar.copy)
         w, e, s = LAST
         cast_w(w, e, 0, LAST_SHARES[w][0])
         dst = cast_tile(*LAST)
@@ -339,7 +340,7 @@ def tile_routed_moe_kernel(tc, xT, w1, w3, w2, gate, offs, pos1, pos2, out):
         for j, (a, b, m) in enumerate(LAST_PIECES):
             share_cast(last_piece(a, b), dst[:, a:b], m)
             for half in range(2):
-                if RELU_AT[half] == j:
+                if j == len(LAST_PIECES) - 1:
                     rectify(e, half)
             if j == 0:
                 quantise_w(w, e, 0)

@@ -31,7 +31,6 @@ LAST_SHARES = ((64, 72), (56, 0))
 LAST_PIECES = ((0, 80, 52), (80, 128, 16))
 RELU_AT = (2, 2)
 PREQ = False
-WARM = 3
 LATE_LOADS = ((0, 1), (1, 2), (2, 3), (3, 4), (4, 5))
 VCOPY = 4
 PIECES = ((0, 384), (384, 768))
@@ -355,9 +354,6 @@ def tile_routed_moe_kernel(tc, xT, w1, w3, w2, gate, offs, pos1, pos2, out):
             project(w, e, half, s, False)
         for late in range(EARLY_W2, E):
             cast_w2(late, late + 1, late_casts[min(late, 3)])
-        idle = psum_y.tile([P, K_PASS], F32, name="acc_y")
-        for warm in range(WARM):
-            nc.tensor.matmul(idle[:], w2_cast[0][:, 0:P], w2_cast[0], start=True, stop=True)
         hide(e, 0)
         hide(e, 1)
         quantise_h(e, 0)

@@ -20,24 +20,23 @@ MULT = mybir.AluOpType.mult
 ADD = mybir.AluOpType.add
 RELU = mybir.ActivationFunctionType.Relu
 
+LIST_ROWS = 16
 SLICE = 512
 HALF = 128
-RING = 5
-WHOLE = 8
-EARLY_W2 = 0
-WHOLE_SHARES = ((128, 24), (112, 0))
-SHARES = ((40, 96), (64, 40))
-LAST_SHARES = ((64, 72), (56, 0))
-LAST_PIECES = ((0, 80, 52), (80, 128, 16))
-RELU_AT = (2, 2)
-PREQ = False
-LATE_LOADS = ((0, 1), (1, 2), (2, 3), (3, 4), (4, 5))
-VCOPY = 4
-PIECES = ((0, 384), (384, 768))
-LAST = (1, E - 1, PASSES - 1)
-AHEAD = 3
-X_SHARE = (128, 40)
+RUN = 4
+X_CALLS = ((0, 512), (512, T))
 SCALE_ROW = (0, 4)
+
+RING = 5
+AHEAD = 3
+WHOLE = 8
+LAST = (1, E - 1, PASSES - 1)
+
+X_SHARE = (128, 40)
+WHOLE_SHARES = (P, 0)
+PASS_SHARES = ((40, 88), (56, 40))
+LAST_PIECES = ((0, 72, P // 2), (72, P, 0))
+OUT_PIECES = ((0, T // 2), (T // 2, T))
 
 
 def tile_routed_moe_kernel(tc, xT, w1, w3, w2, gate, offs, pos1, pos2, out):
@@ -49,9 +48,9 @@ def tile_routed_moe_kernel(tc, xT, w1, w3, w2, gate, offs, pos1, pos2, out):
         psum = ctx.enter_context(tc.psum_pool(name="psum", bufs=2))
         psum_y = ctx.enter_context(tc.psum_pool(name="psum_y", bufs=4))
 
-        offs_t = keep.tile([P, SLOTS // 16], U16, name="offs_t")
-        pos1_t = keep.tile([P, T // 16], U16, name="pos1_t")
-        pos2_t = keep.tile([P, T // 16], U16, name="pos2_t")
+        offs_t = keep.tile([P, SLOTS // LIST_ROWS], U16, name="offs_t")
+        pos1_t = keep.tile([P, T // LIST_ROWS], U16, name="pos1_t")
+        pos2_t = keep.tile([P, T // LIST_ROWS], U16, name="pos2_t")
         x_raw = [keep.tile([P, PACK, T], F32, name=f"x_raw{s}", align_bytes=256) for s in range(PASSES)]
         x_bf = [keep.tile([P, T * PACK], BF16, name=f"x_bf{s}", align_bytes=64) for s in range(PASSES)]
         x_words = [keep.tile([P, T], U32, name=f"x_words{s}", align_bytes=64) for s in range(PASSES)]
@@ -59,9 +58,9 @@ def tile_routed_moe_kernel(tc, xT, w1, w3, w2, gate, offs, pos1, pos2, out):
         y_all = keep.tile([P, SLOTS], F32, name="y_all", align_bytes=256)
         gate_t = keep.tile([P, 2, T], F32, name="gate_t", align_bytes=256)
         ring = [keep.tile([P, PASSES, PACK, H], F32, name=f"ring{r}", align_bytes=256) for r in range(RING)]
-        w2_late = keep.tile([P, E - 1 - EARLY_W2, PACK, N], F32, name="w2_late", align_bytes=256)
+        w2_raw = keep.tile([P, E - 1, PACK, N], F32, name="w2_raw", align_bytes=256)
         w2_last = y_all[:, 3 * HALF : 11 * HALF].rearrange("p (r c) -> p r c", r=2)[:, :, 0:C]
-        w2_last = w2_last.rearrange("p r (t n) -> p r t n", t=2)
+        w2_last = w2_last.rearrange("p r (u n) -> p r u n", u=2)
         slot_words = {}
         slot_bytes = {}
         cast = {}
@@ -72,7 +71,6 @@ def tile_routed_moe_kernel(tc, xT, w1, w3, w2, gate, offs, pos1, pos2, out):
         sums = {}
         hidden = {}
         hidden_q = {}
-        results = {}
 
         def staged(w, e):
             return ring[(2 * e + w) % RING]
@@ -93,18 +91,24 @@ def tile_routed_moe_kernel(tc, xT, w1, w3, w2, gate, offs, pos1, pos2, out):
                     if (w, e, s) != LAST:
                         nc.sync.dma_start(out=staged(w, e)[:, s], in_=src[:, s])
                     else:
-                        for a, b, m in LAST_PIECES:
+                        for a, b, scalar_m in LAST_PIECES:
                             nc.sync.dma_start(out=last_piece(a, b), in_=src[:, s, :, a * PACK : b * PACK])
 
-        def load_w2(tile, a, b):
-            nc.sync.dma_start(out=tile, in_=w2[a:b].rearrange("e (p t) n -> p e t n", t=PACK))
+        def load_tail():
+            for e in range(E - 1):
+                src = w2[e : e + 1].rearrange("e (p t) n -> p e t n", t=PACK)
+                nc.sync.dma_start(out=w2_raw[:, e : e + 1], in_=src)
+            nc.sync.dma_start(out=w2_last, in_=w2[E - 1].rearrange("(p r u) n -> p r u n", r=2, u=2))
+            for which, (pos_t, pos) in enumerate(((pos1_t, pos1), (pos2_t, pos2))):
+                nc.sync.dma_start(pos_t[:], pos)
+                nc.sync.dma_start(out=gate_t[:, which, :], in_=gate[which])
 
-        def share_cast(raw, to, m):
+        def share_cast(raw, to, scalar_m):
             src = raw.rearrange("p k (m t) -> p m k t", t=PACK)
-            if m > 0:
-                nc.scalar.copy(to[:, 0:m], src[:, 0:m])
-            if m < to.shape[1]:
-                nc.vector.tensor_copy(to[:, m:], src[:, m:])
+            if scalar_m > 0:
+                nc.scalar.copy(to[:, 0:scalar_m], src[:, 0:scalar_m])
+            if scalar_m < to.shape[1]:
+                nc.vector.tensor_copy(to[:, scalar_m:], src[:, scalar_m:])
 
         def cast_tile(w, e, s):
             w_bf = work.tile([P, H * PACK], BF16, name="w_bf", align_bytes=64, bufs=4)
@@ -129,53 +133,50 @@ def tile_routed_moe_kernel(tc, xT, w1, w3, w2, gate, offs, pos1, pos2, out):
             code_tiles(w, e, s)
             quantise_columns(w, e, s, 0, H)
 
-        def cast_w2(a, b, copy):
-            if a == 1:
-                w_bf = cast[LAST][:, (PACK - a) * K_PASS : (PACK + 1 - a) * K_PASS]
-            else:
-                own = keep.tile([P, (b - a) * N * PACK], BF16, name=f"w2_bf{a}", align_bytes=64)
-                w_bf = own[:]
-            for e in range(a, b):
-                raw = w2_late[:, e - EARLY_W2].rearrange("p (r t) n -> p r t n", r=2) if e < E - 1 else w2_last
-                to = w_bf[:, (e - a) * K_PASS : (e - a + 1) * K_PASS]
-                order = "c i r t" if e == 1 else "c r t i"
-                copy(
-                    to.rearrange("p (c i r t) -> p " + order, i=4, r=2, t=2),
-                    raw.rearrange("p r t (c i) -> p " + order, i=4),
-                )
-            w2_cast[a] = w_bf
+        def w2_views(e, to, order):
+            raw = w2_raw[:, e].rearrange("p (r u) n -> p r u n", r=2) if e < E - 1 else w2_last
+            w2_cast[e] = to
+            return (
+                to.rearrange("p (c j r u) -> p " + order, j=RUN, r=2, u=2),
+                raw.rearrange("p r u (c j) -> p " + order, j=RUN),
+            )
 
-        def gpsimd_cast(to, src):
+        def cast_w2(e, copy):
+            w_bf = keep.tile([P, N * PACK], BF16, name=f"w2_bf{e}", align_bytes=64)
+            copy(*w2_views(e, w_bf[:], "c r u j"))
+
+        def cast_w2_on_gpsimd(e):
+            to, src = w2_views(e, cast[LAST][:, (PACK - 1) * K_PASS :], "c j r u")
             nc.gpsimd.tensor_scalar(to, src, 1.0, 0.0, MULT, ADD)
 
-        def quantise_w2(a, b):
-            words = keep.tile([P, (b - a) * N], U32, name=f"w2_words{a}", align_bytes=64)
-            scales = keep.tile([P, (b - a) * N], U8, name=f"w2_scales{a}", align_bytes=64)
-            nc.vector.quantize_mx(out=words[:].bitcast(FP8X4), scales=scales[:], in_=w2_cast[a])
-            for e in range(a, b):
-                cols = slice((e - a) * N, (e - a + 1) * N)
-                w2_quantised[e] = (words[:, cols], scales[:, cols])
+        def quantise_w2(e):
+            words = keep.tile([P, N], U32, name=f"w2_words{e}", align_bytes=64)
+            scales = keep.tile([P, N], U8, name=f"w2_scales{e}", align_bytes=64)
+            nc.vector.quantize_mx(out=words[:].bitcast(FP8X4), scales=scales[:], in_=w2_cast[e])
+            w2_quantised[e] = (words[:], scales[:])
+
+        def list_columns(tile, a, b):
+            return tile[:, a // LIST_ROWS : b // LIST_ROWS]
 
         def gather_words(q, s):
-            a, b = q * SLICE, (q + 1) * SLICE
             if s == 0:
-                words = work.tile([P, PASSES, SLICE], U32, name="slot_words", align_bytes=64, bufs=3)
+                words = work.tile([P, PASSES, SLICE], U32, name="slot_words", align_bytes=64, bufs=SLOTS // SLICE)
                 slot_words[q] = words
-            nc.vector.tensor_copy(slot_words[q][:, s, :], x_words[s][:].indirect(offs_t[:, a // 16 : b // 16]))
+            offsets = list_columns(offs_t, q * SLICE, (q + 1) * SLICE)
+            nc.vector.tensor_copy(slot_words[q][:, s, :], x_words[s][:].indirect(offsets))
 
         def gather_bytes(q):
-            a, b = q * SLICE, (q + 1) * SLICE
-            scales = work.tile([P, SLICE], U8, name="slot_bytes", align_bytes=64, bufs=3)
-            nc.vector.tensor_copy(scales[:], x_bytes[:].indirect(offs_t[:, a // 16 : b // 16]))
+            scales = work.tile([P, SLICE], U8, name="slot_bytes", align_bytes=64, bufs=SLOTS // SLICE)
+            nc.vector.tensor_copy(scales[:], x_bytes[:].indirect(list_columns(offs_t, q * SLICE, (q + 1) * SLICE)))
             slot_bytes[q] = scales
 
-        def project(w, e, half, s, first):
+        def project(w, e, half, s, opens):
             q, a = divmod(e * C + half * HALF, SLICE)
-            if first:
+            if opens:
                 acc = psum.tile([P, PACK, HALF], F32, name=("acc_a", "acc_b")[w])
                 sums[(w, e, half)] = acc
             words, scales = quantised[(w, e, s)]
-            tiles = list(range(PACK)) if first or half == 0 else list(reversed(range(PACK)))
+            tiles = list(range(PACK)) if opens or half == 0 else list(reversed(range(PACK)))
             for t in tiles:
                 nc.tensor.matmul_mx(
                     out=sums[(w, e, half)][:, t, :],
@@ -183,45 +184,37 @@ def tile_routed_moe_kernel(tc, xT, w1, w3, w2, gate, offs, pos1, pos2, out):
                     lhsT_scale=scales[:, t * P : (t + 1) * P],
                     rhs=slot_words[q][:, s, a : a + HALF].bitcast(FP8X4),
                     rhs_scale=slot_bytes[q][SCALE_ROW[s] : P, a : a + HALF],
-                    start=(first and t == tiles[0]),
-                    stop=(not first and t == tiles[-1]),
+                    start=(opens and t == tiles[0]),
+                    stop=(not opens and t == tiles[-1]),
                 )
 
-        def by_slot(acc, rows):
-            return acc[:].rearrange("p t (k n) -> p k n t", k=rows)
+        def by_slot(acc):
+            return acc[:].rearrange("p t (k n) -> p k n t", k=PACK)
 
         def rectify(e, half):
-            s = 0 if whole(1, e) else 1
             if e < E - 1:
-                dead = staged(1, e)[:, s, :, half * HALF : (half + 1) * HALF]
+                rows = staged(1, e)[:, 0 if whole(1, e) else 1]
             else:
-                rows = staged(1, e)[:, 1].rearrange("p k c -> p (k c)").rearrange("p (k c) -> p k c", k=2)
-                dead = rows[:, :, (RELU_AT[0] * 2 - 2 + half) * C : (RELU_AT[0] * 2 - 1 + half) * C]
-            r = dead.rearrange("p k (n t) -> p k n t", t=PACK)
-            nc.scalar.activation(r, by_slot(sums[(0, e, half)], r.shape[1]), RELU)
+                rows = last_piece(*LAST_PIECES[0][:2])
+            r = rows[:, :, half * HALF : (half + 1) * HALF].rearrange("p k (n t) -> p k n t", t=PACK)
+            nc.scalar.activation(r, by_slot(sums[(0, e, half)]), RELU)
             relus[(e, half)] = r
 
         def hide(e, half):
             if e < E - 1:
-                s = 1 if whole(0, e + 1) else 0
-                h = staged(0, e + 1)[:, s, half, H // 2 : H].bitcast(BF16).rearrange("p (k c) -> p k c", k=2)
+                h = staged(0, e + 1)[:, 1 if whole(0, e + 1) else 0, half, H // 2 : H].bitcast(BF16)
             else:
                 h_tile = work.tile([P, HALF * PACK], BF16, name="h", align_bytes=64)
-                h = h_tile[:].rearrange("p (k c) -> p k c", k=2)
-            rows = relus[(e, half)].shape[1]
+                h = h_tile[:]
             nc.vector.tensor_tensor(
-                h.rearrange("p r (k n t) -> p r k n t", k=rows // 2, t=PACK),
-                by_slot(sums[(1, e, half)], rows).rearrange("p (r k) n t -> p r k n t", r=2),
-                relus[(e, half)].rearrange("p (r k) n t -> p r k n t", r=2),
-                MULT,
+                h.rearrange("p (k n t) -> p k n t", k=PACK, t=PACK), by_slot(sums[(1, e, half)]), relus[(e, half)], MULT
             )
             hidden[(e, half)] = h
 
         def quantise_h(e, half):
             words = work.tile([P, HALF], U32, name="h_words", align_bytes=64, bufs=2 * E)
             scales = work.tile([P, HALF], U8, name="h_scales", align_bytes=64, bufs=2 * E)
-            h = hidden[(e, half)]
-            nc.vector.quantize_mx(out=words[:].bitcast(FP8X4), scales=scales[:], in_=h.rearrange("p r c -> p (r c)"))
+            nc.vector.quantize_mx(out=words[:].bitcast(FP8X4), scales=scales[:], in_=hidden[(e, half)])
             hidden_q[(e, half)] = (words, scales)
 
         def project_back(e, half, acc):
@@ -245,13 +238,13 @@ def tile_routed_moe_kernel(tc, xT, w1, w3, w2, gate, offs, pos1, pos2, out):
                     project_back(e, half, acc[:, c : c + HALF])
             copy(y_all[:, a * C : b * C], acc[:])
 
-        def finish_last():
+        def finish_last_expert():
             e = E - 1
-            for half in range(2):
+            for half, copy in enumerate((nc.vector.tensor_copy, nc.scalar.copy)):
                 acc = sums[(0, e, half)][:, 0, :]
                 project_back(e, half, acc)
                 c = e * C + half * HALF
-                (nc.vector.tensor_copy, nc.scalar.copy)[half](y_all[:, c : c + HALF], acc)
+                copy(y_all[:, c : c + HALF], acc)
 
         nc.gpsimd.memset(x_bytes[:], 0)
         for s in range(PASSES):
@@ -265,11 +258,11 @@ def tile_routed_moe_kernel(tc, xT, w1, w3, w2, gate, offs, pos1, pos2, out):
             load(w, e)
 
         for s in range(PASSES):
-            dst = x_bf[s][:].rearrange("p (c i t) -> p c t i", i=4, t=PACK)
-            src = x_raw[s][:].rearrange("p t (c i) -> p c t i", i=4)
+            dst = x_bf[s][:].rearrange("p (c j t) -> p c t j", j=RUN, t=PACK)
+            src = x_raw[s][:].rearrange("p t (c j) -> p c t j", j=RUN)
             nc.scalar.copy(dst[:, X_SHARE[s] :], src[:, X_SHARE[s] :])
             nc.vector.tensor_copy(dst[:, 0 : X_SHARE[s]], src[:, 0 : X_SHARE[s]])
-            for a, b in ((0, 512), (512, 768)):
+            for a, b in X_CALLS:
                 nc.vector.quantize_mx(
                     out=x_words[s][:, a:b].bitcast(FP8X4),
                     scales=x_bytes[SCALE_ROW[s] : P, a:b],
@@ -277,111 +270,89 @@ def tile_routed_moe_kernel(tc, xT, w1, w3, w2, gate, offs, pos1, pos2, out):
                 )
             gather_words(0, s)
         gather_bytes(0)
-        for e in range(EARLY_W2):
-            cast_w2(e, e + 1, nc.scalar.copy)
 
-        for i, (w, e) in enumerate(matrices):
+        for i, (w, e) in enumerate(matrices[:-1]):
             if i + AHEAD < len(matrices):
                 load(*matrices[i + AHEAD])
             if i + AHEAD == len(matrices):
-                for a, b in LATE_LOADS:
-                    load_w2(w2_late[:, a - EARLY_W2 : b - EARLY_W2], a, b)
-                nc.sync.dma_start(out=w2_last, in_=w2[E - 1].rearrange("(p r t) n -> p r t n", r=2, t=2))
-                for which, (pos_t, pos) in enumerate(((pos1_t, pos1), (pos2_t, pos2))):
-                    nc.sync.dma_start(pos_t[:], pos)
-                    nc.sync.dma_start(out=gate_t[:, which, :], in_=gate[which])
-            if i == len(matrices) - 1:
-                break
+                load_tail()
             if i == 0:
-                order = ((1, P), (0, P))
-            elif whole(w, e):
-                order = ((1, WHOLE_SHARES[w][1]), (0, WHOLE_SHARES[w][0]))
+                shares = (P, P)
             else:
-                shares = SHARES if e < E - 1 else LAST_SHARES
-                order = ((0, shares[w][0]), (1, shares[w][1]))
-            cast_w(w, e, *order[0])
+                shares = WHOLE_SHARES if whole(w, e) else PASS_SHARES[w]
+            first, second = (1, 0) if whole(w, e) else (0, 1)
+            before = e - 1 if w == 0 and e > 0 else None
+            cast_w(w, e, first, shares[first])
             if whole(w, e):
-                cast_w(w, e, *order[1])
-            if w == 0 and e > 0:
-                hide(e - 1, 0)
+                cast_w(w, e, second, shares[second])
+            if before is not None:
+                hide(before, 0)
                 if whole(w, e):
-                    hide(e - 1, 1)
-                    quantise_h(e - 1, 0)
-            quantise_w(w, e, order[0][0])
+                    hide(before, 1)
+                    quantise_h(before, 0)
+            quantise_w(w, e, first)
             for half in range(2):
-                project(w, e, half, order[0][0], True)
-            if w == 0 and e > 0 and not whole(w, e):
-                hide(e - 1, 1)
-                quantise_h(e - 1, 0)
+                project(w, e, half, first, True)
             if not whole(w, e):
-                cast_w(w, e, *order[1])
+                if before is not None:
+                    hide(before, 1)
+                    quantise_h(before, 0)
+                cast_w(w, e, second, shares[second])
             if w == 1:
                 for half in range(2):
                     rectify(e, half)
-            elif e > 0:
-                quantise_h(e - 1, 1)
-            quantise_w(w, e, order[1][0])
+            if before is not None:
+                quantise_h(before, 1)
+            quantise_w(w, e, second)
             for half in range(2):
-                project(w, e, half, order[1][0], False)
+                project(w, e, half, second, False)
             if i == 0:
-                for early in range(EARLY_W2):
-                    quantise_w2(early, early + 1)
                 for q in range(1, SLOTS // SLICE):
                     gather_words(q, 0)
                     gather_words(q, 1)
                     gather_bytes(q)
 
-        late_casts = (nc.vector.tensor_copy, gpsimd_cast, nc.scalar.copy, nc.scalar.copy)
         w, e, s = LAST
-        cast_w(w, e, 0, LAST_SHARES[w][0])
+        cast_w(w, e, 0, PASS_SHARES[w][0])
         dst = cast_tile(*LAST)
         code_tiles(*LAST)
-        for j, (a, b, m) in enumerate(LAST_PIECES):
-            share_cast(last_piece(a, b), dst[:, a:b], m)
-            for half in range(2):
-                if j == len(LAST_PIECES) - 1:
-                    rectify(e, half)
-            if j == 0:
-                quantise_w(w, e, 0)
-                for half in range(2):
-                    project(w, e, half, 0, True)
-                for t in range(PACK):
-                    if PREQ:
-                        quantise_columns(w, e, s, t * P, t * P + P // 2)
+        (a, b, scalar_m), (c, d, no_scalar) = LAST_PIECES
+        share_cast(last_piece(a, b), dst[:, a:b], scalar_m)
+        for half in range(2):
+            rectify(e, half)
+        quantise_w(w, e, 0)
+        for half in range(2):
+            project(w, e, half, 0, True)
+        share_cast(last_piece(c, d), dst[:, c:d], no_scalar)
         for t in range(PACK):
-            quantise_columns(w, e, s, t * P + (P // 2 if PREQ else 0), (t + 1) * P)
+            quantise_columns(w, e, s, t * P, (t + 1) * P)
         for half in range(2):
             project(w, e, half, s, False)
-        for late in range(EARLY_W2, E):
-            cast_w2(late, late + 1, late_casts[min(late, 3)])
-        hide(e, 0)
-        hide(e, 1)
+
+        cast_w2(0, nc.vector.tensor_copy)
+        cast_w2_on_gpsimd(1)
+        for late in range(2, E):
+            cast_w2(late, nc.scalar.copy)
+        for half in range(2):
+            hide(e, half)
         quantise_h(e, 0)
-        quantise_w2(EARLY_W2, EARLY_W2 + 1)
+        quantise_w2(0)
         quantise_h(e, 1)
-        for late in range(EARLY_W2 + 1, E):
-            quantise_w2(late, late + 1)
+        for late in range(1, E):
+            quantise_w2(late)
         finish_experts(0, 2, nc.scalar.copy)
         finish_experts(2, 4, nc.vector.tensor_copy)
         finish_experts(4, 5, nc.scalar.copy)
-        finish_last()
+        finish_last_expert()
 
-        first = keep.tile([P, T], F32, name="first")
-        nc.vector.tensor_tensor(first[:], y_all[:].indirect(pos1_t[:]), gate_t[:, 0, :], MULT)
-        second = {}
-
-        def fetch(a, b):
-            prod = work.tile([P, b - a], F32, name="second", bufs=3)
-            nc.vector.tensor_tensor(prod[:], y_all[:].indirect(pos2_t[:, a // 16 : b // 16]), gate_t[:, 1, a:b], MULT)
-            second[a] = prod
-
-        def finish(a, b):
-            o = work.tile([P, b - a], F32, name="o", align_bytes=256, bufs=3)
-            nc.vector.tensor_tensor(o[:], first[:, a:b], second[a][:], ADD)
+        first_products = keep.tile([P, T], F32, name="first_products")
+        nc.vector.tensor_tensor(first_products[:], y_all[:].indirect(pos1_t[:]), gate_t[:, 0, :], MULT)
+        second_products = []
+        for a, b in OUT_PIECES:
+            prod = work.tile([P, b - a], F32, name="second_products")
+            nc.vector.tensor_tensor(prod[:], y_all[:].indirect(list_columns(pos2_t, a, b)), gate_t[:, 1, a:b], MULT)
+            second_products.append(prod)
+        for (a, b), prod in zip(OUT_PIECES, second_products):
+            o = work.tile([P, b - a], F32, name="o", align_bytes=256)
+            nc.vector.tensor_tensor(o[:], first_products[:, a:b], prod[:], ADD)
             nc.sync.dma_start(out=out[:, a:b], in_=o[:])
-
-        fetch(*PIECES[0])
-        for done, ahead in zip(PIECES, PIECES[1:]):
-            fetch(*ahead)
-            finish(*done)
-        finish(*PIECES[-1])

@@ -22,19 +22,20 @@ RELU = mybir.ActivationFunctionType.Relu
 
 LIST_ROWS = 16
 SLICE = 512
-HALF = 128
+HALF = C // 2
 RUN = 4
 X_CALLS = ((0, 512), (512, T))
 SCALE_ROW = (0, 4)
 
-RING = 5
 AHEAD = 3
+RING = 5
 WHOLE = 8
 LAST = (1, E - 1, PASSES - 1)
 
 X_SHARE = (128, 40)
-WHOLE_SHARES = (P, 0)
-PASS_SHARES = ((40, 88), (56, 40))
+WHOLE_SHARES = ((P, 24), (112, 0))
+PASS_SHARES = ((40, 96), (80, 40))
+LAST_SHARES = ((P // 2, 88), (56,))
 LAST_PIECES = ((0, 72, P // 2), (72, P, 0))
 OUT_PIECES = ((0, T // 2), (T // 2, T))
 
@@ -189,14 +190,14 @@ def tile_routed_moe_kernel(tc, xT, w1, w3, w2, gate, offs, pos1, pos2, out):
                 )
 
         def by_slot(acc):
-            return acc[:].rearrange("p t (k n) -> p k n t", k=PACK)
+            return acc[:].rearrange("p t (g j) -> p g j t", g=PACK)
 
         def rectify(e, half):
             if e < E - 1:
                 rows = staged(1, e)[:, 0 if whole(1, e) else 1]
             else:
                 rows = last_piece(*LAST_PIECES[0][:2])
-            r = rows[:, :, half * HALF : (half + 1) * HALF].rearrange("p k (n t) -> p k n t", t=PACK)
+            r = rows[:, :, half * HALF : (half + 1) * HALF].rearrange("p g (j t) -> p g j t", t=PACK)
             nc.scalar.activation(r, by_slot(sums[(0, e, half)]), RELU)
             relus[(e, half)] = r
 
@@ -207,7 +208,7 @@ def tile_routed_moe_kernel(tc, xT, w1, w3, w2, gate, offs, pos1, pos2, out):
                 h_tile = work.tile([P, HALF * PACK], BF16, name="h", align_bytes=64)
                 h = h_tile[:]
             nc.vector.tensor_tensor(
-                h.rearrange("p (k n t) -> p k n t", k=PACK, t=PACK), by_slot(sums[(1, e, half)]), relus[(e, half)], MULT
+                h.rearrange("p (g j t) -> p g j t", g=PACK, t=PACK), by_slot(sums[(1, e, half)]), relus[(e, half)], MULT
             )
             hidden[(e, half)] = h
 
@@ -234,8 +235,8 @@ def tile_routed_moe_kernel(tc, xT, w1, w3, w2, gate, offs, pos1, pos2, out):
             acc = psum_y.tile([P, (b - a) * C], F32, name="acc_y")
             for e in range(a, b):
                 for half in range(2):
-                    c = (e - a) * C + half * HALF
-                    project_back(e, half, acc[:, c : c + HALF])
+                    col = (e - a) * C + half * HALF
+                    project_back(e, half, acc[:, col : col + HALF])
             copy(y_all[:, a * C : b * C], acc[:])
 
         def finish_last_expert():
@@ -243,8 +244,8 @@ def tile_routed_moe_kernel(tc, xT, w1, w3, w2, gate, offs, pos1, pos2, out):
             for half, copy in enumerate((nc.vector.tensor_copy, nc.scalar.copy)):
                 acc = sums[(0, e, half)][:, 0, :]
                 project_back(e, half, acc)
-                c = e * C + half * HALF
-                copy(y_all[:, c : c + HALF], acc)
+                col = e * C + half * HALF
+                copy(y_all[:, col : col + HALF], acc)
 
         nc.gpsimd.memset(x_bytes[:], 0)
         for s in range(PASSES):
@@ -279,7 +280,7 @@ def tile_routed_moe_kernel(tc, xT, w1, w3, w2, gate, offs, pos1, pos2, out):
             if i == 0:
                 shares = (P, P)
             else:
-                shares = WHOLE_SHARES if whole(w, e) else PASS_SHARES[w]
+                shares = (WHOLE_SHARES if whole(w, e) else PASS_SHARES if e < E - 1 else LAST_SHARES)[w]
             first, second = (1, 0) if whole(w, e) else (0, 1)
             before = e - 1 if w == 0 and e > 0 else None
             cast_w(w, e, first, shares[first])
@@ -313,17 +314,18 @@ def tile_routed_moe_kernel(tc, xT, w1, w3, w2, gate, offs, pos1, pos2, out):
                     gather_bytes(q)
 
         w, e, s = LAST
-        cast_w(w, e, 0, PASS_SHARES[w][0])
+        cast_w(w, e, 0, LAST_SHARES[w][0])
         dst = cast_tile(*LAST)
         code_tiles(*LAST)
-        (a, b, scalar_m), (c, d, no_scalar) = LAST_PIECES
+        a, b, scalar_m = LAST_PIECES[0]
         share_cast(last_piece(a, b), dst[:, a:b], scalar_m)
         for half in range(2):
             rectify(e, half)
         quantise_w(w, e, 0)
         for half in range(2):
             project(w, e, half, 0, True)
-        share_cast(last_piece(c, d), dst[:, c:d], no_scalar)
+        a, b, scalar_m = LAST_PIECES[1]
+        share_cast(last_piece(a, b), dst[:, a:b], scalar_m)
         for t in range(PACK):
             quantise_columns(w, e, s, t * P, (t + 1) * P)
         for half in range(2):

@@ -37,6 +37,11 @@ WHOLE_SHARES = ((P, 24), (112, 0))
 PASS_SHARES = ((40, 96), (80, 40))
 LAST_SHARES = ((P // 2, 88), (56,))
 LAST_PIECES = ((0, 72, P // 2), (72, P, 0))
+W2_LOADS = ((0, 1), (1, 3), (3, 4), (4, 5))
+PAIRS = ((1, 5, 0), (1, 4, 1))
+CUT = (1, 0)
+FIFTH = ((128, 24), (88, 0))
+SECOND_SHARES = (128, 96)
 OUT_PIECES = ((0, T // 2), (T // 2, T))
 
 
@@ -49,6 +54,7 @@ def tile_routed_moe_kernel(tc, xT, w1, w3, w2, gate, offs, pos1, pos2, out):
         psum = ctx.enter_context(tc.psum_pool(name="psum", bufs=2))
         psum_y = ctx.enter_context(tc.psum_pool(name="psum_y", bufs=4))
 
+        w2_loads = []
         offs_t = keep.tile([P, SLOTS // LIST_ROWS], U16, name="offs_t")
         pos1_t = keep.tile([P, T // LIST_ROWS], U16, name="pos1_t")
         pos2_t = keep.tile([P, T // LIST_ROWS], U16, name="pos2_t")
@@ -59,9 +65,14 @@ def tile_routed_moe_kernel(tc, xT, w1, w3, w2, gate, offs, pos1, pos2, out):
         y_all = keep.tile([P, SLOTS], F32, name="y_all", align_bytes=256)
         gate_t = keep.tile([P, 2, T], F32, name="gate_t", align_bytes=256)
         ring = [keep.tile([P, PASSES, PACK, H], F32, name=f"ring{r}", align_bytes=256) for r in range(RING)]
-        w2_raw = keep.tile([P, E - 1, PACK, N], F32, name="w2_raw", align_bytes=256)
+        w2_raw = {}
+        for a, b in W2_LOADS:
+            rows = keep.tile([P, b - a, PACK, N], F32, name=f"w2_raw{a}", align_bytes=256)
+            w2_raw.update({e: rows[:, e - a] for e in range(a, b)})
+            w2_loads.append((rows, a, b))
         w2_last = y_all[:, 3 * HALF : 11 * HALF].rearrange("p (r c) -> p r c", r=2)[:, :, 0:C]
         w2_last = w2_last.rearrange("p r (u n) -> p r u n", u=2)
+        h_last = keep.tile([P, C * PACK], BF16, name="h_last", align_bytes=64)
         slot_words = {}
         slot_bytes = {}
         cast = {}
@@ -96,28 +107,36 @@ def tile_routed_moe_kernel(tc, xT, w1, w3, w2, gate, offs, pos1, pos2, out):
                             nc.sync.dma_start(out=last_piece(a, b), in_=src[:, s, :, a * PACK : b * PACK])
 
         def load_tail():
-            for e in range(E - 1):
-                src = w2[e : e + 1].rearrange("e (p t) n -> p e t n", t=PACK)
-                nc.sync.dma_start(out=w2_raw[:, e : e + 1], in_=src)
+            for rows, a, b in w2_loads:
+                nc.sync.dma_start(out=rows[:], in_=w2[a:b].rearrange("e (p t) n -> p e t n", t=PACK))
             nc.sync.dma_start(out=w2_last, in_=w2[E - 1].rearrange("(p r u) n -> p r u n", r=2, u=2))
             for which, (pos_t, pos) in enumerate(((pos1_t, pos1), (pos2_t, pos2))):
                 nc.sync.dma_start(pos_t[:], pos)
                 nc.sync.dma_start(out=gate_t[:, which, :], in_=gate[which])
 
-        def share_cast(raw, to, scalar_m):
+        def share_cast(raw, to, scalar_m, cut=0, pairs=False):
             src = raw.rearrange("p k (m t) -> p m k t", t=PACK)
-            if scalar_m > 0:
-                nc.scalar.copy(to[:, 0:scalar_m], src[:, 0:scalar_m])
-            if scalar_m < to.shape[1]:
-                nc.vector.tensor_copy(to[:, scalar_m:], src[:, scalar_m:])
+            width = to.shape[1]
+            for a, b in ((0, cut), (cut, scalar_m)) if 0 < cut < scalar_m else ((0, scalar_m),):
+                if b > a:
+                    nc.scalar.copy(to[:, a:b], src[:, a:b])
+            for a, b in ((cut, width), (scalar_m, cut)) if cut > scalar_m else ((scalar_m, width),):
+                for t0, t1 in ((0, 2), (2, PACK)) if pairs else ((0, PACK),):
+                    if b > a:
+                        nc.vector.tensor_copy(to[:, a:b, :, t0:t1], src[:, a:b, :, t0:t1])
 
         def cast_tile(w, e, s):
             w_bf = work.tile([P, H * PACK], BF16, name="w_bf", align_bytes=64, bufs=4)
             cast[(w, e, s)] = w_bf
             return w_bf[:].rearrange("p (t m k) -> p m k t", t=PACK, k=PACK)
 
+        def in_pairs(w, e, s):
+            return not whole(w, e) and (w, e, s) in PAIRS
+
         def cast_w(w, e, s, scalar_m):
-            share_cast(staged(w, e)[:, s], cast_tile(w, e, s), scalar_m)
+            held = (1 if whole(w, e) else 0) if w == 0 else (0 if whole(w, e) else 1)
+            cut = P // 2 if s == held and (w, e) != (0, 0) and CUT[w] else 0
+            share_cast(staged(w, e)[:, s], cast_tile(w, e, s), scalar_m, cut, in_pairs(w, e, s))
 
         def code_tiles(w, e, s):
             words = quant.tile([P, H], U32, name="w_words", align_bytes=64)
@@ -132,10 +151,11 @@ def tile_routed_moe_kernel(tc, xT, w1, w3, w2, gate, offs, pos1, pos2, out):
 
         def quantise_w(w, e, s):
             code_tiles(w, e, s)
-            quantise_columns(w, e, s, 0, H)
+            for a, b in ((0, H // 2), (H // 2, H)) if in_pairs(w, e, s) else ((0, H),):
+                quantise_columns(w, e, s, a, b)
 
         def w2_views(e, to, order):
-            raw = w2_raw[:, e].rearrange("p (r u) n -> p r u n", r=2) if e < E - 1 else w2_last
+            raw = w2_raw[e].rearrange("p (r u) n -> p r u n", r=2) if e < E - 1 else w2_last
             w2_cast[e] = to
             return (
                 to.rearrange("p (c j r u) -> p " + order, j=RUN, r=2, u=2),
@@ -205,18 +225,25 @@ def tile_routed_moe_kernel(tc, xT, w1, w3, w2, gate, offs, pos1, pos2, out):
             if e < E - 1:
                 h = staged(0, e + 1)[:, 1 if whole(0, e + 1) else 0, half, H // 2 : H].bitcast(BF16)
             else:
-                h_tile = work.tile([P, HALF * PACK], BF16, name="h", align_bytes=64)
-                h = h_tile[:]
+                h = h_last[:, half * K_PASS : (half + 1) * K_PASS]
             nc.vector.tensor_tensor(
                 h.rearrange("p (g j t) -> p g j t", g=PACK, t=PACK), by_slot(sums[(1, e, half)]), relus[(e, half)], MULT
             )
             hidden[(e, half)] = h
 
         def quantise_h(e, half):
-            words = work.tile([P, HALF], U32, name="h_words", align_bytes=64, bufs=2 * E)
-            scales = work.tile([P, HALF], U8, name="h_scales", align_bytes=64, bufs=2 * E)
+            words = work.tile([P, HALF], U32, name="h_words", align_bytes=64, bufs=2 * (E - 1))
+            scales = work.tile([P, HALF], U8, name="h_scales", align_bytes=64, bufs=2 * (E - 1))
             nc.vector.quantize_mx(out=words[:].bitcast(FP8X4), scales=scales[:], in_=hidden[(e, half)])
-            hidden_q[(e, half)] = (words, scales)
+            hidden_q[(e, half)] = (words[:], scales[:])
+
+        def quantise_last_h():
+            words = keep.tile([P, C], U32, name=f"w2_raw{E - 3}", align_bytes=256)
+            scales = keep.tile([P, C], U8, name="last_h_scales", align_bytes=64)
+            nc.vector.quantize_mx(out=words[:].bitcast(FP8X4), scales=scales[:], in_=h_last[:])
+            for half in range(2):
+                cols = slice(half * HALF, (half + 1) * HALF)
+                hidden_q[(E - 1, half)] = (words[:, cols], scales[:, cols])
 
         def project_back(e, half, acc):
             w_words, w_scales = w2_quantised[e]
@@ -225,8 +252,8 @@ def tile_routed_moe_kernel(tc, xT, w1, w3, w2, gate, offs, pos1, pos2, out):
                 out=acc,
                 lhsT=w_words.bitcast(FP8X4),
                 lhsT_scale=w_scales,
-                rhs=h_words[:].bitcast(FP8X4),
-                rhs_scale=h_scales[:],
+                rhs=h_words.bitcast(FP8X4),
+                rhs_scale=h_scales,
                 start=True,
                 stop=True,
             )
@@ -279,8 +306,10 @@ def tile_routed_moe_kernel(tc, xT, w1, w3, w2, gate, offs, pos1, pos2, out):
                 load_tail()
             if i == 0:
                 shares = (P, P)
+            elif i == 1:
+                shares = SECOND_SHARES
             else:
-                shares = (WHOLE_SHARES if whole(w, e) else PASS_SHARES if e < E - 1 else LAST_SHARES)[w]
+                shares = (FIFTH if e == 4 and whole(w, e) else WHOLE_SHARES if whole(w, e) else PASS_SHARES if e < E - 1 else LAST_SHARES)[w]
             first, second = (1, 0) if whole(w, e) else (0, 1)
             before = e - 1 if w == 0 and e > 0 else None
             cast_w(w, e, first, shares[first])
@@ -325,7 +354,7 @@ def tile_routed_moe_kernel(tc, xT, w1, w3, w2, gate, offs, pos1, pos2, out):
         for half in range(2):
             project(w, e, half, 0, True)
         a, b, scalar_m = LAST_PIECES[1]
-        share_cast(last_piece(a, b), dst[:, a:b], scalar_m)
+        share_cast(last_piece(a, b), dst[:, a:b], scalar_m, 0, True)
         for t in range(PACK):
             quantise_columns(w, e, s, t * P, (t + 1) * P)
         for half in range(2):
@@ -337,10 +366,10 @@ def tile_routed_moe_kernel(tc, xT, w1, w3, w2, gate, offs, pos1, pos2, out):
             cast_w2(late, nc.scalar.copy)
         for half in range(2):
             hide(e, half)
-        quantise_h(e, 0)
-        quantise_w2(0)
-        quantise_h(e, 1)
-        for late in range(1, E):
+        for late in range(E - 2):
+            quantise_w2(late)
+        quantise_last_h()
+        for late in range(E - 2, E):
             quantise_w2(late)
         finish_experts(0, 2, nc.scalar.copy)
         finish_experts(2, 4, nc.vector.tensor_copy)

@@ -35,8 +35,7 @@ LAST = (1, E - 1, PASSES - 1)
 X_SHARE = (128, 40)
 WHOLE_SHARES = ((P, 24), (112, 0))
 PASS_SHARES = ((40, 96), (80, 40))
-LAST_SHARES = ((P // 2, 88), (56,))
-LAST_PIECES = ((0, 72, P // 2), (72, P, 0))
+LAST_SHARES = ((P // 2, 80), (48, 28))
 W2_LOADS = ((0, 1), (1, 3), (3, 4), (4, 5))
 PAIRS = ((1, 5, 0), (1, 4, 1))
 CUT = (1, 0)
@@ -90,21 +89,13 @@ def tile_routed_moe_kernel(tc, xT, w1, w3, w2, gate, offs, pos1, pos2, out):
         def whole(w, e):
             return 2 * e + w < WHOLE
 
-        def last_piece(a, b):
-            rows = staged(*LAST[:2])[:, LAST[2]].rearrange("p k c -> p (k c)")
-            return rows[:, a * PACK * PACK : b * PACK * PACK].rearrange("p (k c) -> p k c", k=PACK)
-
         def load(w, e):
             src = (w1, w3)[w][e].rearrange("(s p t) c -> p s t c", s=PASSES, t=PACK)
             if whole(w, e):
                 nc.sync.dma_start(out=staged(w, e)[:], in_=src)
             else:
                 for s in range(PASSES):
-                    if (w, e, s) != LAST:
-                        nc.sync.dma_start(out=staged(w, e)[:, s], in_=src[:, s])
-                    else:
-                        for a, b, scalar_m in LAST_PIECES:
-                            nc.sync.dma_start(out=last_piece(a, b), in_=src[:, s, :, a * PACK : b * PACK])
+                    nc.sync.dma_start(out=staged(w, e)[:, s], in_=src[:, s])
 
         def load_tail():
             for rows, a, b in w2_loads:
@@ -213,10 +204,7 @@ def tile_routed_moe_kernel(tc, xT, w1, w3, w2, gate, offs, pos1, pos2, out):
             return acc[:].rearrange("p t (g j) -> p g j t", g=PACK)
 
         def rectify(e, half):
-            if e < E - 1:
-                rows = staged(1, e)[:, 0 if whole(1, e) else 1]
-            else:
-                rows = last_piece(*LAST_PIECES[0][:2])
+            rows = staged(1, e)[:, 0 if whole(1, e) or e == E - 1 else 1]
             r = rows[:, :, half * HALF : (half + 1) * HALF].rearrange("p g (j t) -> p g j t", t=PACK)
             nc.scalar.activation(r, by_slot(sums[(0, e, half)]), RELU)
             relus[(e, half)] = r
@@ -344,17 +332,13 @@ def tile_routed_moe_kernel(tc, xT, w1, w3, w2, gate, offs, pos1, pos2, out):
 
         w, e, s = LAST
         cast_w(w, e, 0, LAST_SHARES[w][0])
-        dst = cast_tile(*LAST)
-        code_tiles(*LAST)
-        a, b, scalar_m = LAST_PIECES[0]
-        share_cast(last_piece(a, b), dst[:, a:b], scalar_m)
         for half in range(2):
             rectify(e, half)
         quantise_w(w, e, 0)
         for half in range(2):
             project(w, e, half, 0, True)
-        a, b, scalar_m = LAST_PIECES[1]
-        share_cast(last_piece(a, b), dst[:, a:b], scalar_m, 0, True)
+        share_cast(staged(w, e)[:, s], cast_tile(*LAST), LAST_SHARES[w][s], 0, True)
+        code_tiles(*LAST)
         for t in range(PACK):
             quantise_columns(w, e, s, t * P, (t + 1) * P)
         for half in range(2):

@@ -35,12 +35,16 @@ LAST = (1, E - 1, PASSES - 1)
 X_SHARE = (128, 40)
 WHOLE_SHARES = ((P, 24), (112, 0))
 PASS_SHARES = ((40, 96), (80, 40))
-LAST_SHARES = ((P // 2, 80), (48, 28))
-W2_LOADS = ((0, 1), (1, 3), (3, 4), (4, 5))
-PAIRS = ((1, 5, 0), (1, 4, 1))
+LAST_SHARES = ((P // 2, 88), (40, 36))
+W2_LOADS = ((0, 1), (1, 2), (2, 3), (3, 4), (4, 5), (5, 6))
+PAIRS = ()
 CUT = (1, 0)
 FIFTH = ((128, 24), (88, 0))
 SECOND_SHARES = (128, 96)
+FPAIR = 0
+PIN = 4
+GAP = 2
+ON_G = 3
 OUT_PIECES = ((0, T // 2), (T // 2, T))
 
 
@@ -61,7 +65,6 @@ def tile_routed_moe_kernel(tc, xT, w1, w3, w2, gate, offs, pos1, pos2, out):
         x_bf = [keep.tile([P, T * PACK], BF16, name=f"x_bf{s}", align_bytes=64) for s in range(PASSES)]
         x_words = [keep.tile([P, T], U32, name=f"x_words{s}", align_bytes=64) for s in range(PASSES)]
         x_bytes = keep.tile([P, T], U8, name="x_bytes", align_bytes=64)
-        y_all = keep.tile([P, SLOTS], F32, name="y_all", align_bytes=256)
         gate_t = keep.tile([P, 2, T], F32, name="gate_t", align_bytes=256)
         ring = [keep.tile([P, PASSES, PACK, H], F32, name=f"ring{r}", align_bytes=256) for r in range(RING)]
         w2_raw = {}
@@ -69,9 +72,7 @@ def tile_routed_moe_kernel(tc, xT, w1, w3, w2, gate, offs, pos1, pos2, out):
             rows = keep.tile([P, b - a, PACK, N], F32, name=f"w2_raw{a}", align_bytes=256)
             w2_raw.update({e: rows[:, e - a] for e in range(a, b)})
             w2_loads.append((rows, a, b))
-        w2_last = y_all[:, 3 * HALF : 11 * HALF].rearrange("p (r c) -> p r c", r=2)[:, :, 0:C]
-        w2_last = w2_last.rearrange("p r (u n) -> p r u n", u=2)
-        h_last = keep.tile([P, C * PACK], BF16, name="h_last", align_bytes=64)
+        last_h = []
         slot_words = {}
         slot_bytes = {}
         cast = {}
@@ -100,7 +101,6 @@ def tile_routed_moe_kernel(tc, xT, w1, w3, w2, gate, offs, pos1, pos2, out):
         def load_tail():
             for rows, a, b in w2_loads:
                 nc.sync.dma_start(out=rows[:], in_=w2[a:b].rearrange("e (p t) n -> p e t n", t=PACK))
-            nc.sync.dma_start(out=w2_last, in_=w2[E - 1].rearrange("(p r u) n -> p r u n", r=2, u=2))
             for which, (pos_t, pos) in enumerate(((pos1_t, pos1), (pos2_t, pos2))):
                 nc.sync.dma_start(pos_t[:], pos)
                 nc.sync.dma_start(out=gate_t[:, which, :], in_=gate[which])
@@ -146,7 +146,7 @@ def tile_routed_moe_kernel(tc, xT, w1, w3, w2, gate, offs, pos1, pos2, out):
                 quantise_columns(w, e, s, a, b)
 
         def w2_views(e, to, order):
-            raw = w2_raw[e].rearrange("p (r u) n -> p r u n", r=2) if e < E - 1 else w2_last
+            raw = w2_raw[e].rearrange("p (r u) n -> p r u n", r=2)
             w2_cast[e] = to
             return (
                 to.rearrange("p (c j r u) -> p " + order, j=RUN, r=2, u=2),
@@ -158,7 +158,7 @@ def tile_routed_moe_kernel(tc, xT, w1, w3, w2, gate, offs, pos1, pos2, out):
             copy(*w2_views(e, w_bf[:], "c r u j"))
 
         def cast_w2_on_gpsimd(e):
-            to, src = w2_views(e, cast[LAST][:, (PACK - 1) * K_PASS :], "c j r u")
+            to, src = w2_views(e, w2_cast[GAP - 1], "c j r u")
             nc.gpsimd.tensor_scalar(to, src, 1.0, 0.0, MULT, ADD)
 
         def quantise_w2(e):
@@ -213,7 +213,9 @@ def tile_routed_moe_kernel(tc, xT, w1, w3, w2, gate, offs, pos1, pos2, out):
             if e < E - 1:
                 h = staged(0, e + 1)[:, 1 if whole(0, e + 1) else 0, half, H // 2 : H].bitcast(BF16)
             else:
-                h = h_last[:, half * K_PASS : (half + 1) * K_PASS]
+                if half == 0:
+                    last_h.append(keep.tile([P, C * PACK], BF16, name=f"w2_raw{GAP - 1}", align_bytes=256))
+                h = last_h[0][:, half * K_PASS : (half + 1) * K_PASS]
             nc.vector.tensor_tensor(
                 h.rearrange("p (g j t) -> p g j t", g=PACK, t=PACK), by_slot(sums[(1, e, half)]), relus[(e, half)], MULT
             )
@@ -226,9 +228,9 @@ def tile_routed_moe_kernel(tc, xT, w1, w3, w2, gate, offs, pos1, pos2, out):
             hidden_q[(e, half)] = (words[:], scales[:])
 
         def quantise_last_h():
-            words = keep.tile([P, C], U32, name=f"w2_raw{E - 3}", align_bytes=256)
+            words = keep.tile([P, C], U32, name=f"w2_raw{PIN}", align_bytes=256)
             scales = keep.tile([P, C], U8, name="last_h_scales", align_bytes=64)
-            nc.vector.quantize_mx(out=words[:].bitcast(FP8X4), scales=scales[:], in_=h_last[:])
+            nc.vector.quantize_mx(out=words[:].bitcast(FP8X4), scales=scales[:], in_=last_h[0][:])
             for half in range(2):
                 cols = slice(half * HALF, (half + 1) * HALF)
                 hidden_q[(E - 1, half)] = (words[:, cols], scales[:, cols])
@@ -337,23 +339,28 @@ def tile_routed_moe_kernel(tc, xT, w1, w3, w2, gate, offs, pos1, pos2, out):
         quantise_w(w, e, 0)
         for half in range(2):
             project(w, e, half, 0, True)
-        share_cast(staged(w, e)[:, s], cast_tile(*LAST), LAST_SHARES[w][s], 0, True)
+        share_cast(staged(w, e)[:, s], cast_tile(*LAST), LAST_SHARES[w][s], 0, FPAIR)
         code_tiles(*LAST)
         for t in range(PACK):
             quantise_columns(w, e, s, t * P, (t + 1) * P)
         for half in range(2):
             project(w, e, half, s, False)
 
-        cast_w2(0, nc.vector.tensor_copy)
-        cast_w2_on_gpsimd(1)
-        for late in range(2, E):
+        for late in range(GAP):
             cast_w2(late, nc.scalar.copy)
+            quantise_w2(late)
+        for late in range(GAP, E):
+            if late == ON_G:
+                cast_w2_on_gpsimd(late)
+            else:
+                cast_w2(late, nc.scalar.copy)
+        y_all = keep.tile([P, SLOTS], F32, name=f"w2_raw{E - 1}", align_bytes=256)
         for half in range(2):
             hide(e, half)
-        for late in range(E - 2):
+        for late in range(GAP, PIN + 1):
             quantise_w2(late)
         quantise_last_h()
-        for late in range(E - 2, E):
+        for late in range(PIN + 1, E):
             quantise_w2(late)
         finish_experts(0, 2, nc.scalar.copy)
         finish_experts(2, 4, nc.vector.tensor_copy)

@@ -35,15 +35,16 @@ LAST = (1, E - 1, PASSES - 1)
 X_SHARE = (128, 40)
 WHOLE_SHARES = ((P, 24), (112, 0))
 PASS_SHARES = ((40, 96), (80, 40))
-LAST_SHARES = ((P // 2, 88), (40, 36))
-W2_LOADS = ((0, 1), (1, 2), (2, 3), (3, 4), (4, 5), (5, 6))
-PAIRS = ()
+LAST_SHARES = ((P // 2, 80), (48,))
+W2_LOADS = ((0, 1), (1, 2), (2, 3), (3, 4), (4, 5))
+PAIRS = ((1, 5, 0), (0, 5, 1), (1, 4, 1))
 CUT = (1, 0)
 FIFTH = ((128, 24), (88, 0))
 SECOND_SHARES = (128, 96)
-FPAIR = 0
+LAST_PIECES = ((0, 72, 28), (72, 128, 0))
 PIN = 4
 GAP = 2
+DCUT = 32
 ON_G = 3
 OUT_PIECES = ((0, T // 2), (T // 2, T))
 
@@ -67,6 +68,9 @@ def tile_routed_moe_kernel(tc, xT, w1, w3, w2, gate, offs, pos1, pos2, out):
         x_bytes = keep.tile([P, T], U8, name="x_bytes", align_bytes=64)
         gate_t = keep.tile([P, 2, T], F32, name="gate_t", align_bytes=256)
         ring = [keep.tile([P, PASSES, PACK, H], F32, name=f"ring{r}", align_bytes=256) for r in range(RING)]
+        y_all = keep.tile([P, SLOTS], F32, name="y_all", align_bytes=256)
+        w2_last = y_all[:, 2 * C - N // 2 : 6 * C - N // 2].rearrange("p (r c) -> p r c", r=2)[:, :, 0:C]
+        w2_last = w2_last.rearrange("p r (u n) -> p r u n", u=2)
         w2_raw = {}
         for a, b in W2_LOADS:
             rows = keep.tile([P, b - a, PACK, N], F32, name=f"w2_raw{a}", align_bytes=256)
@@ -90,17 +94,26 @@ def tile_routed_moe_kernel(tc, xT, w1, w3, w2, gate, offs, pos1, pos2, out):
         def whole(w, e):
             return 2 * e + w < WHOLE
 
+        def last_piece(a, b):
+            rows = staged(*LAST[:2])[:, LAST[2]].rearrange("p k c -> p (k c)")
+            return rows[:, a * PACK * PACK : b * PACK * PACK].rearrange("p (k c) -> p k c", k=PACK)
+
         def load(w, e):
             src = (w1, w3)[w][e].rearrange("(s p t) c -> p s t c", s=PASSES, t=PACK)
             if whole(w, e):
                 nc.sync.dma_start(out=staged(w, e)[:], in_=src)
             else:
                 for s in range(PASSES):
-                    nc.sync.dma_start(out=staged(w, e)[:, s], in_=src[:, s])
+                    if (w, e, s) != LAST:
+                        nc.sync.dma_start(out=staged(w, e)[:, s], in_=src[:, s])
+                    else:
+                        for a, b, scalar_m in LAST_PIECES:
+                            nc.sync.dma_start(out=last_piece(a, b), in_=src[:, s, :, a * PACK : b * PACK])
 
         def load_tail():
             for rows, a, b in w2_loads:
                 nc.sync.dma_start(out=rows[:], in_=w2[a:b].rearrange("e (p t) n -> p e t n", t=PACK))
+            nc.sync.dma_start(out=w2_last, in_=w2[E - 1].rearrange("(p r u) n -> p r u n", r=2, u=2))
             for which, (pos_t, pos) in enumerate(((pos1_t, pos1), (pos2_t, pos2))):
                 nc.sync.dma_start(pos_t[:], pos)
                 nc.sync.dma_start(out=gate_t[:, which, :], in_=gate[which])
@@ -146,7 +159,7 @@ def tile_routed_moe_kernel(tc, xT, w1, w3, w2, gate, offs, pos1, pos2, out):
                 quantise_columns(w, e, s, a, b)
 
         def w2_views(e, to, order):
-            raw = w2_raw[e].rearrange("p (r u) n -> p r u n", r=2)
+            raw = w2_raw[e].rearrange("p (r u) n -> p r u n", r=2) if e < E - 1 else w2_last
             w2_cast[e] = to
             return (
                 to.rearrange("p (c j r u) -> p " + order, j=RUN, r=2, u=2),
@@ -155,7 +168,10 @@ def tile_routed_moe_kernel(tc, xT, w1, w3, w2, gate, offs, pos1, pos2, out):
 
         def cast_w2(e, copy):
             w_bf = keep.tile([P, N * PACK], BF16, name=f"w2_bf{e}", align_bytes=64)
-            copy(*w2_views(e, w_bf[:], "c r u j"))
+            to, src = w2_views(e, w_bf[:], "c r u j")
+            groups = N // RUN
+            for a, b in ((0, groups),) if e < E - 1 else ((0, groups // 2), (groups // 2, groups)):
+                copy(to[:, a:b], src[:, a:b])
 
         def cast_w2_on_gpsimd(e):
             to, src = w2_views(e, w2_cast[GAP - 1], "c j r u")
@@ -333,13 +349,15 @@ def tile_routed_moe_kernel(tc, xT, w1, w3, w2, gate, offs, pos1, pos2, out):
                     gather_bytes(q)
 
         w, e, s = LAST
-        cast_w(w, e, 0, LAST_SHARES[w][0])
+        share_cast(staged(w, e)[:, 0], cast_tile(w, e, 0), LAST_SHARES[w][0], DCUT, in_pairs(w, e, 0))
         for half in range(2):
             rectify(e, half)
         quantise_w(w, e, 0)
         for half in range(2):
             project(w, e, half, 0, True)
-        share_cast(staged(w, e)[:, s], cast_tile(*LAST), LAST_SHARES[w][s], 0, FPAIR)
+        dst = cast_tile(*LAST)
+        for a, b, scalar_m in LAST_PIECES:
+            share_cast(last_piece(a, b), dst[:, a:b], scalar_m, 0, b == P)
         code_tiles(*LAST)
         for t in range(PACK):
             quantise_columns(w, e, s, t * P, (t + 1) * P)
@@ -354,7 +372,6 @@ def tile_routed_moe_kernel(tc, xT, w1, w3, w2, gate, offs, pos1, pos2, out):
                 cast_w2_on_gpsimd(late)
             else:
                 cast_w2(late, nc.scalar.copy)
-        y_all = keep.tile([P, SLOTS], F32, name=f"w2_raw{E - 1}", align_bytes=256)
         for half in range(2):
             hide(e, half)
         for late in range(GAP, PIN + 1):

@@ -30,22 +30,16 @@ SCALE_ROW = (0, 4)
 AHEAD = 3
 RING = 5
 WHOLE = 8
-LAST = (1, E - 1, PASSES - 1)
+LAST = E - 1
 
 X_SHARE = (128, 40)
+FIRST_SHARES = ((P, P), (P, 96))
 WHOLE_SHARES = ((P, 24), (112, 0))
 PASS_SHARES = ((40, 96), (80, 40))
-LAST_SHARES = ((P // 2, 80), (48,))
-W2_LOADS = ((0, 1), (1, 2), (2, 3), (3, 4), (4, 5))
-PAIRS = ((1, 5, 0), (0, 5, 1), (1, 4, 1))
-CUT = (1, 0)
-FIFTH = ((128, 24), (88, 0))
-SECOND_SHARES = (128, 96)
-LAST_PIECES = ((0, 72, 28), (72, 128, 0))
-PIN = 4
-GAP = 2
-DCUT = 32
-ON_G = 3
+LAST_W1_SHARES = (P // 2, 80)
+TILE_PAIRS = ((0, 2), (2, PACK))
+EARLY_W2 = 2
+GPSIMD_W2 = 3
 OUT_PIECES = ((0, T // 2), (T // 2, T))
 
 
@@ -58,7 +52,6 @@ def tile_routed_moe_kernel(tc, xT, w1, w3, w2, gate, offs, pos1, pos2, out):
         psum = ctx.enter_context(tc.psum_pool(name="psum", bufs=2))
         psum_y = ctx.enter_context(tc.psum_pool(name="psum_y", bufs=4))
 
-        w2_loads = []
         offs_t = keep.tile([P, SLOTS // LIST_ROWS], U16, name="offs_t")
         pos1_t = keep.tile([P, T // LIST_ROWS], U16, name="pos1_t")
         pos2_t = keep.tile([P, T // LIST_ROWS], U16, name="pos2_t")
@@ -69,14 +62,9 @@ def tile_routed_moe_kernel(tc, xT, w1, w3, w2, gate, offs, pos1, pos2, out):
         gate_t = keep.tile([P, 2, T], F32, name="gate_t", align_bytes=256)
         ring = [keep.tile([P, PASSES, PACK, H], F32, name=f"ring{r}", align_bytes=256) for r in range(RING)]
         y_all = keep.tile([P, SLOTS], F32, name="y_all", align_bytes=256)
+        w2_raw = [keep.tile([P, 2, 2, N], F32, name=f"w2_raw{e}", align_bytes=256)[:] for e in range(LAST)]
         w2_last = y_all[:, 2 * C - N // 2 : 6 * C - N // 2].rearrange("p (r c) -> p r c", r=2)[:, :, 0:C]
-        w2_last = w2_last.rearrange("p r (u n) -> p r u n", u=2)
-        w2_raw = {}
-        for a, b in W2_LOADS:
-            rows = keep.tile([P, b - a, PACK, N], F32, name=f"w2_raw{a}", align_bytes=256)
-            w2_raw.update({e: rows[:, e - a] for e in range(a, b)})
-            w2_loads.append((rows, a, b))
-        last_h = []
+        w2_raw.append(w2_last.rearrange("p r (u n) -> p r u n", u=2))
         slot_words = {}
         slot_bytes = {}
         cast = {}
@@ -94,87 +82,91 @@ def tile_routed_moe_kernel(tc, xT, w1, w3, w2, gate, offs, pos1, pos2, out):
         def whole(w, e):
             return 2 * e + w < WHOLE
 
-        def last_piece(a, b):
-            rows = staged(*LAST[:2])[:, LAST[2]].rearrange("p k c -> p (k c)")
-            return rows[:, a * PACK * PACK : b * PACK * PACK].rearrange("p (k c) -> p k c", k=PACK)
+        def column_half(s, side):
+            rows = staged(1, LAST)[:, s].rearrange("p k c -> p (k c)")
+            return rows.rearrange("p (side k c) -> p side k c", side=2, k=PACK)[:, side]
 
         def load(w, e):
             src = (w1, w3)[w][e].rearrange("(s p t) c -> p s t c", s=PASSES, t=PACK)
             if whole(w, e):
                 nc.sync.dma_start(out=staged(w, e)[:], in_=src)
+            elif (w, e) != (1, LAST):
+                for s in range(PASSES):
+                    nc.sync.dma_start(out=staged(w, e)[:, s], in_=src[:, s])
             else:
                 for s in range(PASSES):
-                    if (w, e, s) != LAST:
-                        nc.sync.dma_start(out=staged(w, e)[:, s], in_=src[:, s])
-                    else:
-                        for a, b, scalar_m in LAST_PIECES:
-                            nc.sync.dma_start(out=last_piece(a, b), in_=src[:, s, :, a * PACK : b * PACK])
+                    for side in range(2):
+                        columns = src[:, s, :, side * H // 2 : (side + 1) * H // 2]
+                        nc.sync.dma_start(out=column_half(s, side), in_=columns)
 
         def load_tail():
-            for rows, a, b in w2_loads:
-                nc.sync.dma_start(out=rows[:], in_=w2[a:b].rearrange("e (p t) n -> p e t n", t=PACK))
-            nc.sync.dma_start(out=w2_last, in_=w2[E - 1].rearrange("(p r u) n -> p r u n", r=2, u=2))
-            for which, (pos_t, pos) in enumerate(((pos1_t, pos1), (pos2_t, pos2))):
-                nc.sync.dma_start(pos_t[:], pos)
-                nc.sync.dma_start(out=gate_t[:, which, :], in_=gate[which])
+            for e in range(E):
+                nc.sync.dma_start(out=w2_raw[e], in_=w2[e].rearrange("(p r u) n -> p r u n", r=2, u=2))
+            nc.sync.dma_start(pos1_t[:], pos1)
+            nc.sync.dma_start(out=gate_t[:], in_=gate.rearrange("g p n -> p g n"))
+            nc.sync.dma_start(pos2_t[:], pos2)
 
-        def share_cast(raw, to, scalar_m, cut=0, pairs=False):
-            src = raw.rearrange("p k (m t) -> p m k t", t=PACK)
-            width = to.shape[1]
-            for a, b in ((0, cut), (cut, scalar_m)) if 0 < cut < scalar_m else ((0, scalar_m),):
-                if b > a:
-                    nc.scalar.copy(to[:, a:b], src[:, a:b])
-            for a, b in ((cut, width), (scalar_m, cut)) if cut > scalar_m else ((scalar_m, width),):
-                for t0, t1 in ((0, 2), (2, PACK)) if pairs else ((0, PACK),):
-                    if b > a:
-                        nc.vector.tensor_copy(to[:, a:b, :, t0:t1], src[:, a:b, :, t0:t1])
+        def by_column(raw):
+            return raw.rearrange("p k (m t) -> p m k t", t=PACK)
+
+        def cast_in_pairs(to, src):
+            for a, b in TILE_PAIRS:
+                nc.vector.tensor_copy(to[:, :, :, a:b], src[:, :, :, a:b])
 
         def cast_tile(w, e, s):
             w_bf = work.tile([P, H * PACK], BF16, name="w_bf", align_bytes=64, bufs=4)
             cast[(w, e, s)] = w_bf
             return w_bf[:].rearrange("p (t m k) -> p m k t", t=PACK, k=PACK)
 
-        def in_pairs(w, e, s):
-            return not whole(w, e) and (w, e, s) in PAIRS
+        def h_pass(e):
+            return 1 if whole(0, e) else 0
 
         def cast_w(w, e, s, scalar_m):
-            held = (1 if whole(w, e) else 0) if w == 0 else (0 if whole(w, e) else 1)
-            cut = P // 2 if s == held and (w, e) != (0, 0) and CUT[w] else 0
-            share_cast(staged(w, e)[:, s], cast_tile(w, e, s), scalar_m, cut, in_pairs(w, e, s))
+            src, to = by_column(staged(w, e)[:, s]), cast_tile(w, e, s)
+            if scalar_m > 0:
+                nc.scalar.copy(to[:, 0:scalar_m], src[:, 0:scalar_m])
+            if (w, e, s) == (0, LAST, 1):
+                cast_in_pairs(to[:, scalar_m:], src[:, scalar_m:])
+            elif w == 0 and s == h_pass(e) and scalar_m < P // 2:
+                nc.vector.tensor_copy(to[:, P // 2 :], src[:, P // 2 :])
+                nc.vector.tensor_copy(to[:, scalar_m : P // 2], src[:, scalar_m : P // 2])
+            elif scalar_m < P:
+                nc.vector.tensor_copy(to[:, scalar_m:], src[:, scalar_m:])
 
         def code_tiles(w, e, s):
             words = quant.tile([P, H], U32, name="w_words", align_bytes=64)
             scales = quant.tile([P, H], U8, name="w_scales", align_bytes=64)
             quantised[(w, e, s)] = (words, scales)
 
-        def quantise_columns(w, e, s, a, b):
+        def quantise_tiles(w, e, s, a, b):
             words, scales = quantised[(w, e, s)]
             nc.vector.quantize_mx(
-                out=words[:, a:b].bitcast(FP8X4), scales=scales[:, a:b], in_=cast[(w, e, s)][:, PACK * a : PACK * b]
+                out=words[:, a * P : b * P].bitcast(FP8X4),
+                scales=scales[:, a * P : b * P],
+                in_=cast[(w, e, s)][:, a * K_PASS : b * K_PASS],
             )
 
         def quantise_w(w, e, s):
             code_tiles(w, e, s)
-            for a, b in ((0, H // 2), (H // 2, H)) if in_pairs(w, e, s) else ((0, H),):
-                quantise_columns(w, e, s, a, b)
+            for a, b in TILE_PAIRS if (w, e, s) in ((0, LAST, 1), (1, LAST, 0)) else ((0, PACK),):
+                quantise_tiles(w, e, s, a, b)
 
         def w2_views(e, to, order):
-            raw = w2_raw[e].rearrange("p (r u) n -> p r u n", r=2) if e < E - 1 else w2_last
             w2_cast[e] = to
             return (
                 to.rearrange("p (c j r u) -> p " + order, j=RUN, r=2, u=2),
-                raw.rearrange("p r u (c j) -> p " + order, j=RUN),
+                w2_raw[e].rearrange("p r u (c j) -> p " + order, j=RUN),
             )
 
-        def cast_w2(e, copy):
+        def cast_w2(e):
             w_bf = keep.tile([P, N * PACK], BF16, name=f"w2_bf{e}", align_bytes=64)
             to, src = w2_views(e, w_bf[:], "c r u j")
             groups = N // RUN
-            for a, b in ((0, groups),) if e < E - 1 else ((0, groups // 2), (groups // 2, groups)):
-                copy(to[:, a:b], src[:, a:b])
+            for a, b in ((0, groups),) if e < LAST else ((0, groups // 2), (groups // 2, groups)):
+                nc.scalar.copy(to[:, a:b], src[:, a:b])
 
         def cast_w2_on_gpsimd(e):
-            to, src = w2_views(e, w2_cast[GAP - 1], "c j r u")
+            to, src = w2_views(e, w2_cast[EARLY_W2 - 1], "c j r u")
             nc.gpsimd.tensor_scalar(to, src, 1.0, 0.0, MULT, ADD)
 
         def quantise_w2(e):
@@ -220,36 +212,33 @@ def tile_routed_moe_kernel(tc, xT, w1, w3, w2, gate, offs, pos1, pos2, out):
             return acc[:].rearrange("p t (g j) -> p g j t", g=PACK)
 
         def rectify(e, half):
-            rows = staged(1, e)[:, 0 if whole(1, e) or e == E - 1 else 1]
+            rows = staged(1, e)[:, 0 if whole(1, e) else 1] if e < LAST else column_half(0, 0)
             r = rows[:, :, half * HALF : (half + 1) * HALF].rearrange("p g (j t) -> p g j t", t=PACK)
             nc.scalar.activation(r, by_slot(sums[(0, e, half)]), RELU)
             relus[(e, half)] = r
 
-        def hide(e, half):
-            if e < E - 1:
-                h = staged(0, e + 1)[:, 1 if whole(0, e + 1) else 0, half, H // 2 : H].bitcast(BF16)
-            else:
-                if half == 0:
-                    last_h.append(keep.tile([P, C * PACK], BF16, name=f"w2_raw{GAP - 1}", align_bytes=256))
-                h = last_h[0][:, half * K_PASS : (half + 1) * K_PASS]
+        def hide(e, half, h):
             nc.vector.tensor_tensor(
                 h.rearrange("p (g j t) -> p g j t", g=PACK, t=PACK), by_slot(sums[(1, e, half)]), relus[(e, half)], MULT
             )
             hidden[(e, half)] = h
 
+        def hide_in_next_w1(e, half):
+            hide(e, half, staged(0, e + 1)[:, h_pass(e + 1), half, H // 2 : H].bitcast(BF16))
+
         def quantise_h(e, half):
-            words = work.tile([P, HALF], U32, name="h_words", align_bytes=64, bufs=2 * (E - 1))
-            scales = work.tile([P, HALF], U8, name="h_scales", align_bytes=64, bufs=2 * (E - 1))
+            words = work.tile([P, HALF], U32, name="h_words", align_bytes=64, bufs=2 * LAST)
+            scales = work.tile([P, HALF], U8, name="h_scales", align_bytes=64, bufs=2 * LAST)
             nc.vector.quantize_mx(out=words[:].bitcast(FP8X4), scales=scales[:], in_=hidden[(e, half)])
             hidden_q[(e, half)] = (words[:], scales[:])
 
-        def quantise_last_h():
-            words = keep.tile([P, C], U32, name=f"w2_raw{PIN}", align_bytes=256)
+        def quantise_last_h(h):
+            words = keep.tile([P, C], U32, name=f"w2_raw{LAST - 1}", align_bytes=256)
             scales = keep.tile([P, C], U8, name="last_h_scales", align_bytes=64)
-            nc.vector.quantize_mx(out=words[:].bitcast(FP8X4), scales=scales[:], in_=last_h[0][:])
+            nc.vector.quantize_mx(out=words[:].bitcast(FP8X4), scales=scales[:], in_=h)
             for half in range(2):
                 cols = slice(half * HALF, (half + 1) * HALF)
-                hidden_q[(E - 1, half)] = (words[:, cols], scales[:, cols])
+                hidden_q[(LAST, half)] = (words[:, cols], scales[:, cols])
 
         def project_back(e, half, acc):
             w_words, w_scales = w2_quantised[e]
@@ -273,11 +262,10 @@ def tile_routed_moe_kernel(tc, xT, w1, w3, w2, gate, offs, pos1, pos2, out):
             copy(y_all[:, a * C : b * C], acc[:])
 
         def finish_last_expert():
-            e = E - 1
-            for half, copy in enumerate((nc.vector.tensor_copy, nc.scalar.copy)):
-                acc = sums[(0, e, half)][:, 0, :]
-                project_back(e, half, acc)
-                col = e * C + half * HALF
+            for half, copy in enumerate((nc.scalar.copy, nc.vector.tensor_copy)):
+                acc = sums[(0, LAST, half)][:, 0, :]
+                project_back(LAST, half, acc)
+                col = LAST * C + half * HALF
                 copy(y_all[:, col : col + HALF], acc)
 
         nc.gpsimd.memset(x_bytes[:], 0)
@@ -310,28 +298,26 @@ def tile_routed_moe_kernel(tc, xT, w1, w3, w2, gate, offs, pos1, pos2, out):
                 load(*matrices[i + AHEAD])
             if i + AHEAD == len(matrices):
                 load_tail()
-            if i == 0:
-                shares = (P, P)
-            elif i == 1:
-                shares = SECOND_SHARES
+            if e == LAST:
+                shares = LAST_W1_SHARES
             else:
-                shares = (FIFTH if e == 4 and whole(w, e) else WHOLE_SHARES if whole(w, e) else PASS_SHARES if e < E - 1 else LAST_SHARES)[w]
+                shares = (FIRST_SHARES if e == 0 else WHOLE_SHARES if whole(w, e) else PASS_SHARES)[w]
             first, second = (1, 0) if whole(w, e) else (0, 1)
             before = e - 1 if w == 0 and e > 0 else None
             cast_w(w, e, first, shares[first])
             if whole(w, e):
                 cast_w(w, e, second, shares[second])
             if before is not None:
-                hide(before, 0)
+                hide_in_next_w1(before, 0)
                 if whole(w, e):
-                    hide(before, 1)
+                    hide_in_next_w1(before, 1)
                     quantise_h(before, 0)
             quantise_w(w, e, first)
             for half in range(2):
                 project(w, e, half, first, True)
             if not whole(w, e):
                 if before is not None:
-                    hide(before, 1)
+                    hide_in_next_w1(before, 1)
                     quantise_h(before, 0)
                 cast_w(w, e, second, shares[second])
             if w == 1:
@@ -348,37 +334,38 @@ def tile_routed_moe_kernel(tc, xT, w1, w3, w2, gate, offs, pos1, pos2, out):
                     gather_words(q, 1)
                     gather_bytes(q)
 
-        w, e, s = LAST
-        share_cast(staged(w, e)[:, 0], cast_tile(w, e, 0), LAST_SHARES[w][0], DCUT, in_pairs(w, e, 0))
+        to = cast_tile(1, LAST, 0)
+        nc.scalar.copy(to[:, 0 : P // 2], by_column(column_half(0, 0)))
+        cast_in_pairs(to[:, P // 2 :], by_column(column_half(0, 1)))
         for half in range(2):
-            rectify(e, half)
-        quantise_w(w, e, 0)
+            rectify(LAST, half)
+        quantise_w(1, LAST, 0)
         for half in range(2):
-            project(w, e, half, 0, True)
-        dst = cast_tile(*LAST)
-        for a, b, scalar_m in LAST_PIECES:
-            share_cast(last_piece(a, b), dst[:, a:b], scalar_m, 0, b == P)
-        code_tiles(*LAST)
+            project(1, LAST, half, 0, True)
+        to = cast_tile(1, LAST, 1)
+        nc.vector.tensor_copy(to[:, 0 : P // 2], by_column(column_half(1, 0)))
+        cast_in_pairs(to[:, P // 2 :], by_column(column_half(1, 1)))
+        code_tiles(1, LAST, 1)
         for t in range(PACK):
-            quantise_columns(w, e, s, t * P, (t + 1) * P)
+            quantise_tiles(1, LAST, 1, t, t + 1)
         for half in range(2):
-            project(w, e, half, s, False)
+            project(1, LAST, half, 1, False)
 
-        for late in range(GAP):
-            cast_w2(late, nc.scalar.copy)
-            quantise_w2(late)
-        for late in range(GAP, E):
-            if late == ON_G:
-                cast_w2_on_gpsimd(late)
+        for e in range(EARLY_W2):
+            cast_w2(e)
+            quantise_w2(e)
+        for e in range(EARLY_W2, E):
+            if e == GPSIMD_W2:
+                cast_w2_on_gpsimd(e)
             else:
-                cast_w2(late, nc.scalar.copy)
+                cast_w2(e)
+        last_h = keep.tile([P, C * PACK], BF16, name=f"w2_raw{EARLY_W2 - 1}", align_bytes=256)
         for half in range(2):
-            hide(e, half)
-        for late in range(GAP, PIN + 1):
-            quantise_w2(late)
-        quantise_last_h()
-        for late in range(PIN + 1, E):
-            quantise_w2(late)
+            hide(LAST, half, last_h[:, half * K_PASS : (half + 1) * K_PASS])
+        for e in range(EARLY_W2, LAST):
+            quantise_w2(e)
+        quantise_last_h(last_h[:])
+        quantise_w2(LAST)
         finish_experts(0, 2, nc.scalar.copy)
         finish_experts(2, 4, nc.vector.tensor_copy)
         finish_experts(4, 5, nc.scalar.copy)

@@ -19,6 +19,7 @@ FP8X4 = mybir.dt.float8_e4m3fn_x4
 MULT = mybir.AluOpType.mult
 ADD = mybir.AluOpType.add
 RELU = mybir.ActivationFunctionType.Relu
+COPY = mybir.ActivationFunctionType.Copy
 
 LIST_ROWS = 16
 SLICE = 512
@@ -103,8 +104,8 @@ def tile_routed_moe_kernel(tc, xT, w1, w3, w2, gate, offs, pos1, pos2, out):
             for e in range(E):
                 nc.sync.dma_start(out=w2_raw[e], in_=w2[e].rearrange("(p r u) n -> p r u n", r=2, u=2))
             nc.sync.dma_start(pos1_t[:], pos1)
-            nc.sync.dma_start(out=gate_t[:], in_=gate.rearrange("g p n -> p g n"))
             nc.sync.dma_start(pos2_t[:], pos2)
+            nc.sync.dma_start(out=gate_t[:], in_=gate.rearrange("g p n -> p g n"))
 
         def by_column(raw):
             return raw.rearrange("p k (m t) -> p m k t", t=PACK)
@@ -371,12 +372,17 @@ def tile_routed_moe_kernel(tc, xT, w1, w3, w2, gate, offs, pos1, pos2, out):
         finish_experts(4, 5, nc.scalar.copy)
         finish_last_expert()
 
+        fetched = []
+        for a, b in OUT_PIECES:
+            second = work.tile([P, b - a], F32, name="second")
+            nc.scalar.activation(second[:], y_all[:].indirect(list_columns(pos2_t, a, b)), COPY)
+            fetched.append(second)
         first_products = keep.tile([P, T], F32, name="first_products")
         nc.vector.tensor_tensor(first_products[:], y_all[:].indirect(pos1_t[:]), gate_t[:, 0, :], MULT)
         second_products = []
-        for a, b in OUT_PIECES:
+        for (a, b), second in zip(OUT_PIECES, fetched):
             prod = work.tile([P, b - a], F32, name="second_products")
-            nc.vector.tensor_tensor(prod[:], y_all[:].indirect(list_columns(pos2_t, a, b)), gate_t[:, 1, a:b], MULT)
+            nc.vector.tensor_tensor(prod[:], second[:], gate_t[:, 1, a:b], MULT)
             second_products.append(prod)
         for (a, b), prod in zip(OUT_PIECES, second_products):
             o = work.tile([P, b - a], F32, name="o", align_bytes=256)

@@ -38,10 +38,11 @@ FIRST_SHARES = ((P, P), (P, 96))
 WHOLE_SHARES = ((P, 24), (112, 0))
 PASS_SHARES = ((40, 96), (80, 40))
 LAST_W1_SHARES = (P // 2, 80)
+LAST_PASS_0_SHARE = 44
 TILE_PAIRS = ((0, 2), (2, PACK))
 EARLY_W2 = 2
 GPSIMD_W2 = 3
-OUT_PIECES = ((0, T // 2), (T // 2, T))
+OUT_PIECES = ((0, 448), (448, 640), (640, T))
 
 
 def tile_routed_moe_kernel(tc, xT, w1, w3, w2, gate, offs, pos1, pos2, out):
@@ -95,10 +96,10 @@ def tile_routed_moe_kernel(tc, xT, w1, w3, w2, gate, offs, pos1, pos2, out):
                 for s in range(PASSES):
                     nc.sync.dma_start(out=staged(w, e)[:, s], in_=src[:, s])
             else:
-                for s in range(PASSES):
-                    for side in range(2):
-                        columns = src[:, s, :, side * H // 2 : (side + 1) * H // 2]
-                        nc.sync.dma_start(out=column_half(s, side), in_=columns)
+                nc.sync.dma_start(out=staged(w, e)[:, 0], in_=src[:, 0])
+                for side in range(2):
+                    columns = src[:, 1, :, side * H // 2 : (side + 1) * H // 2]
+                    nc.sync.dma_start(out=column_half(1, side), in_=columns)
 
         def load_tail():
             for e in range(E):
@@ -213,7 +214,7 @@ def tile_routed_moe_kernel(tc, xT, w1, w3, w2, gate, offs, pos1, pos2, out):
             return acc[:].rearrange("p t (g j) -> p g j t", g=PACK)
 
         def rectify(e, half):
-            rows = staged(1, e)[:, 0 if whole(1, e) else 1] if e < LAST else column_half(0, 0)
+            rows = staged(1, e)[:, 0 if whole(1, e) or e == LAST else 1]
             r = rows[:, :, half * HALF : (half + 1) * HALF].rearrange("p g (j t) -> p g j t", t=PACK)
             nc.scalar.activation(r, by_slot(sums[(0, e, half)]), RELU)
             relus[(e, half)] = r
@@ -336,8 +337,9 @@ def tile_routed_moe_kernel(tc, xT, w1, w3, w2, gate, offs, pos1, pos2, out):
                     gather_bytes(q)
 
         to = cast_tile(1, LAST, 0)
-        nc.scalar.copy(to[:, 0 : P // 2], by_column(column_half(0, 0)))
-        cast_in_pairs(to[:, P // 2 :], by_column(column_half(0, 1)))
+        src = by_column(staged(1, LAST)[:, 0])
+        nc.scalar.copy(to[:, 0:LAST_PASS_0_SHARE], src[:, 0:LAST_PASS_0_SHARE])
+        cast_in_pairs(to[:, LAST_PASS_0_SHARE:], src[:, LAST_PASS_0_SHARE:])
         for half in range(2):
             rectify(LAST, half)
         quantise_w(1, LAST, 0)
@@ -372,19 +374,37 @@ def tile_routed_moe_kernel(tc, xT, w1, w3, w2, gate, offs, pos1, pos2, out):
         finish_experts(4, 5, nc.scalar.copy)
         finish_last_expert()
 
-        fetched = []
-        for a, b in OUT_PIECES:
-            second = work.tile([P, b - a], F32, name="second")
-            nc.scalar.activation(second[:], y_all[:].indirect(list_columns(pos2_t, a, b)), COPY)
-            fetched.append(second)
+        def fetch(positions, a, b):
+            fetched = keep.tile([P, b - a], F32, name=f"fetched_{a}_{b}_{len(fetches)}")
+            nc.scalar.activation(fetched[:], y_all[:].indirect(list_columns(positions, a, b)), COPY)
+            fetches.append(fetched)
+            return fetched
+
+        fetches = []
+        cut = OUT_PIECES[-1][0]
         first_products = keep.tile([P, T], F32, name="first_products")
-        nc.vector.tensor_tensor(first_products[:], y_all[:].indirect(pos1_t[:]), gate_t[:, 0, :], MULT)
-        second_products = []
-        for (a, b), second in zip(OUT_PIECES, fetched):
-            prod = work.tile([P, b - a], F32, name="second_products")
-            nc.vector.tensor_tensor(prod[:], second[:], gate_t[:, 1, a:b], MULT)
-            second_products.append(prod)
-        for (a, b), prod in zip(OUT_PIECES, second_products):
-            o = work.tile([P, b - a], F32, name="o", align_bytes=256)
-            nc.vector.tensor_tensor(o[:], first_products[:, a:b], prod[:], ADD)
-            nc.sync.dma_start(out=out[:, a:b], in_=o[:])
+        second_products = keep.tile([P, T], F32, name="second_products")
+        seconds = [fetch(pos2_t, *OUT_PIECES[0])]
+        last_firsts = fetch(pos1_t, cut, T)
+        seconds += [fetch(pos2_t, a, b) for a, b in OUT_PIECES[1:]]
+
+        def weigh(j):
+            a, b = OUT_PIECES[j]
+            nc.vector.tensor_tensor(second_products[:, a:b], seconds[j][:], gate_t[:, 1, a:b], MULT)
+
+        def add_and_store(j, o):
+            a, b = OUT_PIECES[j]
+            nc.vector.tensor_tensor(o, first_products[:, a:b], second_products[:, a:b], ADD)
+            nc.sync.dma_start(out=out[:, a:b], in_=o)
+
+        nc.vector.tensor_tensor(
+            first_products[:, 0:cut], y_all[:].indirect(list_columns(pos1_t, 0, cut)), gate_t[:, 0, 0:cut], MULT
+        )
+        weigh(0)
+        nc.vector.tensor_tensor(first_products[:, cut:T], last_firsts[:], gate_t[:, 0, cut:T], MULT)
+        sums_out = keep.tile([P, T], F32, name="sums_out", align_bytes=256)
+        add_and_store(0, sums_out[:, OUT_PIECES[0][0] : OUT_PIECES[0][1]])
+        weigh(1)
+        weigh(2)
+        add_and_store(1, y_all[:, OUT_PIECES[1][0] : OUT_PIECES[1][1]])
+        add_and_store(2, sums_out[:, cut:T])

@@ -211,18 +211,17 @@ def tile_routed_moe_kernel(tc, xT, w1, w3, w2, gate, offs, pos1, pos2, out):
                 )
 
         def by_slot(acc):
-            return acc[:].rearrange("p t (g j) -> p g j t", g=PACK)
+            return acc[:].rearrange("p t (g j u) -> p g j t u", g=PACK, u=2)
 
         def rectify(e, half):
             rows = staged(1, e)[:, 0 if whole(1, e) or e == LAST else 1]
-            r = rows[:, :, half * HALF : (half + 1) * HALF].rearrange("p g (j t) -> p g j t", t=PACK)
+            r = rows[:, :, half * HALF : (half + 1) * HALF].rearrange("p g (j t u) -> p g j t u", t=PACK, u=2)
             nc.scalar.activation(r, by_slot(sums[(0, e, half)]), RELU)
             relus[(e, half)] = r
 
         def hide(e, half, h):
-            nc.vector.tensor_tensor(
-                h.rearrange("p (g j t) -> p g j t", g=PACK, t=PACK), by_slot(sums[(1, e, half)]), relus[(e, half)], MULT
-            )
+            to = h.rearrange("p (g j u t) -> p g j t u", g=PACK, t=PACK, u=2)
+            nc.vector.tensor_tensor(to, by_slot(sums[(1, e, half)]), relus[(e, half)], MULT)
             hidden[(e, half)] = h
 
         def hide_in_next_w1(e, half):

@@ -42,7 +42,7 @@ LAST_PASS_0_SHARE = 44
 TILE_PAIRS = ((0, 2), (2, PACK))
 EARLY_W2 = 2
 GPSIMD_W2 = 3
-OUT_PIECES = ((0, 448), (448, 640), (640, T))
+OUT_PIECES = ((0, T // 2), (T // 2, 5 * T // 6), (5 * T // 6, T))
 
 
 def tile_routed_moe_kernel(tc, xT, w1, w3, w2, gate, offs, pos1, pos2, out):
@@ -62,7 +62,7 @@ def tile_routed_moe_kernel(tc, xT, w1, w3, w2, gate, offs, pos1, pos2, out):
         x_words = [keep.tile([P, T], U32, name=f"x_words{s}", align_bytes=64) for s in range(PASSES)]
         x_bytes = keep.tile([P, T], U8, name="x_bytes", align_bytes=64)
         gate_t = keep.tile([P, 2, T], F32, name="gate_t", align_bytes=256)
-        ring = [keep.tile([P, PASSES, PACK, H], F32, name=f"ring{r}", align_bytes=256) for r in range(RING)]
+        ring = [keep.tile([P, PASSES, PACK, H], F32, name=f"ring{place}", align_bytes=256) for place in range(RING)]
         y_all = keep.tile([P, SLOTS], F32, name="y_all", align_bytes=256)
         w2_raw = [keep.tile([P, 2, 2, N], F32, name=f"w2_raw{e}", align_bytes=256)[:] for e in range(LAST)]
         w2_last = y_all[:, 2 * C - N // 2 : 6 * C - N // 2].rearrange("p (r c) -> p r c", r=2)[:, :, 0:C]
@@ -84,8 +84,8 @@ def tile_routed_moe_kernel(tc, xT, w1, w3, w2, gate, offs, pos1, pos2, out):
         def whole(w, e):
             return 2 * e + w < WHOLE
 
-        def column_half(s, side):
-            rows = staged(1, LAST)[:, s].rearrange("p k c -> p (k c)")
+        def column_half(side):
+            rows = staged(1, LAST)[:, 1].rearrange("p k c -> p (k c)")
             return rows.rearrange("p (side k c) -> p side k c", side=2, k=PACK)[:, side]
 
         def load(w, e):
@@ -99,7 +99,7 @@ def tile_routed_moe_kernel(tc, xT, w1, w3, w2, gate, offs, pos1, pos2, out):
                 nc.sync.dma_start(out=staged(w, e)[:, 0], in_=src[:, 0])
                 for side in range(2):
                     columns = src[:, 1, :, side * H // 2 : (side + 1) * H // 2]
-                    nc.sync.dma_start(out=column_half(1, side), in_=columns)
+                    nc.sync.dma_start(out=column_half(side), in_=columns)
 
         def load_tail():
             for e in range(E):
@@ -112,8 +112,8 @@ def tile_routed_moe_kernel(tc, xT, w1, w3, w2, gate, offs, pos1, pos2, out):
             return raw.rearrange("p k (m t) -> p m k t", t=PACK)
 
         def cast_in_pairs(to, src):
-            for a, b in TILE_PAIRS:
-                nc.vector.tensor_copy(to[:, :, :, a:b], src[:, :, :, a:b])
+            for lo, hi in TILE_PAIRS:
+                nc.vector.tensor_copy(to[:, :, :, lo:hi], src[:, :, :, lo:hi])
 
         def cast_tile(w, e, s):
             w_bf = work.tile([P, H * PACK], BF16, name="w_bf", align_bytes=64, bufs=4)
@@ -140,18 +140,18 @@ def tile_routed_moe_kernel(tc, xT, w1, w3, w2, gate, offs, pos1, pos2, out):
             scales = quant.tile([P, H], U8, name="w_scales", align_bytes=64)
             quantised[(w, e, s)] = (words, scales)
 
-        def quantise_tiles(w, e, s, a, b):
+        def quantise_tiles(w, e, s, lo, hi):
             words, scales = quantised[(w, e, s)]
             nc.vector.quantize_mx(
-                out=words[:, a * P : b * P].bitcast(FP8X4),
-                scales=scales[:, a * P : b * P],
-                in_=cast[(w, e, s)][:, a * K_PASS : b * K_PASS],
+                out=words[:, lo * P : hi * P].bitcast(FP8X4),
+                scales=scales[:, lo * P : hi * P],
+                in_=cast[(w, e, s)][:, lo * K_PASS : hi * K_PASS],
             )
 
         def quantise_w(w, e, s):
             code_tiles(w, e, s)
-            for a, b in TILE_PAIRS if (w, e, s) in ((0, LAST, 1), (1, LAST, 0)) else ((0, PACK),):
-                quantise_tiles(w, e, s, a, b)
+            for lo, hi in TILE_PAIRS if (w, e, s) in ((0, LAST, 1), (1, LAST, 0)) else ((0, PACK),):
+                quantise_tiles(w, e, s, lo, hi)
 
         def w2_views(e, to, order):
             w2_cast[e] = to
@@ -164,8 +164,8 @@ def tile_routed_moe_kernel(tc, xT, w1, w3, w2, gate, offs, pos1, pos2, out):
             w_bf = keep.tile([P, N * PACK], BF16, name=f"w2_bf{e}", align_bytes=64)
             to, src = w2_views(e, w_bf[:], "c r u j")
             groups = N // RUN
-            for a, b in ((0, groups),) if e < LAST else ((0, groups // 2), (groups // 2, groups)):
-                nc.scalar.copy(to[:, a:b], src[:, a:b])
+            for lo, hi in ((0, groups),) if e < LAST else ((0, groups // 2), (groups // 2, groups)):
+                nc.scalar.copy(to[:, lo:hi], src[:, lo:hi])
 
         def cast_w2_on_gpsimd(e):
             to, src = w2_views(e, w2_cast[EARLY_W2 - 1], "c j r u")
@@ -177,8 +177,8 @@ def tile_routed_moe_kernel(tc, xT, w1, w3, w2, gate, offs, pos1, pos2, out):
             nc.vector.quantize_mx(out=words[:].bitcast(FP8X4), scales=scales[:], in_=w2_cast[e])
             w2_quantised[e] = (words[:], scales[:])
 
-        def list_columns(tile, a, b):
-            return tile[:, a // LIST_ROWS : b // LIST_ROWS]
+        def list_columns(tile, lo, hi):
+            return tile[:, lo // LIST_ROWS : hi // LIST_ROWS]
 
         def gather_words(q, s):
             if s == 0:
@@ -193,7 +193,7 @@ def tile_routed_moe_kernel(tc, xT, w1, w3, w2, gate, offs, pos1, pos2, out):
             slot_bytes[q] = scales
 
         def project(w, e, half, s, opens):
-            q, a = divmod(e * C + half * HALF, SLICE)
+            q, lo = divmod(e * C + half * HALF, SLICE)
             if opens:
                 acc = psum.tile([P, PACK, HALF], F32, name=("acc_a", "acc_b")[w])
                 sums[(w, e, half)] = acc
@@ -204,23 +204,23 @@ def tile_routed_moe_kernel(tc, xT, w1, w3, w2, gate, offs, pos1, pos2, out):
                     out=sums[(w, e, half)][:, t, :],
                     lhsT=words[:, t * P : (t + 1) * P].bitcast(FP8X4),
                     lhsT_scale=scales[:, t * P : (t + 1) * P],
-                    rhs=slot_words[q][:, s, a : a + HALF].bitcast(FP8X4),
-                    rhs_scale=slot_bytes[q][SCALE_ROW[s] : P, a : a + HALF],
+                    rhs=slot_words[q][:, s, lo : lo + HALF].bitcast(FP8X4),
+                    rhs_scale=slot_bytes[q][SCALE_ROW[s] : P, lo : lo + HALF],
                     start=(opens and t == tiles[0]),
                     stop=(not opens and t == tiles[-1]),
                 )
 
         def by_slot(acc):
-            return acc[:].rearrange("p t (g j u) -> p g j t u", g=PACK, u=2)
+            return acc[:].rearrange("p t (g j d) -> p g j t d", g=PACK, d=2)
 
         def rectify(e, half):
             rows = staged(1, e)[:, 0 if whole(1, e) or e == LAST else 1]
-            r = rows[:, :, half * HALF : (half + 1) * HALF].rearrange("p g (j t u) -> p g j t u", t=PACK, u=2)
-            nc.scalar.activation(r, by_slot(sums[(0, e, half)]), RELU)
-            relus[(e, half)] = r
+            relu = rows[:, :, half * HALF : (half + 1) * HALF].rearrange("p g (j t d) -> p g j t d", t=PACK, d=2)
+            nc.scalar.activation(relu, by_slot(sums[(0, e, half)]), RELU)
+            relus[(e, half)] = relu
 
         def hide(e, half, h):
-            to = h.rearrange("p (g j u t) -> p g j t u", g=PACK, t=PACK, u=2)
+            to = h.rearrange("p (g j d t) -> p g j t d", g=PACK, t=PACK, d=2)
             nc.vector.tensor_tensor(to, by_slot(sums[(1, e, half)]), relus[(e, half)], MULT)
             hidden[(e, half)] = h
 
@@ -254,13 +254,13 @@ def tile_routed_moe_kernel(tc, xT, w1, w3, w2, gate, offs, pos1, pos2, out):
                 stop=True,
             )
 
-        def finish_experts(a, b, copy):
-            acc = psum_y.tile([P, (b - a) * C], F32, name="acc_y")
-            for e in range(a, b):
+        def finish_experts(lo, hi, copy):
+            acc = psum_y.tile([P, (hi - lo) * C], F32, name="acc_y")
+            for e in range(lo, hi):
                 for half in range(2):
-                    col = (e - a) * C + half * HALF
+                    col = (e - lo) * C + half * HALF
                     project_back(e, half, acc[:, col : col + HALF])
-            copy(y_all[:, a * C : b * C], acc[:])
+            copy(y_all[:, lo * C : hi * C], acc[:])
 
         def finish_last_expert():
             for half, copy in enumerate((nc.scalar.copy, nc.vector.tensor_copy)):
@@ -285,19 +285,19 @@ def tile_routed_moe_kernel(tc, xT, w1, w3, w2, gate, offs, pos1, pos2, out):
             src = x_raw[s][:].rearrange("p t (c j) -> p c t j", j=RUN)
             nc.scalar.copy(dst[:, X_SHARE[s] :], src[:, X_SHARE[s] :])
             nc.vector.tensor_copy(dst[:, 0 : X_SHARE[s]], src[:, 0 : X_SHARE[s]])
-            for a, b in X_CALLS:
+            for lo, hi in X_CALLS:
                 nc.vector.quantize_mx(
-                    out=x_words[s][:, a:b].bitcast(FP8X4),
-                    scales=x_bytes[SCALE_ROW[s] : P, a:b],
-                    in_=x_bf[s][:, PACK * a : PACK * b],
+                    out=x_words[s][:, lo:hi].bitcast(FP8X4),
+                    scales=x_bytes[SCALE_ROW[s] : P, lo:hi],
+                    in_=x_bf[s][:, PACK * lo : PACK * hi],
                 )
             gather_words(0, s)
         gather_bytes(0)
 
-        for i, (w, e) in enumerate(matrices[:-1]):
-            if i + AHEAD < len(matrices):
-                load(*matrices[i + AHEAD])
-            if i + AHEAD == len(matrices):
+        for step, (w, e) in enumerate(matrices[:-1]):
+            if step + AHEAD < len(matrices):
+                load(*matrices[step + AHEAD])
+            if step + AHEAD == len(matrices):
                 load_tail()
             if e == LAST:
                 shares = LAST_W1_SHARES
@@ -329,7 +329,7 @@ def tile_routed_moe_kernel(tc, xT, w1, w3, w2, gate, offs, pos1, pos2, out):
             quantise_w(w, e, second)
             for half in range(2):
                 project(w, e, half, second, False)
-            if i == 0:
+            if step == 0:
                 for q in range(1, SLOTS // SLICE):
                     gather_words(q, 0)
                     gather_words(q, 1)
@@ -345,8 +345,8 @@ def tile_routed_moe_kernel(tc, xT, w1, w3, w2, gate, offs, pos1, pos2, out):
         for half in range(2):
             project(1, LAST, half, 0, True)
         to = cast_tile(1, LAST, 1)
-        nc.vector.tensor_copy(to[:, 0 : P // 2], by_column(column_half(1, 0)))
-        cast_in_pairs(to[:, P // 2 :], by_column(column_half(1, 1)))
+        nc.vector.tensor_copy(to[:, 0 : P // 2], by_column(column_half(0)))
+        cast_in_pairs(to[:, P // 2 :], by_column(column_half(1)))
         code_tiles(1, LAST, 1)
         for t in range(PACK):
             quantise_tiles(1, LAST, 1, t, t + 1)
@@ -373,37 +373,38 @@ def tile_routed_moe_kernel(tc, xT, w1, w3, w2, gate, offs, pos1, pos2, out):
         finish_experts(4, 5, nc.scalar.copy)
         finish_last_expert()
 
-        def fetch(positions, a, b):
-            fetched = keep.tile([P, b - a], F32, name=f"fetched_{a}_{b}_{len(fetches)}")
-            nc.scalar.activation(fetched[:], y_all[:].indirect(list_columns(positions, a, b)), COPY)
-            fetches.append(fetched)
+        def fetch(name, positions, lo, hi):
+            fetched = keep.tile([P, hi - lo], F32, name=name)
+            nc.scalar.activation(fetched[:], y_all[:].indirect(list_columns(positions, lo, hi)), COPY)
             return fetched
 
-        fetches = []
-        cut = OUT_PIECES[-1][0]
+        def weigh_second(piece):
+            lo, hi = OUT_PIECES[piece]
+            nc.vector.tensor_tensor(second_products[:, lo:hi], seconds[piece][:], gate_t[:, 1, lo:hi], MULT)
+
+        def add_and_store(piece, to):
+            lo, hi = OUT_PIECES[piece]
+            nc.vector.tensor_tensor(to[:, lo:hi], first_products[:, lo:hi], second_products[:, lo:hi], ADD)
+            nc.sync.dma_start(out=out[:, lo:hi], in_=to[:, lo:hi])
+
+        last_piece = OUT_PIECES[-1][0]
         first_products = keep.tile([P, T], F32, name="first_products")
         second_products = keep.tile([P, T], F32, name="second_products")
-        seconds = [fetch(pos2_t, *OUT_PIECES[0])]
-        last_firsts = fetch(pos1_t, cut, T)
-        seconds += [fetch(pos2_t, a, b) for a, b in OUT_PIECES[1:]]
-
-        def weigh(j):
-            a, b = OUT_PIECES[j]
-            nc.vector.tensor_tensor(second_products[:, a:b], seconds[j][:], gate_t[:, 1, a:b], MULT)
-
-        def add_and_store(j, o):
-            a, b = OUT_PIECES[j]
-            nc.vector.tensor_tensor(o, first_products[:, a:b], second_products[:, a:b], ADD)
-            nc.sync.dma_start(out=out[:, a:b], in_=o)
+        seconds = [fetch("second0", pos2_t, *OUT_PIECES[0])]
+        last_firsts = fetch("last_firsts", pos1_t, last_piece, T)
+        seconds += [fetch(f"second{piece}", pos2_t, *OUT_PIECES[piece]) for piece in (1, 2)]
 
         nc.vector.tensor_tensor(
-            first_products[:, 0:cut], y_all[:].indirect(list_columns(pos1_t, 0, cut)), gate_t[:, 0, 0:cut], MULT
+            first_products[:, 0:last_piece],
+            y_all[:].indirect(list_columns(pos1_t, 0, last_piece)),
+            gate_t[:, 0, 0:last_piece],
+            MULT,
         )
-        weigh(0)
-        nc.vector.tensor_tensor(first_products[:, cut:T], last_firsts[:], gate_t[:, 0, cut:T], MULT)
-        sums_out = keep.tile([P, T], F32, name="sums_out", align_bytes=256)
-        add_and_store(0, sums_out[:, OUT_PIECES[0][0] : OUT_PIECES[0][1]])
-        weigh(1)
-        weigh(2)
-        add_and_store(1, y_all[:, OUT_PIECES[1][0] : OUT_PIECES[1][1]])
-        add_and_store(2, sums_out[:, cut:T])
+        weigh_second(0)
+        nc.vector.tensor_tensor(first_products[:, last_piece:T], last_firsts[:], gate_t[:, 0, last_piece:T], MULT)
+        total = keep.tile([P, T], F32, name="total", align_bytes=256)
+        add_and_store(0, total)
+        weigh_second(1)
+        weigh_second(2)
+        add_and_store(1, y_all)
+        add_and_store(2, total)

@@ -25,6 +25,7 @@ LIST_ROWS = 16
 SLICE = 512
 HALF = C // 2
 RUN = 4
+W2_RUN = 2
 X_CALLS = ((0, 512), (512, T))
 SCALE_ROW = (0, 4)
 
@@ -156,14 +157,14 @@ def tile_routed_moe_kernel(tc, xT, w1, w3, w2, gate, offs, pos1, pos2, out):
         def w2_views(e, to, order):
             w2_cast[e] = to
             return (
-                to.rearrange("p (c j r u) -> p " + order, j=RUN, r=2, u=2),
-                w2_raw[e].rearrange("p r u (c j) -> p " + order, j=RUN),
+                to.rearrange("p (c j r u) -> p " + order, j=W2_RUN, r=2, u=2),
+                w2_raw[e].rearrange("p r u (c j) -> p " + order, j=W2_RUN),
             )
 
         def cast_w2(e):
             w_bf = keep.tile([P, N * PACK], BF16, name=f"w2_bf{e}", align_bytes=64)
             to, src = w2_views(e, w_bf[:], "c r u j")
-            groups = N // RUN
+            groups = N // W2_RUN
             for lo, hi in ((0, groups),) if e < LAST else ((0, groups // 2), (groups // 2, groups)):
                 nc.scalar.copy(to[:, lo:hi], src[:, lo:hi])
 
@@ -174,7 +175,10 @@ def tile_routed_moe_kernel(tc, xT, w1, w3, w2, gate, offs, pos1, pos2, out):
         def quantise_w2(e):
             words = keep.tile([P, N], U32, name=f"w2_words{e}", align_bytes=64)
             scales = keep.tile([P, N], U8, name=f"w2_scales{e}", align_bytes=64)
-            nc.vector.quantize_mx(out=words[:].bitcast(FP8X4), scales=scales[:], in_=w2_cast[e])
+            for lo, hi in ((0, N),) if e < LAST else ((0, N // 2), (N // 2, N)):
+                nc.vector.quantize_mx(
+                    out=words[:, lo:hi].bitcast(FP8X4), scales=scales[:, lo:hi], in_=w2_cast[e][:, lo * PACK : hi * PACK]
+                )
             w2_quantised[e] = (words[:], scales[:])
 
         def list_columns(tile, lo, hi):

from contextlib import ExitStack

import concourse.mybir as mybir

K, T, E, C, H, N = 1024, 768, 6, 256, 512, 128
P = 128
PACK = 4
K_PASS = P * PACK
PASSES = K // K_PASS
SLOTS = E * C
FLOPS = 2 * SLOTS * (2 * K * H + H * N)

F32 = mybir.dt.float32
BF16 = mybir.dt.bfloat16
U32 = mybir.dt.uint32
U16 = mybir.dt.uint16
U8 = mybir.dt.uint8
FP8X4 = mybir.dt.float8_e4m3fn_x4
MULT = mybir.AluOpType.mult
ADD = mybir.AluOpType.add
RELU = mybir.ActivationFunctionType.Relu
COPY = mybir.ActivationFunctionType.Copy

LIST_ROWS = 16
SLICE = 512
HALF = C // 2
RUN = 4
W2_RUN = 2
X_CALLS = ((0, 512), (512, T))
SCALE_ROW = (0, 4)

AHEAD = 3
RING = 5
WHOLE = 8
LAST = E - 1

X_SHARE = (128, 40)
FIRST_SHARES = ((P, P), (P, 96))
WHOLE_SHARES = ((P, 24), (112, 0))
PASS_SHARES = ((40, 96), (80, 40))
LAST_W1_SHARES = (P // 2, 80)
LAST_PASS_0_SHARE = 44
TILE_PAIRS = ((0, 2), (2, PACK))
EARLY_W2 = 2
GPSIMD_W2 = 3
OUT_PIECES = ((0, T // 2), (T // 2, 5 * T // 6), (5 * T // 6, T))


def tile_routed_moe_kernel(tc, xT, w1, w3, w2, gate, offs, pos1, pos2, out):
    nc = tc.nc
    with ExitStack() as ctx:
        keep = ctx.enter_context(tc.tile_pool(name="keep", bufs=1))
        work = ctx.enter_context(tc.tile_pool(name="work", bufs=2))
        quant = ctx.enter_context(tc.tile_pool(name="quant", bufs=8))
        psum = ctx.enter_context(tc.psum_pool(name="psum", bufs=2))
        psum_y = ctx.enter_context(tc.psum_pool(name="psum_y", bufs=4))

        offs_t = keep.tile([P, SLOTS // LIST_ROWS], U16, name="offs_t")
        pos1_t = keep.tile([P, T // LIST_ROWS], U16, name="pos1_t")
        pos2_t = keep.tile([P, T // LIST_ROWS], U16, name="pos2_t")
        x_raw = [keep.tile([P, PACK, T], F32, name=f"x_raw{s}", align_bytes=256) for s in range(PASSES)]
        x_bf = [keep.tile([P, T * PACK], BF16, name=f"x_bf{s}", align_bytes=64) for s in range(PASSES)]
        x_words = [keep.tile([P, T], U32, name=f"x_words{s}", align_bytes=64) for s in range(PASSES)]
        x_bytes = keep.tile([P, T], U8, name="x_bytes", align_bytes=64)
        gate_t = keep.tile([P, 2, T], F32, name="gate_t", align_bytes=256)
        ring = [keep.tile([P, PASSES, PACK, H], F32, name=f"ring{place}", align_bytes=256) for place in range(RING)]
        y_all = keep.tile([P, SLOTS], F32, name="y_all", align_bytes=256)
        w2_raw = [keep.tile([P, 2, 2, N], F32, name=f"w2_raw{e}", align_bytes=256)[:] for e in range(LAST)]
        w2_last = y_all[:, 2 * C - N // 2 : 6 * C - N // 2].rearrange("p (r c) -> p r c", r=2)[:, :, 0:C]
        w2_raw.append(w2_last.rearrange("p r (u n) -> p r u n", u=2))
        slot_words = {}
        slot_bytes = {}
        cast = {}
        quantised = {}
        w2_cast = {}
        w2_quantised = {}
        relus = {}
        sums = {}
        hidden = {}
        hidden_q = {}

        def staged(w, e):
            return ring[(2 * e + w) % RING]

        def whole(w, e):
            return 2 * e + w < WHOLE

        def column_half(side):
            rows = staged(1, LAST)[:, 1].rearrange("p k c -> p (k c)")
            return rows.rearrange("p (side k c) -> p side k c", side=2, k=PACK)[:, side]

        def load(w, e):
            src = (w1, w3)[w][e].rearrange("(s p t) c -> p s t c", s=PASSES, t=PACK)
            if whole(w, e):
                nc.sync.dma_start(out=staged(w, e)[:], in_=src)
            elif (w, e) != (1, LAST):
                for s in range(PASSES):
                    nc.sync.dma_start(out=staged(w, e)[:, s], in_=src[:, s])
            else:
                nc.sync.dma_start(out=staged(w, e)[:, 0], in_=src[:, 0])
                for side in range(2):
                    columns = src[:, 1, :, side * H // 2 : (side + 1) * H // 2]
                    nc.sync.dma_start(out=column_half(side), in_=columns)

        def load_tail():
            for e in range(E):
                nc.sync.dma_start(out=w2_raw[e], in_=w2[e].rearrange("(p r u) n -> p r u n", r=2, u=2))
            nc.sync.dma_start(pos1_t[:], pos1)
            nc.sync.dma_start(pos2_t[:], pos2)
            nc.sync.dma_start(out=gate_t[:], in_=gate.rearrange("g p n -> p g n"))

        def by_column(raw):
            return raw.rearrange("p k (m t) -> p m k t", t=PACK)

        def cast_in_pairs(to, src):
            for lo, hi in TILE_PAIRS:
                nc.vector.tensor_copy(to[:, :, :, lo:hi], src[:, :, :, lo:hi])

        def cast_tile(w, e, s):
            w_bf = work.tile([P, H * PACK], BF16, name="w_bf", align_bytes=64, bufs=4)
            cast[(w, e, s)] = w_bf
            return w_bf[:].rearrange("p (t m k) -> p m k t", t=PACK, k=PACK)

        def h_pass(e):
            return 1 if whole(0, e) else 0

        def cast_w(w, e, s, scalar_m):
            src, to = by_column(staged(w, e)[:, s]), cast_tile(w, e, s)
            if scalar_m > 0:
                nc.scalar.copy(to[:, 0:scalar_m], src[:, 0:scalar_m])
            if (w, e, s) == (0, LAST, 1):
                cast_in_pairs(to[:, scalar_m:], src[:, scalar_m:])
            elif w == 0 and s == h_pass(e) and scalar_m < P // 2:
                nc.vector.tensor_copy(to[:, P // 2 :], src[:, P // 2 :])
                nc.vector.tensor_copy(to[:, scalar_m : P // 2], src[:, scalar_m : P // 2])
            elif scalar_m < P:
                nc.vector.tensor_copy(to[:, scalar_m:], src[:, scalar_m:])

        def code_tiles(w, e, s):
            words = quant.tile([P, H], U32, name="w_words", align_bytes=64)
            scales = quant.tile([P, H], U8, name="w_scales", align_bytes=64)
            quantised[(w, e, s)] = (words, scales)

        def quantise_tiles(w, e, s, lo, hi):
            words, scales = quantised[(w, e, s)]
            nc.vector.quantize_mx(
                out=words[:, lo * P : hi * P].bitcast(FP8X4),
                scales=scales[:, lo * P : hi * P],
                in_=cast[(w, e, s)][:, lo * K_PASS : hi * K_PASS],
            )

        def quantise_w(w, e, s):
            code_tiles(w, e, s)
            for lo, hi in TILE_PAIRS if (w, e, s) in ((0, LAST, 1), (1, LAST, 0)) else ((0, PACK),):
                quantise_tiles(w, e, s, lo, hi)

        def w2_views(e, to, order):
            w2_cast[e] = to
            return (
                to.rearrange("p (c j r u) -> p " + order, j=W2_RUN, r=2, u=2),
                w2_raw[e].rearrange("p r u (c j) -> p " + order, j=W2_RUN),
            )

        def cast_w2(e):
            w_bf = keep.tile([P, N * PACK], BF16, name=f"w2_bf{e}", align_bytes=64)
            to, src = w2_views(e, w_bf[:], "c r u j")
            groups = N // W2_RUN
            for lo, hi in ((0, groups),) if e < LAST else ((0, groups // 2), (groups // 2, groups)):
                nc.scalar.copy(to[:, lo:hi], src[:, lo:hi])

        def cast_w2_on_gpsimd(e):
            to, src = w2_views(e, w2_cast[EARLY_W2 - 1], "c j r u")
            nc.gpsimd.tensor_scalar(to, src, 1.0, 0.0, MULT, ADD)

        def quantise_w2(e):
            words = keep.tile([P, N], U32, name=f"w2_words{e}", align_bytes=64)
            scales = keep.tile([P, N], U8, name=f"w2_scales{e}", align_bytes=64)
            for lo, hi in ((0, N),) if e < LAST else ((0, N // 2), (N // 2, N)):
                nc.vector.quantize_mx(
                    out=words[:, lo:hi].bitcast(FP8X4), scales=scales[:, lo:hi], in_=w2_cast[e][:, lo * PACK : hi * PACK]
                )
            w2_quantised[e] = (words[:], scales[:])

        def list_columns(tile, lo, hi):
            return tile[:, lo // LIST_ROWS : hi // LIST_ROWS]

        def gather_words(q, s):
            if s == 0:
                words = work.tile([P, PASSES, SLICE], U32, name="slot_words", align_bytes=64, bufs=SLOTS // SLICE)
                slot_words[q] = words
            offsets = list_columns(offs_t, q * SLICE, (q + 1) * SLICE)
            nc.vector.tensor_copy(slot_words[q][:, s, :], x_words[s][:].indirect(offsets))

        def gather_bytes(q):
            scales = work.tile([P, SLICE], U8, name="slot_bytes", align_bytes=64, bufs=SLOTS // SLICE)
            nc.vector.tensor_copy(scales[:], x_bytes[:].indirect(list_columns(offs_t, q * SLICE, (q + 1) * SLICE)))
            slot_bytes[q] = scales

        def project(w, e, half, s, opens):
            q, lo = divmod(e * C + half * HALF, SLICE)
            if opens:
                acc = psum.tile([P, PACK, HALF], F32, name=("acc_a", "acc_b")[w])
                sums[(w, e, half)] = acc
            words, scales = quantised[(w, e, s)]
            tiles = list(range(PACK)) if opens or half == 0 else list(reversed(range(PACK)))
            for t in tiles:
                nc.tensor.matmul_mx(
                    out=sums[(w, e, half)][:, t, :],
                    lhsT=words[:, t * P : (t + 1) * P].bitcast(FP8X4),
                    lhsT_scale=scales[:, t * P : (t + 1) * P],
                    rhs=slot_words[q][:, s, lo : lo + HALF].bitcast(FP8X4),
                    rhs_scale=slot_bytes[q][SCALE_ROW[s] : P, lo : lo + HALF],
                    start=(opens and t == tiles[0]),
                    stop=(not opens and t == tiles[-1]),
                )

        def by_slot(acc):
            return acc[:].rearrange("p t (g j d) -> p g j t d", g=PACK, d=2)

        def rectify(e, half):
            rows = staged(1, e)[:, 0 if whole(1, e) or e == LAST else 1]
            relu = rows[:, :, half * HALF : (half + 1) * HALF].rearrange("p g (j t d) -> p g j t d", t=PACK, d=2)
            nc.scalar.activation(relu, by_slot(sums[(0, e, half)]), RELU)
            relus[(e, half)] = relu

        def hide(e, half, h):
            to = h.rearrange("p (g j d t) -> p g j t d", g=PACK, t=PACK, d=2)
            nc.vector.tensor_tensor(to, by_slot(sums[(1, e, half)]), relus[(e, half)], MULT)
            hidden[(e, half)] = h

        def hide_in_next_w1(e, half):
            hide(e, half, staged(0, e + 1)[:, h_pass(e + 1), half, H // 2 : H].bitcast(BF16))

        def quantise_h(e, half):
            words = work.tile([P, HALF], U32, name="h_words", align_bytes=64, bufs=2 * LAST)
            scales = work.tile([P, HALF], U8, name="h_scales", align_bytes=64, bufs=2 * LAST)
            nc.vector.quantize_mx(out=words[:].bitcast(FP8X4), scales=scales[:], in_=hidden[(e, half)])
            hidden_q[(e, half)] = (words[:], scales[:])

        def quantise_last_h(h):
            words = keep.tile([P, C], U32, name=f"w2_raw{LAST - 1}", align_bytes=256)
            scales = keep.tile([P, C], U8, name="last_h_scales", align_bytes=64)
            nc.vector.quantize_mx(out=words[:].bitcast(FP8X4), scales=scales[:], in_=h)
            for half in range(2):
                cols = slice(half * HALF, (half + 1) * HALF)
                hidden_q[(LAST, half)] = (words[:, cols], scales[:, cols])

        def project_back(e, half, acc):
            w_words, w_scales = w2_quantised[e]
            h_words, h_scales = hidden_q[(e, half)]
            nc.tensor.matmul_mx(
                out=acc,
                lhsT=w_words.bitcast(FP8X4),
                lhsT_scale=w_scales,
                rhs=h_words.bitcast(FP8X4),
                rhs_scale=h_scales,
                start=True,
                stop=True,
            )

        def finish_experts(lo, hi, copy):
            acc = psum_y.tile([P, (hi - lo) * C], F32, name="acc_y")
            for e in range(lo, hi):
                for half in range(2):
                    col = (e - lo) * C + half * HALF
                    project_back(e, half, acc[:, col : col + HALF])
            copy(y_all[:, lo * C : hi * C], acc[:])

        def finish_last_expert():
            for half, copy in enumerate((nc.scalar.copy, nc.vector.tensor_copy)):
                acc = sums[(0, LAST, half)][:, 0, :]
                project_back(LAST, half, acc)
                col = LAST * C + half * HALF
                copy(y_all[:, col : col + HALF], acc)

        nc.gpsimd.memset(x_bytes[:], 0)
        for s in range(PASSES):
            nc.sync.dma_start(
                out=x_raw[s][:], in_=xT[s * K_PASS : (s + 1) * K_PASS, :].rearrange("(p t) n -> p t n", t=PACK)
            )
            if s == 0:
                nc.sync.dma_start(offs_t[:], offs)
        matrices = [(w, e) for e in range(E) for w in range(2)]
        for w, e in matrices[:AHEAD]:
            load(w, e)

        for s in range(PASSES):
            dst = x_bf[s][:].rearrange("p (c j t) -> p c t j", j=RUN, t=PACK)
            src = x_raw[s][:].rearrange("p t (c j) -> p c t j", j=RUN)
            nc.scalar.copy(dst[:, X_SHARE[s] :], src[:, X_SHARE[s] :])
            nc.vector.tensor_copy(dst[:, 0 : X_SHARE[s]], src[:, 0 : X_SHARE[s]])
            for lo, hi in X_CALLS:
                nc.vector.quantize_mx(
                    out=x_words[s][:, lo:hi].bitcast(FP8X4),
                    scales=x_bytes[SCALE_ROW[s] : P, lo:hi],
                    in_=x_bf[s][:, PACK * lo : PACK * hi],
                )
            gather_words(0, s)
        gather_bytes(0)

        for step, (w, e) in enumerate(matrices[:-1]):
            if step + AHEAD < len(matrices):
                load(*matrices[step + AHEAD])
            if step + AHEAD == len(matrices):
                load_tail()
            if e == LAST:
                shares = LAST_W1_SHARES
            else:
                shares = (FIRST_SHARES if e == 0 else WHOLE_SHARES if whole(w, e) else PASS_SHARES)[w]
            first, second = (1, 0) if whole(w, e) else (0, 1)
            before = e - 1 if w == 0 and e > 0 else None
            cast_w(w, e, first, shares[first])
            if whole(w, e):
                cast_w(w, e, second, shares[second])
            if before is not None:
                hide_in_next_w1(before, 0)
                if whole(w, e):
                    hide_in_next_w1(before, 1)
                    quantise_h(before, 0)
            quantise_w(w, e, first)
            for half in range(2):
                project(w, e, half, first, True)
            if not whole(w, e):
                if before is not None:
                    hide_in_next_w1(before, 1)
                    quantise_h(before, 0)
                cast_w(w, e, second, shares[second])
            if w == 1:
                for half in range(2):
                    rectify(e, half)
            if before is not None:
                quantise_h(before, 1)
            quantise_w(w, e, second)
            for half in range(2):
                project(w, e, half, second, False)
            if step == 0:
                for q in range(1, SLOTS // SLICE):
                    gather_words(q, 0)
                    gather_words(q, 1)
                    gather_bytes(q)

        to = cast_tile(1, LAST, 0)
        src = by_column(staged(1, LAST)[:, 0])
        nc.scalar.copy(to[:, 0:LAST_PASS_0_SHARE], src[:, 0:LAST_PASS_0_SHARE])
        cast_in_pairs(to[:, LAST_PASS_0_SHARE:], src[:, LAST_PASS_0_SHARE:])
        for half in range(2):
            rectify(LAST, half)
        quantise_w(1, LAST, 0)
        for half in range(2):
            project(1, LAST, half, 0, True)
        to = cast_tile(1, LAST, 1)
        nc.vector.tensor_copy(to[:, 0 : P // 2], by_column(column_half(0)))
        cast_in_pairs(to[:, P // 2 :], by_column(column_half(1)))
        code_tiles(1, LAST, 1)
        for t in range(PACK):
            quantise_tiles(1, LAST, 1, t, t + 1)
        for half in range(2):
            project(1, LAST, half, 1, False)

        for e in range(EARLY_W2):
            cast_w2(e)
            quantise_w2(e)
        for e in range(EARLY_W2, E):
            if e == GPSIMD_W2:
                cast_w2_on_gpsimd(e)
            else:
                cast_w2(e)
        last_h = keep.tile([P, C * PACK], BF16, name=f"w2_raw{EARLY_W2 - 1}", align_bytes=256)
        for half in range(2):
            hide(LAST, half, last_h[:, half * K_PASS : (half + 1) * K_PASS])
        for e in range(EARLY_W2, LAST):
            quantise_w2(e)
        quantise_last_h(last_h[:])
        quantise_w2(LAST)
        finish_experts(0, 2, nc.scalar.copy)
        finish_experts(2, 4, nc.vector.tensor_copy)
        finish_experts(4, 5, nc.scalar.copy)
        finish_last_expert()

        def fetch(name, positions, lo, hi):
            fetched = keep.tile([P, hi - lo], F32, name=name)
            nc.scalar.activation(fetched[:], y_all[:].indirect(list_columns(positions, lo, hi)), COPY)
            return fetched

        def weigh_second(piece):
            lo, hi = OUT_PIECES[piece]
            nc.vector.tensor_tensor(second_products[:, lo:hi], seconds[piece][:], gate_t[:, 1, lo:hi], MULT)

        def add_and_store(piece, to):
            lo, hi = OUT_PIECES[piece]
            nc.vector.tensor_tensor(to[:, lo:hi], first_products[:, lo:hi], second_products[:, lo:hi], ADD)
            nc.sync.dma_start(out=out[:, lo:hi], in_=to[:, lo:hi])

        last_piece = OUT_PIECES[-1][0]
        first_products = keep.tile([P, T], F32, name="first_products")
        second_products = keep.tile([P, T], F32, name="second_products")
        seconds = [fetch("second0", pos2_t, *OUT_PIECES[0])]
        last_firsts = fetch("last_firsts", pos1_t, last_piece, T)
        seconds += [fetch(f"second{piece}", pos2_t, *OUT_PIECES[piece]) for piece in (1, 2)]

        nc.vector.tensor_tensor(
            first_products[:, 0:last_piece],
            y_all[:].indirect(list_columns(pos1_t, 0, last_piece)),
            gate_t[:, 0, 0:last_piece],
            MULT,
        )
        weigh_second(0)
        nc.vector.tensor_tensor(first_products[:, last_piece:T], last_firsts[:], gate_t[:, 0, last_piece:T], MULT)
        total = keep.tile([P, T], F32, name="total", align_bytes=256)
        add_and_store(0, total)
        weigh_second(1)
        weigh_second(2)
        add_and_store(1, y_all)
        add_and_store(2, total)
